import numpy as np, ml_dtypes
CORES = [2,3,42,43,82,83,122,123]
N = 8
import mx_ref
BF = ml_dtypes.bfloat16
def gentries(a):
    return np.ascontiguousarray(a.reshape(8, 16, -1).transpose(0, 2, 1)).reshape(8, -1)
def gtable(e):
    e = np.asarray(e); return np.ascontiguousarray(e.reshape(8, -1, 16).transpose(0, 2, 1)).reshape(128, -1).astype(np.int32)
def gcols(t, e):
    v = np.concatenate([t.reshape(8, 16, -1, 4), np.zeros((8, 16, 1, 4), BF)], axis=2)
    return np.ascontiguousarray(np.stack([v[g][:, e[g]] for g in range(8)])).reshape(128, -1)
def tile(rs):
    return np.stack(rs, axis=2).reshape(128, -1).astype(BF)
def pick(q, e):
    c = np.concatenate([q[0].reshape(128, -1, 4), np.zeros((128, 1, 4), np.uint8)], axis=1); s = np.concatenate([q[1], np.ones((16, 1), np.uint8)], axis=1)
    return (np.ascontiguousarray(c[:, e].reshape(128, -1)), np.ascontiguousarray(s[:, e]))
def join(*qs):
    return (np.concatenate([q[0] for q in qs], axis=1), np.concatenate([q[1] for q in qs], axis=1))
def put(q, e, v):
    c, s = q[0].reshape(128, -1, 4).copy(), q[1].copy(); c[:, e] = v[0].reshape(128, -1, 4); s[:, e] = v[1]
    return (c.reshape(128, -1), s)
def pk(c, s):
    return (np.ascontiguousarray(c), mx_ref.live(s))
def emit(q):
    return q[0], q[1]
def packed(v, rng):
    q = [mx_ref.quantize(np.ascontiguousarray(v[r])) for r in range(N)]
    return np.stack([a for a, b in q]), np.stack([mx_ref.plane(b, rng) for a, b in q])
def values_of_codes():
    e, c = np.zeros((128, 128, 4), np.float32), np.zeros((128, 2, 4), np.uint8)
    e[np.arange(128), np.arange(128), 0] = 1
    c[:127, :, 0] = np.arange(256).reshape(2, 128).T[:127]
    return mx_ref.matmul(mx_ref.quantize(e.reshape(128, 512).astype(BF)), (c.reshape(128, 8), np.full((16, 2), 127, np.uint8))).T.reshape(-1).astype(np.float64)
CODE_VALUE, SCALE_VALUE = values_of_codes(), 2.0 ** (np.arange(256) - 127.0)
def decode(q):
    return (CODE_VALUE[q[0]].reshape(16, 8, -1, 4) * SCALE_VALUE[q[1]][:, None, :, None] + 0.0).reshape(128, -1).astype(np.float32)
def f(rng, *shape):
    return mx_ref.flush((rng.standard_normal(shape, dtype=np.float32) * np.exp2(rng.integers(-2, 3, shape[:-1] + (1,)))).astype(BF))
def wide(rng, *shape, cols=0):
    v = rng.standard_normal(shape, dtype=np.float32) * np.exp2(rng.integers(-12, 13, shape)).astype(np.float32)
    if cols: v *= np.repeat(np.exp2(rng.integers(-cols, cols + 1, shape[:-2] + (1, shape[-1] // 4))) * (rng.random(shape[:-2] + (1, shape[-1] // 4)) > 0.0625), 4, axis=-1).astype(np.float32)
    return mx_ref.flush(v.astype(BF))
C, T, R = 256, 2048, 3
def big(v):
    v = v.astype(np.float32)
    v[np.abs(v) < np.float32(2.0 ** -12)] = 0
    return v.astype(BF)
def numbers_of(rng):
    return {"x": big(f(rng, N, 128, 4 * C)), "u": np.array(f(rng, N, 128, 512)), "v": np.array(f(rng, N, 128, 512))}
def lists_of(t):
    return np.stack([gtable(t[r]) for r in range(N)])
def layers(rng, still=[], full=False):
    w = np.zeros((N, 512, 512), np.float32)
    k = rng.random((N, 512, 512))
    k[:, :, np.isin(np.arange(512) // 4 % 16, still)] = 2
    e = np.argpartition(k, 8, axis=2)[:, :, :8]
    a = rng.integers(4, 16, (N, 512, 8)) * 0.25 * rng.choice([-1.0, 1.0], (N, 512, 8))
    if full: a = 4.0 * rng.choice([-1.0, 1.0], (N, 512, 1)) * np.ones((1, 1, 8))
    np.put_along_axis(w, e, a.astype(np.float32), axis=2)
    w[:, np.isin(np.arange(512) % 16, still)] = 0
    return w
def weights(rng, w):
    c, s = packed(np.ascontiguousarray(w.reshape(N, 512, 128, 4).transpose(0, 2, 1, 3)).reshape(N, 128, 2048).astype(BF), rng)
    return {"wc": c, "ws": s}
def setup_inputs(rng):
    return {**numbers_of(rng), "p": lists_of(rng.integers(0, T, (N, 8, C))), **weights(rng, layers(rng))}
def setup_inputs_ties(rng):
    d = numbers_of(rng)
    x = d["x"].reshape(N, 8, 16, C, 4)
    x[:, :, 0] = 0
    x[:, :, 0, :, 0] = rng.integers(0, 3, (N, 8, C)).astype(np.float32).astype(BF)
    u = d["u"].reshape(N, 128, 128, 4)
    u[:, :, ::16] = 0
    o = rng.permutation(N)
    for r in range(N):
        for h in range(0, 128, 16): u[r, h, h, 0] = 0.0 if r == o[0] else -1.0 if r == o[1] else 1.0
    t = rng.integers(0, T, (N, 8, C))
    t[o[:2]] = C * rng.integers(0, 4, (2, 8, C))
    t[o[2]] = rng.integers(0, T)
    t[o[3]] = C * (7 - np.arange(8))[:, None]
    return {"x": x.reshape(N, 128, 4 * C), "u": u.reshape(N, 128, 512), "v": d["v"], "p": lists_of(t), **weights(rng, layers(rng, [0]))}
def setup_inputs_near(rng):
    d = numbers_of(rng)
    x = d["x"].astype(np.float32).reshape(N, 8, 16, C, 4)
    x[:, :, 0] = 0
    x[:, :, 8:] = 0
    u = d["u"].reshape(N, 128, 128, 4)
    u[:, :, ::16] = 0
    t = rng.integers(0, T, (N, 8, C))
    o = rng.permutation(N) % 4
    for r in range(N):
        s = rng.integers(0, 16, (8, C))
        if o[r] == 1:
            s[5:] = np.minimum(s[5:], 12)
            s[5:, 4:9] = [15, 15, 14, 13, 12]
            t[r] = np.minimum(t[r], T - 2)
            t[r, 5, :16] = T - 1
            t[r, 6, :9] = T - 1
            t[r, 7, :7] = T - 1
        if o[r] < 3: x[r, :, 8] = ((s[:, :, None] >> np.arange(4)) & 1) * np.exp2(np.arange(4) - 22.0)
        if o[r] < 2:
            x[r, :, 0, :, 0] = rng.choice([-1.0, 1.0], (8, 1))
            x[r, :, 11, :, 0] = 2.0 ** -10
        if o[r] == 2:
            for g in rng.permutation(8)[:4]: x[r, g, 0, rng.integers(C), 0] = 2.0 ** 26 * rng.choice([-1.0, 1.0])
        if o[r] == 3:
            x[r, :, 10, :, 0] = np.where(s < 8, 1.125 * 2.0 ** -29, 0.0)
            x[r, :, 11, :, 0] = np.where(s < 8, 0.0, 2.0 ** -29)
        k = 1.0 if o[r] == 0 else 2.0 ** -30
        for h in range(0, 128, 16):
            if o[r] < 2:
                u[r, h, h, 0] = k
                u[r, h + 11, h, 0] = k
            if o[r] == 2: u[r, h, h, 0] = 2.0 ** 30
            if o[r] < 3: u[r, h + 8, h] = k
            else:
                u[r, h + 10, h, 0] = 1.125 * k
                u[r, h + 11, h, 0] = 1.25 * k
    return {"x": x.reshape(N, 128, 4 * C).astype(BF), "u": u.reshape(N, 128, 512), "v": d["v"], "p": lists_of(t), **weights(rng, layers(rng, [0, 8, 9, 10, 11, 12, 13, 14, 15]))}
def setup_inputs_fine(rng):
    d = numbers_of(rng)
    x = (1.0 + (2 * rng.integers(0, 64, (N, 8, 2, 8, C, 4)) + 1) * 2.0 ** -7) * np.exp2(-rng.integers(8, 15, (N, 8, 2, 8, C, 4))) * rng.choice([-1.0, 1.0], (N, 8, 2, 8, C, 4))
    np.put_along_axis(x[..., 0], rng.integers(0, 8, (N, 8, 2, 1, C)), 1.96875 * rng.choice([-1.0, 1.0], (N, 8, 2, 1, C)), axis=3)
    x = x * np.exp2(rng.integers(-1, 3, (N, 8, 2, 1, C, 1)))
    return {"x": x.astype(np.float32).reshape(N, 128, 4 * C).astype(BF), "u": d["u"], "v": d["v"], "p": lists_of(rng.integers(0, T, (N, 8, C))), **weights(rng, layers(rng))}
def setup_inputs_ends(rng):
    k = int(rng.integers(0, 2))
    o = np.roll(np.array([2, 3, k, 1 - k])[np.arange(N) % 4], int(rng.integers(0, N)))
    sign = np.array([1.0, -1.0, 1.0, 1.0])
    x = np.zeros((N, 8, 16, C, 4))
    u = np.array(f(rng, N, 128, 512)).reshape(N, 128, 128, 4)
    v = (rng.integers(0, 2, (N, 128, 512)) * 2.0 - 1.0) * 2.0 ** 30
    w = layers(rng, full=True)
    t = np.zeros((N, 8, C), np.int64)
    for r in range(N):
        a = 2.0 ** 26 * rng.choice([1.0, 0.875, 0.75], (8, 1, C, 1))
        if o[r] == 0: x[r] = a
        if o[r] == 1:
            x[r] = -a
            t[r] = T - 1
        if o[r] < 2:
            w[r] = np.abs(w[r]) * (sign[o[r]] * sign[o[r - 1]])
            if o[r - 1] == 3:
                w[r, :, :64] = np.sum(w[r].reshape(512, 8, 64), axis=1)
                w[r, :, 64:] = 0
        if o[r] == 2:
            x[r] = 2.0 ** -30
            w[r] = 0
            t[r] = (T - 1) * rng.integers(0, 2, (8, C))
        if o[r] == 3:
            x[r] = 2.0 ** 26 * rng.choice([-1.0, 1.0], (8, 1, C, 1))
            x[r, 0] = 2.0 ** 26
            t[r] = (T - 1) * (rng.permutation(8) % 2)[:, None]
        h = rng.permutation(6) % 2 * 2.0 - 1.0
        for g in range(8): u[r, :, 16 * g] = 0.0 if g in (0, 7) else (2.0 ** -30 if o[r] == 2 else 2.0 ** 30) * float(h[g - 1])
    v = (np.where(v < 0, -1.0, 1.0) * np.where(rng.permutation(N) % 2, 2.0 ** -30, 2.0 ** 30)[:, None, None]).astype(np.float32).astype(BF)
    return {"x": x.astype(np.float32).reshape(N, 128, 4 * C).astype(BF), "u": u.reshape(N, 128, 512), "v": v.astype(np.float32).astype(BF), "p": lists_of(t), **weights(rng, w)}
def setup_inputs_spread(rng):
    d = setup_inputs(rng)
    d["x"] = big(wide(rng, N, 128, 4 * C, cols=6))
    return d
def check_inputs(d):
    b = []
    for k, most in (("x", 2.0 ** 26), ("u", 2.0 ** 30), ("v", 2.0 ** 30)):
        a = np.abs(d[k].astype(np.float32))
        if not (np.isfinite(a).all() and ((a == 0) | (a >= 2.0 ** -30) & (a <= most)).all()): b.append("a value of " + k)
    if not ((d["p"] >= 0) & (d["p"] < T)).all(): b.append("an entry of p")
    none, least, most = [emit(mx_ref.quantize(np.full((128, 16), k, np.float32).astype(BF)))[1][0, 0] for k in (0.0, 2.0 ** -30, 2.0 ** 30)]
    for r in range(N):
        if ((d["wc"][r] == 0x7F) | (d["wc"][r] == 0xFF)).any(): b.append("wc: a code that is no number")
        s = mx_ref.live(d["ws"][r])
        if ((s != none) & ((s < least) | (s > most))).any(): b.append("ws: a scale out of range")
        a = np.abs(decode(pk(d["wc"][r], d["ws"][r])).astype(np.float64)).reshape(128, 512, 4)
        if not (np.sum(a, axis=(0, 2)) <= 32).all(): b.append("sizes in a column of W")
    return b
def order_of(t):
    place = np.argsort(np.argsort(T * t.reshape(-1) + np.arange(T))).reshape(8, C)
    o = np.argsort(place, axis=1)
    k = np.stack([np.searchsorted(place[g, o[g]], 8 * np.arange(C) + 7, side="right") for g in range(8)]) - 1
    k = np.maximum(k, 0)
    return place // 8, np.take_along_axis(o, k, axis=1), np.take_along_axis(o, np.minimum(k + 1, C - 1), axis=1)
def reference(x, u, v, p, wc, ws):
    qu = [mx_ref.quantize(u[r]) for r in range(N)]
    lay = [pk(wc[r], ws[r]) for r in range(N)]
    now = [x[r] for r in range(N)]
    pos = np.stack([gentries(p[r]) for r in range(N)]).astype(np.int64)
    for t in range(R):
        own, q = [], []
        for r in range(N):
            own.append(decode(mx_ref.quantize(now[r])).astype(BF))
            c, m, n = order_of(pos[r])
            z = ((gcols(own[r], m).astype(np.float32) + gcols(own[r], n).astype(np.float32)) * np.float32(0.5)).astype(BF)
            q.append(mx_ref.quantize(z))
            s = mx_ref.matmul(qu[r], q[r])[::16] + np.float32(0.0)
            step = np.argsort(np.argsort(s, axis=1, kind="stable"), axis=1)
            pos[r] += np.take_along_axis(step, c, axis=1)
        for r in range(N):
            came = pick(q[(r + N - 1) % N], np.arange(1, C, 2))
            h = tile([mx_ref.matmul(pick(lay[r], np.arange(128 * b, 128 * b + 128)), came) * np.float32(0.03125) for b in range(4)])
            c, m, n = order_of(pos[r])
            now[r] = (own[r].astype(np.float32) + gcols(h, c // 2).astype(np.float32)).astype(BF)
    y, pt = np.zeros((N, 128, C), np.float32), np.zeros((N, 8, C), np.float32)
    oc, osc = np.zeros((N, 128, 4 * C), np.uint8), np.zeros((N, 16, C), np.uint8)
    for r in range(N):
        q = mx_ref.quantize(now[r])
        y[r] = mx_ref.matmul(mx_ref.quantize(v[r]), q)
        pt[r] = pos[r]
        oc[r], osc[r] = emit(q)
    return {"y": y, "pt": pt, "oc": oc, "osc": osc}

@@ -1,0 +1,417 @@
+from concourse.mybir import dt, AluOpType as A, ActivationFunctionType as AF
+
+N, R, C = 8, 3, 256
+TW = 2816
+HW = 2824
+ZI = 2816
+NV = 7
+NS = 7
+F8 = "float8_e4m3fn_x4"
+LISTS = {}
+
+
+def _scratch():
+    s = {}
+
+    def sb(names, w, d="float32"):
+        for n in names.split(): s[n] = ("sbuf", [128, w], d)
+
+    def mx(n, m, w):
+        sb(n, w, F8)
+        sb(m, w, "uint8")
+
+    def lists(buf, d, names, wide):
+        at = 0
+        for n in names.split():
+            w = wide.get(n, 16)
+            LISTS[n] = (buf, at, w)
+            at += (w + 15) // 16 * 16
+        sb(buf, at, d)
+    lists("lstf", "float32", "kl el elf Dm De t16 Kl acc rl lo eqv dm of eqc dmc ofc ivl cf cp kl17 pls lk par", {"kl17": 17, "pls": 17, "lk": 32, "par": 4})
+    lists("lsti", "int32", "iB pl sh4 colI c_lo c_hi place sh3 tt ip iq", {"place": 17, "sh3": 17, "tt": 32, "ip": 2, "iq": 2})
+    lists("lstu", "uint16", "kapU rep oddl ul ru ou lou oc2 hu cu ku colU piU iu x40 x41 x42 x43 L2", {"L2": 34})
+    sb("iA iX amod prow pti", 256, "int32")
+    sb("mask m0 er V Krow k2 Ko mk2 sl SBt dd crow stw inv prs ior ptf yo keepf", 256)
+    sb("ks", 264)
+    sb("mkb mko keepb kval kvale mg mgo Wr kpw", 256, "bfloat16")
+    sb("junk", 256 * (16 - NV), "bfloat16")
+    sb("sgn", 256 * NS, "bfloat16")
+    sb("cmp", 256 * NV, "bfloat16")
+    sb("sc", 128 * NV + 128, "float16")
+    sb("sc2", 288)
+    sb("h", HW + 256, "bfloat16")
+    sb("tabs", HW, "bfloat16")
+    sb("tab2", TW + 16, "bfloat16")
+    sb("gt gtT", 544, "bfloat16")
+    sb("Wc uin vin Bt0 Bt Bh Bm H", 512, "bfloat16")
+    sb("Ct", 4096, "bfloat16")
+    sb("Dt Z P F G XP Xf xin", 1024, "bfloat16")
+    sb("X", 1088, "bfloat16")
+    sb("EE one", 520, "bfloat16")
+    for t in range(4): mx("ec%d" % t, "es%d" % t, 128)
+    for n, m, w in (("bc", "bs", 128), ("hc", "hs", 128), ("mc", "ms", 128), ("xq", "xs", 272), ("zq", "zs", 256), ("cq", "cs", 1024), ("dq", "dqs", 256),
+                    ("uq", "us", 128), ("u2", "u2s", 128), ("vq", "vqs", 128), ("wq", "wp", 512), ("fq", "fqs", 256)): mx(n, m, w)
+    for k in range(R):
+        mx("pk%d" % k, "pp%d" % k, 128)
+        mx("lc%d" % k, "lp%d" % k, 128)
+    for k in range(8): s["ps%d" % k] = ("psum", [128, 512], "float32")
+    return s
+
+
+SCRATCH = _scratch()
+DSEM = ["dp", "drow", "dx", "du", "dw", "dv", "div", "dend"] + [n + str(k) for n in ("dV", "dlk", "dlo", "dk2", "dtab") for k in range(R + 1)]
+SEMAPHORES = ["qV", "qS", "qT", "qG", "snd"] + ["arr%d" % k for k in range(R)] + DSEM
+
+
+def rank_program(g, core, T, topo):
+    rank = T.rank_of(core)
+    if rank is None:
+        return
+    eng = {"V": g.vector, "S": g.scalar, "T": g.tensor, "G": g, "Y": g.sync}
+    know = {q: {} for q in eng}
+    cnt, last, readers, ends = {}, {}, {}, {}
+
+    def c(name, a=0, b=None, step=1):
+        buf, at, w = LISTS[name]
+        return T[buf][:, at + a:at + (w if b is None else b):step]
+
+    def need(q, toks):
+        best = {}
+        for t in toks:
+            if t[1] > best.get(t[0], (0, 0))[1]: best[t[0]] = t
+        for t in sorted(best.values(), key=lambda t: -len(t[3])):
+            if know[q].get(t[0], 0) >= t[1]: continue
+            eng[q].wait_ge(T.sem[t[0]], t[1])
+            for s, v in t[3].items():
+                if v > know[q].get(s, 0): know[q][s] = v
+            know[q][t[0]] = t[1]
+
+    def deps(q, rd, wr, acc=False, copies=False):
+        d = []
+        for k in rd:
+            if k in last: d.append(last[k])
+            if k[:2] == "ps": d += [t for t in readers.get(k, []) if t[2] != q]
+        for k in wr:
+            if k in last and not (acc and last[k][2] == q): d.append(last[k])
+            d += [t for t in readers.get(k, []) if copies or t[2] != q]
+        return d
+
+    def note(tok, rd, wr):
+        for k in rd: readers.setdefault(k, []).append(tok)
+        for k in wr:
+            last[k] = tok
+            readers[k] = []
+
+    def op(q, rd, wr, fn, *a, acc=False, **kw):
+        need(q, deps(q, rd, wr, acc))
+        s = "q" + q
+        cnt[s] = cnt.get(s, 0) + 1
+        fn(*a, **kw).then_inc(T.sem[s], 1)
+        note((s, cnt[s], q, {**know[q], s: cnt[s]}), rd, wr)
+        ends[s] = cnt[s]
+
+    def dma(sem, items):
+        seen, rds, wrs = {}, [], []
+        for q, o, i, rd, wr in items: need(q, deps(q, rd, wr, copies=True))
+        for q, o, i, rd, wr in items:
+            cnt[sem] = cnt.get(sem, 0) + 16
+            eng[q].dma_start(o, i).then_inc(T.sem[sem], 16)
+            for s, v in know[q].items(): seen[s] = max(v, seen.get(s, 0))
+            rds += rd
+            wrs += wr
+        seen[sem] = cnt[sem]
+        note((sem, cnt[sem], "dma", seen), rds, wrs)
+        ends[sem] = cnt[sem]
+
+    V, S, PE = g.vector, g.scalar, g.tensor
+    vts, vtt, vcp, vscan, act = V.tensor_scalar, V.tensor_tensor, V.tensor_copy, V.tensor_tensor_scan, S.activation
+
+    def quant(qn, sn, tn, a, n):
+        op("V", [tn], [qn, sn], V.quantize_mx, T[qn][:, 0:n], T[sn][:, 0:n], T[tn][:, a:a + 4 * n])
+
+    def mm(bank, lq, ls, la, rq, rs, ra, n, start=True, stop=True):
+        op("T", [lq, ls, rq, rs], [bank], PE.matmul_mx, T[bank][:, 0:n], T[lq][:, la:la + 128], T[ls][:, la:la + 128],
+           T[rq][:, ra:ra + n], T[rs][:, ra:ra + n], start, stop, acc=not start)
+
+    dma("dp", [("Y", c("pl"), T.p[:], [], ["pl"])])
+    dma("drow", [("YS"[x % 2], T.prow[x::16, :], T.p[:], [], ["prow"]) for x in range(16)])
+    dma("dx", [("Y", T.xin[:], T.x[:], [], ["xin"])])
+    dma("du", [("S", T.uin[:], T.u[:], [], ["uin"])])
+
+    def iota(n, pat, base=0, cm=0, small=False):
+        out = c(n) if n in LISTS else T[n][:]
+        if small: op("G", [], [n], g.iota, out, pat, base, cm, allow_small_or_imprecise_dtypes=True)
+        else: op("G", [], [n], g.iota, out, pat, base, cm)
+
+    def zeros(n, w, after=()):
+        op("G", list(after), [n], g.iota, T[n][:], [[0, w]], 0, 0, allow_small_or_imprecise_dtypes=True)
+    iota("iB", [[1, 16]])
+    iota("iA", [[0, 256]], 0, 1)
+    iota("er", [[1, 256]], small=True)
+    iota("iX", [[0, 16], [1, 16]])
+    iota("V", [[1, 256]], small=True)
+    iota("kval", [[1, 16], [16, 16]], 1, small=True)
+    iota("ip", [[0, 2]], 0, 1)
+    op("V", ["iA"], ["amod"], vts, T.amod[:], T.iA[:], 15, None, A.bitwise_and)
+    a16 = T.amod[:, 0:16]
+    op("V", ["iB"], ["of"], vts, c("of"), c("iB"), 16.0, None, A.mult)
+    op("V", ["amod"], ["t16"], vts, c("t16"), a16, 16.0, None, A.mult)
+    op("V", ["of", "amod"], ["el"], vtt, c("el"), c("of"), a16, A.add)
+    op("V", ["t16", "iB"], ["kl"], vtt, c("kl"), c("t16"), c("iB"), A.add)
+    op("S", ["er"], ["er"], act, T.er[:], T.er[:], AF.Copy, scale=1.0 / 256)
+    op("V", ["el"], ["elf"], vts, c("elf"), c("el"), 1.0 / 256, None, A.mult)
+    op("V", ["kl"], ["kapU"], vcp, c("kapU"), c("kl"))
+    op("V", [], ["one"], V.memset, T.one[:], 0.5)
+    op("V", [], ["Bt0"], V.memset, T.Bt0[:], 1.0)
+    op("V", [], ["ks"], V.memset, T.ks[:, 256:264], TW - 1.0)
+    op("V", [], ["sc"], V.memset, T.sc[:, 0:128], 0.0)
+    op("V", ["amod", "iX"], ["mask"], vtt, T.mask[:], T.amod[:], T.iX[:], A.is_equal)
+    op("V", ["iX"], ["keepf"], vts, T.keepf[:], T.iX[:], 1.0, None, A.min)
+    op("V", ["iX"], ["keepb"], vts, T.keepb[:], T.iX[:], 1.0, None, A.min)
+    op("V", ["pl", "elf"], ["Kl"], vtt, c("Kl"), c("pl"), c("elf"), A.add)
+    op("V", ["prow", "kapU", "er"], ["Krow"], vtt, T.Krow[:], T.prow[:].indirect(c("kapU")), T.er[:], A.add)
+    op("G", ["one"], ["EE"], g.affine_select, T.EE[:], T.one[:], [[-1, 520]], A.is_equal, 0.0, 4, 4)
+    zeros("tab2", TW + 16)
+    op("G", ["Bt0"], ["Bt"], g.affine_select, T.Bt[:], T.Bt0[:], [[-16, 8], [0, 64]], A.is_ge, 0.0, 0, 1)
+    op("G", ["Bt"], ["Bt"], g.affine_select, T.Bt[:], T.Bt[:], [[16, 8], [0, 64]], A.is_ge, 0.0, 15, -1)
+    iota("kvale", [[1, 256]], 1, small=True)
+    zeros("Wc", 512)
+    zeros("Ct", 4096)
+    zeros("Dt", 1024)
+
+    def consts1():
+        op("V", [], ["h"], V.memset, T.h[:], 0.0)
+        op("V", ["kl"], ["Dm"], vts, c("Dm"), c("kl"), HW - 1.0, None, A.add)
+        op("V", ["ip"], ["iq"], vts, c("iq"), c("ip"), 4, 1, A.arith_shift_right, A.bitwise_and)
+        op("V", ["iq"], ["par"], vcp, c("par", 0, 1), c("iq", 0, 1))
+        op("V", ["par"], ["par"], vts, c("par", 1, 2), c("par", 0, 1), -1.0, 1.0, A.mult, A.add)
+        op("V", ["par"], ["par"], vts, c("par", 2, 4), c("par", 0, 2), float(ZI), None, A.mult)
+        for t in range(4): quant("ec%d" % t, "es%d" % t, "EE", 4 - t, 128)
+
+    def consts2():
+        op("V", ["kl"], ["kl17"], vcp, c("kl17", 0, 16), c("kl"))
+        op("V", ["kl"], ["kl17"], vts, c("kl17", 16, 17), c("kl", 15, 16), 1.0, None, A.add, acc=True)
+        op("V", [], ["sc2"], V.memset, T.sc2[:, 0:16], 0.0)
+        op("V", ["el"], ["De"], vts, c("De"), c("el"), 256.0, None, A.add)
+        op("S", ["Bt"], ["Bh"], act, T.Bh[:], T.Bt[:], AF.Copy, scale=0.5)
+        for t in range(4): op("S", ["Bt"], ["Bm"], act, T.Bm[:, t::4], T.Bt[:, t::4], AF.Copy, scale=1.0 if 8 + t < 16 - NS else 0.5, acc=t > 0)
+        op("V", ["iB"], ["ul"], vts, c("ul"), c("iB"), 16.0, None, A.mult)
+        op("V", ["iB"], ["rep"], vts, c("rep"), c("iB"), 16.0, 15.0, A.mult, A.add)
+        op("V", ["el"], ["oddl"], vts, c("oddl"), c("el"), 2.0, 1.0, A.mult, A.add)
+        quant("uq", "us", "uin", 0, 128)
+        op("V", [], ["crow"], V.memset, T.crow[:, 0:256 - 16 * NS], 8.0 * NS)
+        op("V", ["uq", "ul"], ["u2"], vcp, T.u2[:].bitcast(dt.uint32), T.uq[:].bitcast(dt.uint32).indirect(c("ul", 0, 8)))
+        op("V", ["us", "ul"], ["u2s"], vcp, T.u2s[:], T.us[:].indirect(c("ul", 0, 8)))
+        op("V", [], ["crow"], V.memset, T.crow[:, 256 - 16 * NS:256], 8.0 * NS - 8, acc=True)
+        op("V", ["amod", "iX"], ["m0"], vtt, T.m0[:], T.amod[:], T.iX[:], A.is_lt)
+        quant("bc", "bs", "Bt", 0, 128)
+        op("V", ["m0"], ["m0"], vts, T.m0[:], T.m0[:], -1e-35, None, A.mult)
+
+    def order_begin(n):
+        dma("dV%d" % n, [("Y", T.V[0::2, :], T.Krow[0::2, :], ["Krow"], ["V"])])
+        for b in range(NV, 16):
+            op("S", ["Krow", "Kl"], ["junk", "acc"], act, T.junk[:, 256 * (b - NV):256 * (b - NV) + 256], T.Krow[:], AF.Sign, bias=c("Kl", b, b + 1), scale=-1.0,
+               accum_out=c("acc", b, b + 1), acc=b > NV)
+        for b in range(NV):
+            op("V", ["Krow", "Kl"], ["cmp"], vts, T.cmp[:, 256 * b:256 * b + 256], T.Krow[:], c("Kl", b, b + 1), None, A.is_lt, acc=True)
+        w = 128 * NV
+        op("V", ["cmp"], ["sc"], vscan, T.sc[:, 128:128 + w], T.cmp[:, 0:2 * w:2], T.cmp[:, 1:2 * w:2], 0.0, A.add, A.add)
+        op("V", ["acc"], ["ruS"], vts, c("ru", NV, 16), c("acc", NV, 16), 0.5, 127.5, A.mult, A.add)
+        op("V", ["sc"], ["rl"], vtt, c("rl", 0, NV), T.sc[:, 255::128], T.sc[:, 127:127 + w:128], A.subtract)
+        op("V", ["rl"], ["ruV"], vcp, c("ru", 0, NV), c("rl", 0, NV))
+        op("V", ["ruS", "ruV", "V"], ["ks"], vcp, T.ks[:, 0:256].indirect(c("ru")), T.V[:])
+        dma("dlk%d" % n, [("Y", c("lk", 0, 16), T.ks[0::16, 0:256], ["ks"], ["lk"]), ("Y", c("lk", 16, 32), T.ks[0::16, 1:257], ["ks"], ["lk"])])
+        dma("dlo%d" % n, [("Y", c("lo"), T.ks[1::16, 0:256], ["ks"], ["lo"])])
+        dma("dk2%d" % n, [("Y", T.k2[0::2, :], T.ks[0::2, 0:256], ["ks"], ["k2"]), ("Y", T.k2[1::2, :], T.ks[0::2, 0:256], ["ks"], ["k2"])])
+
+    def order_tables(n):
+        t0, t1 = c("tt", 0, 16), c("tt", 31, 32)
+        op("V", ["lk"], ["tt"], vts, c("tt"), c("lk"), -0.498, None, A.add)
+        op("V", ["tt"], ["eqv"], vtt, c("eqv"), t0, c("tt", 16, 32), A.is_equal)
+        op("V", ["eqv", "Dm"], ["dm"], vtt, c("dm"), c("eqv"), c("Dm"), A.mult)
+        op("V", ["tt", "dm"], ["of"], vtt, c("of"), c("dm"), t0, A.max)
+        op("V", ["of"], ["ou"], vts, c("ou"), c("of"), 1.0, None, A.add)
+        op("V", ["ou", "kval"], ["h"], vcp, T.h[:].indirect(c("ou")), T.kval[:])
+        op("V", ["h"], ["tabs"], vscan, T.tabs[:], T.h[:, 0:HW], T.h[:, 0:HW], 0.0, A.max, A.max)
+        items = []
+        for e in range(N):
+            if e < N - 1: items.append((T.tab2[17 * e + 16::16, 0:TW], T.tabs[16 * e:16 * e + 7 - e, 1:TW + 1]))
+            if e: items.append((T.tab2[e:16 * e:16, 0:TW], T.tabs[16 * e:16 * e + e, 0:TW]))
+        dma("dtab%d" % n, [("YS"[k % 2], o, i, ["tabs"], ["tab2"]) for k, (o, i) in enumerate(items)])
+        op("V", ["tt", "par"], ["L2a"], vts, c("L2", 0, 32, 2), t0, c("par", 1, 2), c("par", 2, 3), A.mult, A.add)
+        op("V", ["tt", "par"], ["L2b"], vts, c("L2", 1, 32, 2), t0, c("par", 0, 1), c("par", 3, 4), A.mult, A.add)
+        op("V", ["tt", "par"], ["L2c"], vts, c("L2", 32, 33), t1, c("par", 1, 2), c("par", 2, 3), A.mult, A.add)
+        op("V", ["tt", "par"], ["L2d"], vts, c("L2", 33, 34), t1, c("par", 0, 1), c("par", 3, 4), A.mult, A.add)
+        if n < R: zeros("h", HW + 256, ["tabs"])
+
+    def order_places():
+        op("V", ["tab2", "L2a", "L2b", "L2c", "L2d"], ["gt"], vcp, T.gt[:], T.tab2[:].indirect(c("L2")))
+        op("V", ["gt"], ["gtT"], V.transpose, T.gtT[:], T.gt[:])
+        op("V", ["gtT"], ["sc2"], vscan, T.sc2[:, 16:288], T.gtT[:, 0::2], T.gtT[:, 1::2], 0.0, A.add, A.add)
+        op("V", ["sc2"], ["pls"], vtt, c("pls"), T.sc2[:, 31::16], T.sc2[:, 15:287:16], A.subtract)
+        op("V", ["pls", "kl17"], ["place"], vtt, c("place"), c("pls"), c("kl17"), A.add)
+
+    def keep_keys():
+        op("S", ["k2", "kapU"], ["Ko"], act, T.Ko[:], T.k2[:].indirect(c("kapU")), AF.Copy)
+
+    def cells(n):
+        op("V", ["place"], ["sh3"], vts, c("sh3"), c("place"), 3, None, A.arith_shift_right)
+        op("V", ["sh3"], ["eqc"], vtt, c("eqc"), c("sh3", 0, 16), c("sh3", 1, 17), A.is_equal)
+        op("V", ["eqc", "De"], ["dmc"], vtt, c("dmc"), c("eqc"), c("De"), A.mult)
+        op("V", ["dmc", "sh3"], ["ofc"], vtt, c("ofc"), c("dmc"), c("sh3", 0, 16), A.max)
+        op("V", ["ofc"], ["oc2"], vcp, c("oc2"), c("ofc"))
+        op("V", ["oc2", "kvale"], ["Wc"], vcp, T.Wc[:].indirect(c("oc2")), T.kvale[:])
+        op("V", ["Wc"], ["kpw"], vts, T.kpw[:], T.Wc[:, 0:256], 0.0, None, A.is_equal)
+        op("V", ["Wc", "kpw"], ["Wr"], vscan, T.Wr[:], T.kpw[:], T.Wc[:, 0:256], 0.0, A.mult, A.add)
+        if n < R - 1: zeros("Wc", 512, ["Wr"])
+        op("V", ["Wr", "mask"], ["mkb"], vtt, T.mkb[:], T.Wr[:], T.mask[:], A.mult)
+        op("V", ["mkb", "keepb"], ["mko"], vscan, T.mko[:], T.keepb[:], T.mkb[:], 0.0, A.mult, A.add)
+        op("V", ["mko"], ["ku"], vts, c("ku"), T.mko[:, 15::16], -1.0, 0.0, A.add, A.max)
+
+    XK = ["X0", "X1", "X2", "X3"]
+
+    def tail():
+        op("V", XK, ["Xt"], vcp, T.X[:, 1024:1084], T.X[:, 4:64])
+        op("S", XK, ["Xu"], act, T.X[:, 1084:1088], T.X[:, 1020:1024], AF.Copy)
+        op("V", XK + ["Xt", "Xu"], ["xq", "xs"], V.quantize_mx, T.xq[:], T.xs[:], T.X[:])
+
+    def unpack_pairs():
+        for t in range(4):
+            mm("ps%d" % t, "ec%d" % t, "es%d" % t, 0, "xq", "xs", 0, 256, True, False)
+            mm("ps%d" % t, "ec%d" % t, "es%d" % t, 0, "xq", "xs", 16, 256, False, True)
+            op("S", ["ps%d" % t], ["P%d" % t], act, T.P[:, 256 * t:256 * t + 256], T["ps%d" % t][:, 0:256], AF.Copy)
+        for t in range(4):
+            mm("ps%d" % (4 + t), "ec%d" % t, "es%d" % t, 0, "xq", "xs", 0, 256)
+
+    def unpack_keep():
+        for t in range(4):
+            op("S", ["ps%d" % (4 + t)], ["F%d" % t], act, T.F[:, 256 * t:256 * t + 256], T["ps%d" % (4 + t)][:, 0:256], AF.Copy, scale=2.0)
+
+    def deal(t, key, out):
+        op("V", ["H%d" % t, "hu", "G%d" % t], [key], vtt, out, T.H[:, 128 * t:128 * t + 128].indirect(c("hu")), T.G[:, 256 * t:256 * t + 256], A.add)
+
+    order_begin(0)
+    consts1()
+    order_tables(0)
+    for t in range(4):
+        op("V", ["lo"], ["x4%d" % t], vts, c("x4%d" % t), c("lo"), 4.0, float(t), A.mult, A.add)
+    for t in range(2):
+        op("S", ["xin", "x4%d" % t], ["X%d" % t], act, T.X[:, t:1024:4], T.xin[:].indirect(c("x4%d" % t)), AF.Copy)
+    for t in range(2, 4):
+        op("V", ["xin", "x4%d" % t], ["X%d" % t], vcp, T.X[:, t:1024:4], T.xin[:].indirect(c("x4%d" % t)))
+    tail()
+    unpack_pairs()
+    consts2()
+    order_places()
+    cells(0)
+    quant("hc", "hs", "Bh", 0, 128)
+    quant("mc", "ms", "Bm", 0, 128)
+    keep_keys()
+    dma("dw", [("Y", T.wq[:].bitcast(dt.uint8), T.wc[:], [], ["wq"]), ("Y", T.wp[:], T.ws[:], [], ["wp"])])
+    dma("dv", [("Y", T.vin[:], T.v[:], [], ["vin"])])
+
+    nxt = T.cores[(rank + 1) % N]
+    rid, pid, sen = topo.addr(nxt)
+    m4 = sum(1 << e for e in topo.engines(core, nxt)[0:4])
+
+    for n in range(R):
+        for t in (0, 1):
+            op("V", ["P%d" % t, "ku"], ["Z%d" % t], vcp, T.Z[:, t:1024:4], T.P[:, 256 * t:256 * t + 256].indirect(c("ku")))
+        for t in (2, 3):
+            op("S", ["P%d" % t, "ku"], ["Z%d" % t], act, T.Z[:, t:1024:4], T.P[:, 256 * t:256 * t + 256].indirect(c("ku")), AF.Copy)
+        op("V", ["Z0", "Z1", "Z2", "Z3"], ["zq", "zs"], V.quantize_mx, T.zq[:], T.zs[:], T.Z[:])
+        mm("ps0", "u2", "u2s", 0, "zq", "zs", 0, 256)
+        mm("ps1", "u2", "u2s", 0, "zq", "zs", 0, 256)
+        op("V", ["sh3"], ["cu"], vcp, c("cu"), c("sh3", 0, 16))
+        op("V", ["ps0", "mask"], ["mk2"], vtt, T.mk2[:], T.ps0[:, 0:256], T.mask[:], A.mult)
+        op("V", ["mk2", "keepf"], ["sl"], vscan, T.sl[:], T.keepf[:], T.mk2[:], 0.0, A.mult, A.add)
+        for j in range(NS):
+            b = 16 - NS + j
+            op("S", ["ps1", "sl"], ["sg%d" % j], act, T.sgn[:, 256 * j:256 * j + 256], T.ps1[:, 0:256], AF.Sign, bias=T.sl[:, 16 * b + 15:16 * b + 16], scale=-1.0)
+            if j == 0:
+                op("S", ["zs", "oddl"], ["pp%d" % n], act, T["pp%d" % n][:], T.zs[:].indirect(c("oddl", 0, 8)), AF.Copy)
+                op("S", ["sl", "rep"], ["SBt"], act, T.SBt[:], T.sl[:].indirect(c("rep")), AF.Copy)
+        for j in range(NS):
+            b = 16 - NS + j
+            o, ck, ce = 1024 * (b // 4) + b % 4, "S%d" % (b // 4), 1024 * (b // 4) + 1024
+            op("S", ["sg%d" % j, "Ct"], [ck], act, T.Ct[:, o:o + 64 * b:4], T.sgn[:, 256 * j:256 * j + 16 * b], AF.Sign, bias=-0.5, scale=-1.0, acc=True)
+            if b < 15: op("S", ["sg%d" % j, "Ct"], [ck], act, T.Ct[:, o + 64 * b + 64:ce:4], T.sgn[:, 256 * j + 16 * b + 16:256 * j + 256], AF.Sign, bias=0.5, scale=-1.0, acc=True)
+        for b in range(16 - NS):
+            k = b // 4
+            o, s1 = 1024 * k + b % 4, T.sl[:, 16 * b + 15:16 * b + 16]
+            if b: op("V", ["ps0", "sl", "Ct"], ["C%d" % k], vts, T.Ct[:, o:o + 64 * b:4], T.ps0[:, 0:16 * b], s1, None, A.is_gt, acc=True)
+            op("V", ["ps0", "sl", "Ct"], ["C%d" % k], vts, T.Ct[:, o + 64 * b + 64:1024 * k + 1024:4], T.ps0[:, 16 * b + 16:256], s1, None, A.is_ge, acc=True)
+            if b == 1:
+                op("V", ["zq", "oddl"], ["pk%d" % n], vcp, T["pk%d" % n][:].bitcast(dt.uint32), T.zq[:].bitcast(dt.uint32).indirect(c("oddl", 0, 8)))
+            if b == 7: op("V", ["C0", "C1", "Ct"], ["cq0"], V.quantize_mx, T.cq[:, 0:512], T.cs[:, 0:512], T.Ct[:, 0:2048])
+        need("G", [last["pk%d" % n], last["pp%d" % n]])
+        g.remote_dma(T["lc%d" % n][:].bitcast(dt.uint8), T["pk%d" % n][:].bitcast(dt.uint8), T.sem["arr%d" % n], T.sem.snd, pid, rid, m4)
+        g.remote_dma(T["lp%d" % n][:], T["pp%d" % n][:], T.sem["arr%d" % n], T.sem.snd, pid, rid, m4)
+        op("V", ["ps0", "SBt"], ["dd"], vtt, T.dd[:], T.ps0[:, 0:256], T.SBt[:], A.subtract)
+        op("V", ["dd", "m0"], ["Dt"], vtt, T.Dt[:, 0::4], T.dd[:], T.m0[:], A.is_gt)
+        op("V", ["C2", "S2", "Ct"] if NS < 8 else ["S2", "Ct"], ["cq2"], V.quantize_mx, T.cq[:, 512:768], T.cs[:, 512:768], T.Ct[:, 2048:3072])
+        op("V", ["Dt"], ["dq"], V.quantize_mx, T.dq[:], T.dqs[:], T.Dt[:])
+        op("V", ["S3", "Ct"], ["cq3"], V.quantize_mx, T.cq[:, 768:1024], T.cs[:, 768:1024], T.Ct[:, 3072:4096])
+
+        def total(lq, ls, rq, rs, key, ra, start, stop):
+            op("T", [lq, ls, key], ["ps2"], PE.matmul_mx, T.ps2[:, 0:256], T[lq][:], T[ls][:], T[rq][:, ra:ra + 256], T[rs][:, ra:ra + 256], start, stop, acc=not start)
+        total("bc", "bs", "cq", "cs", "cq0", 0, True, False)
+        total("bc", "bs", "cq", "cs", "cq0", 256, False, False)
+        total("mc", "ms", "cq", "cs", "cq2", 512, False, False)
+        total("bc", "bs", "dq", "dqs", "dq", 0, False, False)
+        total("hc", "hs", "cq", "cs", "cq3", 768, False, True)
+        op("V", ["ps2", "crow"], ["stw"], vtt, T.stw[:], T.ps2[:, 0:256], T.crow[:], A.add)
+        op("V", ["stw", "cu", "mask"], ["mg"], vtt, T.mg[:], T.stw[:].indirect(c("cu")), T.mask[:], A.mult)
+        op("V", ["stw", "cu", "Ko"], ["Krow"], vtt, T.Krow[:], T.stw[:].indirect(c("cu")), T.Ko[:], A.add)
+        op("V", ["mg", "keepb"], ["mgo"], vscan, T.mgo[:], T.keepb[:], T.mg[:], 0.0, A.mult, A.add)
+        op("V", ["mgo", "lk"], ["Kl"], vtt, c("Kl"), T.mgo[:, 15::16], c("lk", 0, 16), A.add)
+        order_begin(n + 1)
+        unpack_keep()
+        if n == R - 1: quant("vq", "vqs", "vin", 0, 128)
+        order_tables(n + 1)
+        op("V", ["lo"], ["lou"], vcp, c("lou"), c("lo"))
+        for t in range(4):
+            op("S", ["F%d" % t, "lou"], ["G%d" % t], act, T.G[:, 256 * t:256 * t + 256], T.F[:, 256 * t:256 * t + 256].indirect(c("lou")), AF.Copy)
+        need("T", [("arr%d" % n, 8, "R", {})])
+        ends["arr%d" % n] = 8
+        for t in range(4):
+            mm("ps%d" % (4 + t), "wq", "wp", 128 * t, "lc%d" % n, "lp%d" % n, 0, 128)
+            op("S", ["ps%d" % (4 + t)], ["H%d" % t], act, T.H[:, 128 * t:128 * t + 128], T["ps%d" % (4 + t)][:, 0:128], AF.Copy, scale=0.03125)
+        keep_keys()
+        if n == R - 1:
+            op("G", [], ["ior"], g.iota, T.ior[:], [[1, 256]], 0, 0, allow_small_or_imprecise_dtypes=True)
+            op("V", ["lk", "tt"], ["cf"], vtt, c("cf"), c("lk", 0, 16), c("tt", 0, 16), A.subtract)
+            op("V", ["cf"], ["colI"], vts, c("colI"), c("cf"), 256.0, None, A.mult)
+            op("V", ["colI"], ["c_lo"], vts, c("c_lo"), c("colI"), 15, None, A.bitwise_and)
+            op("V", ["colI"], ["c_hi"], vts, c("c_hi"), c("colI"), 4, None, A.arith_shift_right)
+            op("V", ["colI"], ["colU"], vcp, c("colU"), c("colI"))
+            op("V", ["c_lo"], ["cf"], vts, c("cf"), c("c_lo"), 16.0, None, A.mult)
+            op("V", ["cf", "c_hi"], ["cp"], vtt, c("cp"), c("cf"), c("c_hi"), A.add)
+            op("V", ["cp"], ["piU"], vcp, c("piU"), c("cp"))
+            op("V", ["piU", "ior"], ["inv"], vcp, T.inv[:].indirect(c("piU")), T.ior[:])
+            dma("div", [("Y", c("ivl"), T.inv[0::16, :], ["inv"], ["ivl"])])
+        order_places()
+        op("V", ["place"], ["sh4"], vts, c("sh4"), c("place", 0, 16), 4, None, A.arith_shift_right)
+        op("V", ["sh4"], ["hu"], vcp, c("hu"), c("sh4"))
+        if n < R - 1:
+            for t in range(4): deal(t, "X%d" % t, T.X[:, t:1024:4])
+            tail()
+            unpack_pairs()
+            cells(n + 1)
+        else:
+            op("V", ["ivl"], ["iu"], vcp, c("iu"), c("ivl"))
+            for t in range(4):
+                deal(t, "XP%d" % t, T.XP[:, 256 * t:256 * t + 256])
+                if t < 3: op("S", ["XP%d" % t, "iu"], ["Xf%d" % t], act, T.Xf[:, t:1024:4], T.XP[:, 256 * t:256 * t + 256].indirect(c("iu")), AF.Copy)
+                else: op("V", ["XP%d" % t, "iu"], ["Xf%d" % t], vcp, T.Xf[:, t:1024:4], T.XP[:, 256 * t:256 * t + 256].indirect(c("iu")))
+
+    op("V", ["Xf0", "Xf1", "Xf2", "Xf3"], ["fq", "fqs"], V.quantize_mx, T.fq[:], T.fqs[:], T.Xf[:])
+    mm("ps0", "vq", "vqs", 0, "fq", "fqs", 0, 256)
+    op("V", ["Ko", "colU"], ["prs"], vcp, T.prs[:].indirect(c("colU")), T.Ko[:])
+    dma("dend", [("Y", T.oc[:], T.fq[:].bitcast(dt.uint8), ["fq"], [])] + [("YS"[k % 2], T.osc[4 * k:4 * k + 4, :], T.fqs[32 * k:32 * k + 4, :], ["fqs"], []) for k in range(4)])
+    op("S", ["ps0"], ["yo"], act, T.yo[:], T.ps0[:, 0:256], AF.Copy)
+    op("V", ["prs"], ["pti"], vts, T.pti[:], T.prs[:], -0.498, None, A.add)
+    op("V", ["pti"], ["ptf"], vcp, T.ptf[:], T.pti[:])
+    dma("dend", [("S", T.y[:], T.yo[:], ["yo"], []), ("Y", T.pt[:], T.ptf[0::16, :], ["ptf"], [])])
+    for s, v in ends.items(): g.wait_ge(T.sem[s], v)
+    g.wait_ge(T.sem.snd, 8 * R)

@@ -1,11 +1,11 @@
 from concourse.mybir import dt, AluOpType as A, ActivationFunctionType as AF
 
 N, R, C = 8, 3, 256
-TW = 2816
-HW = 2824
-ZI = 2816
+HW = 2832
 NV = 7
-NS = 7
+ND = 2
+M = 12582912.0
+FAR = 4096.0
 F8 = "float8_e4m3fn_x4"
 LISTS = {}
 
@@ -27,39 +27,38 @@ def _scratch():
             LISTS[n] = (buf, at, w)
             at += (w + 15) // 16 * 16
         sb(buf, at, d)
-    lists("lstf", "float32", "kl el elf Dm De t16 Kl acc rl lo eqv dm of eqc dmc ofc ivl cf cp kl17 pls lk par", {"kl17": 17, "pls": 17, "lk": 32, "par": 4})
-    lists("lsti", "int32", "iB pl sh4 colI c_lo c_hi place sh3 tt ip iq", {"place": 17, "sh3": 17, "tt": 32, "ip": 2, "iq": 2})
-    lists("lstu", "uint16", "kapU rep oddl ul ru ou lou oc2 hu cu ku colU piU iu x40 x41 x42 x43 L2", {"L2": 34})
-    sb("iA iX amod prow pti", 256, "int32")
-    sb("mask m0 er V Krow k2 Ko mk2 sl SBt dd crow stw inv prs ior ptf yo keepf", 256)
+    lists("lstf", "float32", "kl el Kl acc rl rf sd0 sdx of pm cf cg plf par", {"sd0": 32, "sdx": 64, "of": 32})
+    lists("lsti", "int32", "iB pl ip iq", {"ip": 2, "iq": 4})
+    lists("lstu", "uint16", "kapU ul ru ou lou pu hu cu ku colU iu L", {})
+    sb("prow", 256, "int32")
+    sb("er Krow mk2 sl Ks kT los ivs ptk ptf yo", 256)
+    sb("AB", 512)
     sb("ks", 264)
-    sb("mkb mko keepb kval kvale mg mgo Wr kpw", 256, "bfloat16")
+    sb("mask iX c1 c2 keepb kval lor ivr stw gt gtT gm gm0 gk prw mid kuh", 256, "bfloat16")
+    sb("plc", 256, "float16")
     sb("junk", 256 * (16 - NV), "bfloat16")
-    sb("sgn", 256 * NS, "bfloat16")
     sb("cmp", 256 * NV, "bfloat16")
     sb("sc", 128 * NV + 128, "float16")
-    sb("sc2", 288)
     sb("h", HW + 256, "bfloat16")
-    sb("tabs", HW, "bfloat16")
-    sb("tab2", TW + 16, "bfloat16")
-    sb("gt gtT", 544, "bfloat16")
-    sb("Wc uin vin Bt0 Bt Bh Bm H", 512, "bfloat16")
-    sb("Ct", 4096, "bfloat16")
-    sb("Dt Z P F G XP Xf xin", 1024, "bfloat16")
-    sb("X", 1088, "bfloat16")
+    sb("tabs tab2", HW, "bfloat16")
+    sb("Wp", 2048, "bfloat16")
+    sb("uin vin Bt H", 512, "bfloat16")
+    sb("Ct sg", 4096, "bfloat16")
+    sb("Ws Z P F G Hg XP Xf xin", 1024, "bfloat16")
+    sb("X", 1032, "bfloat16")
     sb("EE one", 520, "bfloat16")
     for t in range(4): mx("ec%d" % t, "es%d" % t, 128)
-    for n, m, w in (("bc", "bs", 128), ("hc", "hs", 128), ("mc", "ms", 128), ("xq", "xs", 272), ("zq", "zs", 256), ("cq", "cs", 1024), ("dq", "dqs", 256),
+    for n, m, w in (("bc", "bs", 128), ("xq", "xs", 256), ("xr", "xt", 256), ("cq", "cs", 1024),
                     ("uq", "us", 128), ("u2", "u2s", 128), ("vq", "vqs", 128), ("wq", "wp", 512), ("fq", "fqs", 256)): mx(n, m, w)
     for k in range(R):
-        mx("pk%d" % k, "pp%d" % k, 128)
-        mx("lc%d" % k, "lp%d" % k, 128)
+        mx("zq%d" % k, "zs%d" % k, 256)
+        mx("lc%d" % k, "lp%d" % k, 256)
     for k in range(8): s["ps%d" % k] = ("psum", [128, 512], "float32")
     return s
 
 
 SCRATCH = _scratch()
-DSEM = ["dp", "drow", "dx", "du", "dw", "dv", "div", "dend"] + [n + str(k) for n in ("dV", "dlk", "dlo", "dk2", "dtab") for k in range(R + 1)]
+DSEM = ["dp", "drow", "dx", "du", "dw", "dv", "dend", "dpt"] + ["dtab%d" % k for k in range(R + 1)]
 SEMAPHORES = ["qV", "qS", "qT", "qG", "snd"] + ["arr%d" % k for k in range(R)] + DSEM
 
 
@@ -126,159 +125,155 @@ def rank_program(g, core, T, topo):
     V, S, PE = g.vector, g.scalar, g.tensor
     vts, vtt, vcp, vscan, act = V.tensor_scalar, V.tensor_tensor, V.tensor_copy, V.tensor_tensor_scan, S.activation
 
-    def quant(qn, sn, tn, a, n):
-        op("V", [tn], [qn, sn], V.quantize_mx, T[qn][:, 0:n], T[sn][:, 0:n], T[tn][:, a:a + 4 * n])
+    def quant(qn, sn, tn, a, n, rd=None):
+        op("V", rd or [tn], [qn, sn], V.quantize_mx, T[qn][:, 0:n], T[sn][:, 0:n], T[tn][:, a:a + 4 * n])
 
-    def mm(bank, lq, ls, la, rq, rs, ra, n, start=True, stop=True):
-        op("T", [lq, ls, rq, rs], [bank], PE.matmul_mx, T[bank][:, 0:n], T[lq][:, la:la + 128], T[ls][:, la:la + 128],
+    def mm(bank, lq, ls, la, rq, rs, ra, n, start=True, stop=True, key=None):
+        op("T", [lq, ls] + ([key] if key else [rq, rs]), [bank], PE.matmul_mx, T[bank][:, 0:n], T[lq][:, la:la + 128], T[ls][:, la:la + 128],
            T[rq][:, ra:ra + n], T[rs][:, ra:ra + n], start, stop, acc=not start)
 
-    dma("dp", [("Y", c("pl"), T.p[:], [], ["pl"])])
+    def hold(out, ok, cn, row, rk):
+        op("V", [cn, rk], [ok], vscan, out, T[cn][:], row, 0.0, A.add, A.min)
+
     dma("drow", [("YS"[x % 2], T.prow[x::16, :], T.p[:], [], ["prow"]) for x in range(16)])
+    dma("dp", [("Y", c("pl"), T.p[:], [], ["pl"])])
     dma("dx", [("Y", T.xin[:], T.x[:], [], ["xin"])])
-    dma("du", [("S", T.uin[:], T.u[:], [], ["uin"])])
+    dma("du", [("Y", T.uin[:], T.u[:], [], ["uin"])])
 
     def iota(n, pat, base=0, cm=0, small=False):
         out = c(n) if n in LISTS else T[n][:]
         if small: op("G", [], [n], g.iota, out, pat, base, cm, allow_small_or_imprecise_dtypes=True)
         else: op("G", [], [n], g.iota, out, pat, base, cm)
 
-    def zeros(n, w, after=()):
-        op("G", list(after), [n], g.iota, T[n][:], [[0, w]], 0, 0, allow_small_or_imprecise_dtypes=True)
-    iota("iB", [[1, 16]])
-    iota("iA", [[0, 256]], 0, 1)
-    iota("er", [[1, 256]], small=True)
-    iota("iX", [[0, 16], [1, 16]])
-    iota("V", [[1, 256]], small=True)
-    iota("kval", [[1, 16], [16, 16]], 1, small=True)
+    def zeros(n, a, b):
+        op("G", [], [n], g.iota, T[n][:, a:b], [[0, b - a]], 0, 0, allow_small_or_imprecise_dtypes=True)
+
+    def width(n):
+        return (2048 + 255 * n + 7) // 8 * 8
     iota("ip", [[0, 2]], 0, 1)
-    op("V", ["iA"], ["amod"], vts, T.amod[:], T.iA[:], 15, None, A.bitwise_and)
-    a16 = T.amod[:, 0:16]
-    op("V", ["iB"], ["of"], vts, c("of"), c("iB"), 16.0, None, A.mult)
-    op("V", ["amod"], ["t16"], vts, c("t16"), a16, 16.0, None, A.mult)
-    op("V", ["of", "amod"], ["el"], vtt, c("el"), c("of"), a16, A.add)
-    op("V", ["t16", "iB"], ["kl"], vtt, c("kl"), c("t16"), c("iB"), A.add)
-    op("S", ["er"], ["er"], act, T.er[:], T.er[:], AF.Copy, scale=1.0 / 256)
-    op("V", ["el"], ["elf"], vts, c("elf"), c("el"), 1.0 / 256, None, A.mult)
-    op("V", ["kl"], ["kapU"], vcp, c("kapU"), c("kl"))
+    iota("iB", [[1, 16]])
     op("V", [], ["one"], V.memset, T.one[:], 0.5)
-    op("V", [], ["Bt0"], V.memset, T.Bt0[:], 1.0)
-    op("V", [], ["ks"], V.memset, T.ks[:, 256:264], TW - 1.0)
-    op("V", [], ["sc"], V.memset, T.sc[:, 0:128], 0.0)
-    op("V", ["amod", "iX"], ["mask"], vtt, T.mask[:], T.amod[:], T.iX[:], A.is_equal)
-    op("V", ["iX"], ["keepf"], vts, T.keepf[:], T.iX[:], 1.0, None, A.min)
-    op("V", ["iX"], ["keepb"], vts, T.keepb[:], T.iX[:], 1.0, None, A.min)
-    op("V", ["pl", "elf"], ["Kl"], vtt, c("Kl"), c("pl"), c("elf"), A.add)
-    op("V", ["prow", "kapU", "er"], ["Krow"], vtt, T.Krow[:], T.prow[:].indirect(c("kapU")), T.er[:], A.add)
     op("G", ["one"], ["EE"], g.affine_select, T.EE[:], T.one[:], [[-1, 520]], A.is_equal, 0.0, 4, 4)
-    zeros("tab2", TW + 16)
-    op("G", ["Bt0"], ["Bt"], g.affine_select, T.Bt[:], T.Bt0[:], [[-16, 8], [0, 64]], A.is_ge, 0.0, 0, 1)
+    iota("kval", [[1, 256]], 1, small=True)
+    iota("iX", [[0, 16], [1, 16]], small=True)
+    zeros("h", 0, width(0) + 8)
+    iota("prw", [[0, 8], [1, 2], [0, 16]], small=True)
+    iota("gk", [[32, 8], [0, 2], [1, 16]], small=True)
+    op("G", ["one"], ["Bt"], g.affine_select, T.Bt[:], T.one[:, 0:512], [[-16, 8], [0, 64]], A.is_ge, 0.0, 0, 1)
     op("G", ["Bt"], ["Bt"], g.affine_select, T.Bt[:], T.Bt[:], [[16, 8], [0, 64]], A.is_ge, 0.0, 15, -1)
-    iota("kvale", [[1, 256]], 1, small=True)
-    zeros("Wc", 512)
-    zeros("Ct", 4096)
-    zeros("Dt", 1024)
+    iota("mid", [[1, 64], [-16, 4]], small=True)
+    op("V", [], ["kse"], V.memset, T.ks[:, 256:264], HW - 1.0)
+    op("V", [], ["sc"], V.memset, T.sc[:, 0:128], 0.0)
+    op("V", [], ["sd0"], V.memset, c("sd0"), 0.0)
+    op("V", ["ip"], ["iq0"], vts, c("iq", 0, 1), c("ip", 0, 1), 15, None, A.bitwise_and)
+    op("V", ["ip"], ["iq1"], vts, c("iq", 1, 2), c("ip", 0, 1), 4, 6, A.arith_shift_right, A.bitwise_and)
+    op("V", ["ip"], ["iq2"], vts, c("iq", 2, 3), c("ip", 0, 1), 16, None, A.bitwise_and)
+    op("V", ["iq0", "iq1", "iq2"], ["pa"], vcp, c("par", 0, 3), c("iq", 0, 3))
+    pa, pq, ph, pa16, pfix, pfix1, pown, ptab, pk = [c("par", k, k + 1) for k in range(9)]
+    op("V", ["iB", "pa"], ["el"], vts, c("el"), c("iB"), 16.0, pa, A.mult, A.add)
+    op("V", ["pa"], ["pa16"], vts, pa16, pa, 16.0, None, A.mult)
+    op("V", ["pa"], ["pfix"], vts, pfix, pa, -FAR, 15 * FAR, A.mult, A.add)
+    op("V", ["pa"], ["pfix1"], vts, pfix1, pa, -FAR, 15 * FAR - 1, A.mult, A.add)
+    op("V", ["pa"], ["pown"], vtt, pown, pa, pq, A.subtract)
+    op("V", ["pa"], ["ptab"], vts, ptab, pa, 8.0, None, A.is_lt)
+    op("V", ["pa"], ["pk"], vts, pk, pa, 15.0, None, A.is_equal)
+    op("V", ["iB", "pa16"], ["kapU"], vts, c("kapU"), c("iB"), pa16, None, A.add)
+    op("V", ["iB"], ["ul"], vts, c("ul"), c("iB"), 16.0, None, A.mult)
+    op("V", ["el"], ["kl"], vts, c("kl"), c("el"), 1.0 / 256, None, A.mult)
+    op("V", ["el"], ["sdd"], vts, c("sdx", 0, 32, 2), c("el"), M + HW - 1.0, None, A.add)
+    op("S", ["kval"], ["er"], act, T.er[:], T.kval[:], AF.Identity, scale=1.0 / 256, bias=-1.0 / 256)
+    for t in range(4): quant("ec%d" % t, "es%d" % t, "EE", 4 - t, 128)
+    op("V", ["pl", "kl"], ["Kl"], vtt, c("Kl"), c("pl"), c("kl"), A.add)
+    op("V", ["prow", "kapU", "er"], ["Krow"], vtt, T.Krow[:], T.prow[:].indirect(c("kapU")), T.er[:], A.add)
 
     def consts1():
-        op("V", [], ["h"], V.memset, T.h[:], 0.0)
-        op("V", ["kl"], ["Dm"], vts, c("Dm"), c("kl"), HW - 1.0, None, A.add)
-        op("V", ["ip"], ["iq"], vts, c("iq"), c("ip"), 4, 1, A.arith_shift_right, A.bitwise_and)
-        op("V", ["iq"], ["par"], vcp, c("par", 0, 1), c("iq", 0, 1))
-        op("V", ["par"], ["par"], vts, c("par", 1, 2), c("par", 0, 1), -1.0, 1.0, A.mult, A.add)
-        op("V", ["par"], ["par"], vts, c("par", 2, 4), c("par", 0, 2), float(ZI), None, A.mult)
-        for t in range(4): quant("ec%d" % t, "es%d" % t, "EE", 4 - t, 128)
+        op("V", ["iX", "pa"], ["mask"], vts, T.mask[:], T.iX[:], pa, None, A.is_equal)
 
     def consts2():
-        op("V", ["kl"], ["kl17"], vcp, c("kl17", 0, 16), c("kl"))
-        op("V", ["kl"], ["kl17"], vts, c("kl17", 16, 17), c("kl", 15, 16), 1.0, None, A.add, acc=True)
-        op("V", [], ["sc2"], V.memset, T.sc2[:, 0:16], 0.0)
-        op("V", ["el"], ["De"], vts, c("De"), c("el"), 256.0, None, A.add)
-        op("S", ["Bt"], ["Bh"], act, T.Bh[:], T.Bt[:], AF.Copy, scale=0.5)
-        for t in range(4): op("S", ["Bt"], ["Bm"], act, T.Bm[:, t::4], T.Bt[:, t::4], AF.Copy, scale=1.0 if 8 + t < 16 - NS else 0.5, acc=t > 0)
-        op("V", ["iB"], ["ul"], vts, c("ul"), c("iB"), 16.0, None, A.mult)
-        op("V", ["iB"], ["rep"], vts, c("rep"), c("iB"), 16.0, 15.0, A.mult, A.add)
-        op("V", ["el"], ["oddl"], vts, c("oddl"), c("el"), 2.0, 1.0, A.mult, A.add)
-        quant("uq", "us", "uin", 0, 128)
-        op("V", [], ["crow"], V.memset, T.crow[:, 0:256 - 16 * NS], 8.0 * NS)
-        op("V", ["uq", "ul"], ["u2"], vcp, T.u2[:].bitcast(dt.uint32), T.uq[:].bitcast(dt.uint32).indirect(c("ul", 0, 8)))
-        op("V", ["us", "ul"], ["u2s"], vcp, T.u2s[:], T.us[:].indirect(c("ul", 0, 8)))
-        op("V", [], ["crow"], V.memset, T.crow[:, 256 - 16 * NS:256], 8.0 * NS - 8, acc=True)
-        op("V", ["amod", "iX"], ["m0"], vtt, T.m0[:], T.amod[:], T.iX[:], A.is_lt)
-        quant("bc", "bs", "Bt", 0, 128)
-        op("V", ["m0"], ["m0"], vts, T.m0[:], T.m0[:], -1e-35, None, A.mult)
+        op("S", ["mask"], ["c2"], act, T.c2[:], T.mask[:], AF.Copy, scale=FAR)
+        op("S", ["junk"], ["tab2"], act, T.tab2[:, 0:2304], T.junk[:, 0:2304], AF.Identity, scale=0.0, bias=1.0)
+        op("S", ["mask"], ["c1"], act, T.c1[:], T.mask[:], AF.Identity, scale=18 * FAR, bias=-FAR)
+        op("S", ["iX"], ["keepb"], act, T.keepb[:], T.iX[:], AF.Sign)
 
-    def order_begin(n):
-        dma("dV%d" % n, [("Y", T.V[0::2, :], T.Krow[0::2, :], ["Krow"], ["V"])])
+    def consts3():
+        op("V", ["prw", "pown", "ptab"], ["gm0"], vts, T.gm0[:], T.prw[:], pown, ptab, A.not_equal, A.mult)
+        op("V", ["gk", "pa", "pk"], ["gk"], vts, T.gk[:], T.gk[:], ph, pk, A.add, A.mult)
+        quant("uq", "us", "uin", 0, 128)
+        op("V", ["gm0", "gk"], ["gm"], vtt, T.gm[:], T.gm0[:], T.gk[:], A.add)
+        op("V", ["uq", "ul"], ["u2"], vcp, T.u2[:].bitcast(dt.uint32), T.uq[:].bitcast(dt.uint32).indirect(c("ul", 0, 8)))
+        op("V", ["mid", "pa"], ["mid"], vts, T.mid[:], T.mid[:], pa, 0.5, A.is_gt, A.subtract)
+        quant("bc", "bs", "Bt", 0, 128)
+
+    def ranks(n):
+        if n:
+            hold(T.Ks[:], "Ks", "c1", T.Krow[:], "Krow")
+            op("S", ["Ks", "pfix"], ["Kl"], act, c("Kl", NV, 16), T.Ks[:, 16 * NV + 15::16], AF.Identity, bias=pfix)
         for b in range(NV, 16):
             op("S", ["Krow", "Kl"], ["junk", "acc"], act, T.junk[:, 256 * (b - NV):256 * (b - NV) + 256], T.Krow[:], AF.Sign, bias=c("Kl", b, b + 1), scale=-1.0,
                accum_out=c("acc", b, b + 1), acc=b > NV)
         for b in range(NV):
-            op("V", ["Krow", "Kl"], ["cmp"], vts, T.cmp[:, 256 * b:256 * b + 256], T.Krow[:], c("Kl", b, b + 1), None, A.is_lt, acc=True)
+            o = T.cmp[:, 256 * b:256 * b + 256]
+            if n: op("V", ["Krow", "Ks", "pfix"], ["cmp"], vts, o, T.Krow[:], pfix, T.Ks[:, 16 * b + 15:16 * b + 16], A.subtract, A.is_lt, acc=True)
+            else: op("V", ["Krow", "Kl"], ["cmp"], vts, o, T.Krow[:], c("Kl", b, b + 1), None, A.is_lt, acc=True)
         w = 128 * NV
         op("V", ["cmp"], ["sc"], vscan, T.sc[:, 128:128 + w], T.cmp[:, 0:2 * w:2], T.cmp[:, 1:2 * w:2], 0.0, A.add, A.add)
-        op("V", ["acc"], ["ruS"], vts, c("ru", NV, 16), c("acc", NV, 16), 0.5, 127.5, A.mult, A.add)
         op("V", ["sc"], ["rl"], vtt, c("rl", 0, NV), T.sc[:, 255::128], T.sc[:, 127:127 + w:128], A.subtract)
         op("V", ["rl"], ["ruV"], vcp, c("ru", 0, NV), c("rl", 0, NV))
-        op("V", ["ruS", "ruV", "V"], ["ks"], vcp, T.ks[:, 0:256].indirect(c("ru")), T.V[:])
-        dma("dlk%d" % n, [("Y", c("lk", 0, 16), T.ks[0::16, 0:256], ["ks"], ["lk"]), ("Y", c("lk", 16, 32), T.ks[0::16, 1:257], ["ks"], ["lk"])])
-        dma("dlo%d" % n, [("Y", c("lo"), T.ks[1::16, 0:256], ["ks"], ["lo"])])
-        dma("dk2%d" % n, [("Y", T.k2[0::2, :], T.ks[0::2, 0:256], ["ks"], ["k2"]), ("Y", T.k2[1::2, :], T.ks[0::2, 0:256], ["ks"], ["k2"])])
+        if n == 0: consts1()
+        op("V", ["acc"], ["ruS"], vts, c("ru", NV, 16), c("acc", NV, 16), 0.5, 127.5, A.mult, A.add)
 
-    def order_tables(n):
-        t0, t1 = c("tt", 0, 16), c("tt", 31, 32)
-        op("V", ["lk"], ["tt"], vts, c("tt"), c("lk"), -0.498, None, A.add)
-        op("V", ["tt"], ["eqv"], vtt, c("eqv"), t0, c("tt", 16, 32), A.is_equal)
-        op("V", ["eqv", "Dm"], ["dm"], vtt, c("dm"), c("eqv"), c("Dm"), A.mult)
-        op("V", ["tt", "dm"], ["of"], vtt, c("of"), c("dm"), t0, A.max)
-        op("V", ["of"], ["ou"], vts, c("ou"), c("of"), 1.0, None, A.add)
+    def tables(n):
+        w = width(n)
+        op("V", ["ruS", "ruV", "Krow", "kse"], ["ks"], vcp, T.ks[:, 0:256].indirect(c("ru")), T.Krow[:])
+        hold(T.AB[:, 0:256], "A", "c2", T.ks[:, 0:256], "ks")
+        hold(T.AB[:, 256:512], "B", "c2", T.ks[:, 1:257], "ks")
+        op("V", ["A", "B"], ["sdp"], vts, c("sdx", 1, 64, 2), T.AB[:, 15::16], -0.498, M, A.add, A.add)
+        op("V", ["sdp"], ["sd0"], vtt, c("sd0", 1, 32, 2), c("sdx", 1, 32, 2), c("sdx", 33, 64, 2), A.is_equal)
+        op("V", ["sd0", "sdp", "sdd"], ["of"], vscan, c("of"), c("sd0"), c("sdx", 0, 32), 0.0, A.mult, A.max)
+        op("V", ["of"], ["ou"], vts, c("ou"), c("of", 1, 32, 2), 1.0 - M, None, A.add)
         op("V", ["ou", "kval"], ["h"], vcp, T.h[:].indirect(c("ou")), T.kval[:])
-        op("V", ["h"], ["tabs"], vscan, T.tabs[:], T.h[:, 0:HW], T.h[:, 0:HW], 0.0, A.max, A.max)
+        op("V", ["h"], ["tabs"], vscan, T.tabs[:, 0:w + 8], T.h[:, 0:w + 8], T.h[:, 0:w + 8], 0.0, A.max, A.max)
         items = []
         for e in range(N):
-            if e < N - 1: items.append((T.tab2[17 * e + 16::16, 0:TW], T.tabs[16 * e:16 * e + 7 - e, 1:TW + 1]))
-            if e: items.append((T.tab2[e:16 * e:16, 0:TW], T.tabs[16 * e:16 * e + e, 0:TW]))
+            hs = e + e % 2
+            if hs < N: items.append((T.tab2[16 * hs + e::16, 0:w], T.tabs[16 * e:16 * e + N - hs, 1:w + 1]))
+            if hs: items.append((T.tab2[e:16 * hs:16, 0:w], T.tabs[16 * e + 8:16 * e + 8 + hs, 0:w]))
         dma("dtab%d" % n, [("YS"[k % 2], o, i, ["tabs"], ["tab2"]) for k, (o, i) in enumerate(items)])
-        op("V", ["tt", "par"], ["L2a"], vts, c("L2", 0, 32, 2), t0, c("par", 1, 2), c("par", 2, 3), A.mult, A.add)
-        op("V", ["tt", "par"], ["L2b"], vts, c("L2", 1, 32, 2), t0, c("par", 0, 1), c("par", 3, 4), A.mult, A.add)
-        op("V", ["tt", "par"], ["L2c"], vts, c("L2", 32, 33), t1, c("par", 1, 2), c("par", 2, 3), A.mult, A.add)
-        op("V", ["tt", "par"], ["L2d"], vts, c("L2", 33, 34), t1, c("par", 0, 1), c("par", 3, 4), A.mult, A.add)
-        if n < R: zeros("h", HW + 256, ["tabs"])
+        if 0 < n < R: zeros("h", 0, width(n + 1) + 8)
 
-    def order_places():
-        op("V", ["tab2", "L2a", "L2b", "L2c", "L2d"], ["gt"], vcp, T.gt[:], T.tab2[:].indirect(c("L2")))
+    def pairs(row, key):
+        op("V", [key], ["kT"], V.transpose, T.kT[:], row)
+        op("V", ["kT"], ["pm"], vts, c("pm"), T.kT[:, 0::16], -0.498, M, A.add, A.add)
+        op("V", ["pm"], ["L"], vts, c("L"), c("pm"), -M, None, A.add)
+
+    def slots(key, outs):
+        op("V", ["ruS", "ruV", "kval"], ["lor"], vcp, T.lor[:].indirect(c("ru")), T.kval[:])
+        hold(T.los[:], "los", "c1", T.lor[:], "lor")
+        op("V", ["los", "pfix1"], ["lou"], vts, c("lou"), T.los[:, 15::16], pfix1, None, A.add)
+        for t in range(4):
+            op("S", ["F%d" % t, "lou"], ["%s%d" % (key, t)], act, outs[t], T.F[:, 256 * t:256 * t + 256].indirect(c("lou")), AF.Copy)
+
+    def places(n, gm):
+        op("V", ["tab2", "L", gm], ["gt"], vtt, T.gt[:], T.tab2[:, 0:width(n)].indirect(c("L")), T[gm][:], A.mult)
         op("V", ["gt"], ["gtT"], V.transpose, T.gtT[:], T.gt[:])
-        op("V", ["gtT"], ["sc2"], vscan, T.sc2[:, 16:288], T.gtT[:, 0::2], T.gtT[:, 1::2], 0.0, A.add, A.add)
-        op("V", ["sc2"], ["pls"], vtt, c("pls"), T.sc2[:, 31::16], T.sc2[:, 15:287:16], A.subtract)
-        op("V", ["pls", "kl17"], ["place"], vtt, c("place"), c("pls"), c("kl17"), A.add)
-
-    def keep_keys():
-        op("S", ["k2", "kapU"], ["Ko"], act, T.Ko[:], T.k2[:].indirect(c("kapU")), AF.Copy)
+        op("V", ["gtT", "keepb"], ["plc"], vscan, T.plc[:], T.keepb[:], T.gtT[:], 0.0, A.mult, A.add)
 
     def cells(n):
-        op("V", ["place"], ["sh3"], vts, c("sh3"), c("place"), 3, None, A.arith_shift_right)
-        op("V", ["sh3"], ["eqc"], vtt, c("eqc"), c("sh3", 0, 16), c("sh3", 1, 17), A.is_equal)
-        op("V", ["eqc", "De"], ["dmc"], vtt, c("dmc"), c("eqc"), c("De"), A.mult)
-        op("V", ["dmc", "sh3"], ["ofc"], vtt, c("ofc"), c("dmc"), c("sh3", 0, 16), A.max)
-        op("V", ["ofc"], ["oc2"], vcp, c("oc2"), c("ofc"))
-        op("V", ["oc2", "kvale"], ["Wc"], vcp, T.Wc[:].indirect(c("oc2")), T.kvale[:])
-        op("V", ["Wc"], ["kpw"], vts, T.kpw[:], T.Wc[:, 0:256], 0.0, None, A.is_equal)
-        op("V", ["Wc", "kpw"], ["Wr"], vscan, T.Wr[:], T.kpw[:], T.Wc[:, 0:256], 0.0, A.mult, A.add)
-        if n < R - 1: zeros("Wc", 512, ["Wr"])
-        op("V", ["Wr", "mask"], ["mkb"], vtt, T.mkb[:], T.Wr[:], T.mask[:], A.mult)
-        op("V", ["mkb", "keepb"], ["mko"], vscan, T.mko[:], T.keepb[:], T.mkb[:], 0.0, A.mult, A.add)
-        op("V", ["mko"], ["ku"], vts, c("ku"), T.mko[:, 15::16], -1.0, 0.0, A.add, A.max)
+        op("V", ["plc"], ["pu"], vcp, c("pu"), T.plc[:, 15::16])
+        op("V", ["pu", "kval"], ["Wp"], vcp, T.Wp[:].indirect(c("pu")), T.kval[:])
+        op("V", ["Wp"], ["Ws"], vscan, T.Ws[:], T.Wp[:, 0::2], T.Wp[:, 1::2], 1.0, A.max, A.max)
+        hold(T.kuh[:], "kuh", "c2", T.Ws[:, 3::4], "Ws")
+        op("V", ["kuh"], ["ku"], vts, c("ku"), T.kuh[:, 15::16], -1.0, None, A.add)
 
     XK = ["X0", "X1", "X2", "X3"]
 
-    def tail():
-        op("V", XK, ["Xt"], vcp, T.X[:, 1024:1084], T.X[:, 4:64])
-        op("S", XK, ["Xu"], act, T.X[:, 1084:1088], T.X[:, 1020:1024], AF.Copy)
-        op("V", XK + ["Xt", "Xu"], ["xq", "xs"], V.quantize_mx, T.xq[:], T.xs[:], T.X[:])
-
-    def unpack_pairs():
+    def unpack():
+        op("S", XK, ["Xu"], act, T.X[:, 1024:1028], T.X[:, 1020:1024], AF.Copy)
+        quant("xq", "xs", "X", 0, 256, XK)
+        quant("xr", "xt", "X", 4, 256, XK + ["Xu"])
         for t in range(4):
             mm("ps%d" % t, "ec%d" % t, "es%d" % t, 0, "xq", "xs", 0, 256, True, False)
-            mm("ps%d" % t, "ec%d" % t, "es%d" % t, 0, "xq", "xs", 16, 256, False, True)
+            mm("ps%d" % t, "ec%d" % t, "es%d" % t, 0, "xr", "xt", 0, 256, False, True)
             op("S", ["ps%d" % t], ["P%d" % t], act, T.P[:, 256 * t:256 * t + 256], T["ps%d" % t][:, 0:256], AF.Copy)
         for t in range(4):
             mm("ps%d" % (4 + t), "ec%d" % t, "es%d" % t, 0, "xq", "xs", 0, 256)
@@ -287,131 +282,139 @@ def rank_program(g, core, T, topo):
         for t in range(4):
             op("S", ["ps%d" % (4 + t)], ["F%d" % t], act, T.F[:, 256 * t:256 * t + 256], T["ps%d" % (4 + t)][:, 0:256], AF.Copy, scale=2.0)
 
-    def deal(t, key, out):
-        op("V", ["H%d" % t, "hu", "G%d" % t], [key], vtt, out, T.H[:, 128 * t:128 * t + 128].indirect(c("hu")), T.G[:, 256 * t:256 * t + 256], A.add)
+    def deal(src, keys, outs):
+        for t in range(4 - ND, 4):
+            op("S", ["H%d" % t, "hu"], ["Hg%d" % t], act, T.Hg[:, 256 * t:256 * t + 256], T.H[:, 128 * t:128 * t + 128].indirect(c("hu")), AF.Copy)
+        for t in range(4):
+            f = T[src][:, 256 * t:256 * t + 256]
+            if t < 4 - ND: op("V", ["H%d" % t, "hu", "%s%d" % (src, t)], [keys[t]], vtt, outs[t], T.H[:, 128 * t:128 * t + 128].indirect(c("hu")), f, A.add)
+            else: op("V", ["Hg%d" % t, "%s%d" % (src, t)], [keys[t]], vtt, outs[t], T.Hg[:, 256 * t:256 * t + 256], f, A.add)
 
-    order_begin(0)
-    consts1()
-    order_tables(0)
-    for t in range(4):
-        op("V", ["lo"], ["x4%d" % t], vts, c("x4%d" % t), c("lo"), 4.0, float(t), A.mult, A.add)
-    for t in range(2):
-        op("S", ["xin", "x4%d" % t], ["X%d" % t], act, T.X[:, t:1024:4], T.xin[:].indirect(c("x4%d" % t)), AF.Copy)
-    for t in range(2, 4):
-        op("V", ["xin", "x4%d" % t], ["X%d" % t], vcp, T.X[:, t:1024:4], T.xin[:].indirect(c("x4%d" % t)))
-    tail()
-    unpack_pairs()
+    ranks(0)
     consts2()
-    order_places()
+    for t in range(4): op("S", ["xin"], ["F%d" % t], act, T.F[:, 256 * t:256 * t + 256], T.xin[:, t::4], AF.Copy)
+    tables(0)
+    zeros("Wp", 0, 2048)
+    slots("X", [T.X[:, t:1024:4] for t in range(4)])
+    pairs(T.ks[:, 0:256], "ks")
+    consts3()
+    op("S", ["us", "ul"], ["u2s"], act, T.u2s[:], T.us[:].indirect(c("ul", 0, 8)), AF.Copy)
+    unpack()
+    places(0, "gm")
     cells(0)
-    quant("hc", "hs", "Bh", 0, 128)
-    quant("mc", "ms", "Bm", 0, 128)
-    keep_keys()
-    dma("dw", [("Y", T.wq[:].bitcast(dt.uint8), T.wc[:], [], ["wq"]), ("Y", T.wp[:], T.ws[:], [], ["wp"])])
+    dma("dw", [("Y", T.wq[:].bitcast(dt.uint8), T.wc[:], ["gt"], ["wq"]), ("Y", T.wp[:], T.ws[:], [], ["wp"])])
     dma("dv", [("Y", T.vin[:], T.v[:], [], ["vin"])])
 
-    nxt = T.cores[(rank + 1) % N]
+    nxt = T.cores[(rank + 1) % len(T.cores)]
     rid, pid, sen = topo.addr(nxt)
     m4 = sum(1 << e for e in topo.engines(core, nxt)[0:4])
 
     for n in range(R):
+        zq, zs = "zq%d" % n, "zs%d" % n
         for t in (0, 1):
             op("V", ["P%d" % t, "ku"], ["Z%d" % t], vcp, T.Z[:, t:1024:4], T.P[:, 256 * t:256 * t + 256].indirect(c("ku")))
         for t in (2, 3):
             op("S", ["P%d" % t, "ku"], ["Z%d" % t], act, T.Z[:, t:1024:4], T.P[:, 256 * t:256 * t + 256].indirect(c("ku")), AF.Copy)
-        op("V", ["Z0", "Z1", "Z2", "Z3"], ["zq", "zs"], V.quantize_mx, T.zq[:], T.zs[:], T.Z[:])
-        mm("ps0", "u2", "u2s", 0, "zq", "zs", 0, 256)
-        mm("ps1", "u2", "u2s", 0, "zq", "zs", 0, 256)
-        op("V", ["sh3"], ["cu"], vcp, c("cu"), c("sh3", 0, 16))
+        op("V", ["plc"], ["cu"], vts, c("cu"), T.plc[:, 15::16], 0.125, -0.4375, A.mult, A.add)
+        quant(zq, zs, "Z", 0, 256, ["Z0", "Z1", "Z2", "Z3"])
+        need("G", [last[zq]])
+        g.remote_dma(T["lc%d" % n][:].bitcast(dt.uint8), T[zq][:].bitcast(dt.uint8), T.sem["arr%d" % n], T.sem.snd, pid, rid, m4)
+        g.remote_dma(T["lp%d" % n][:], T[zs][:], T.sem["arr%d" % n], T.sem.snd, pid, rid, m4)
+        if n == 0: zeros("h", 0, width(1) + 8)
+        if n < R - 1: zeros("Wp", 0, 2048)
+        mm("ps0", "u2", "u2s", 0, zq, zs, 0, 256)
+        mm("ps1", "u2", "u2s", 0, zq, zs, 0, 256)
         op("V", ["ps0", "mask"], ["mk2"], vtt, T.mk2[:], T.ps0[:, 0:256], T.mask[:], A.mult)
-        op("V", ["mk2", "keepf"], ["sl"], vscan, T.sl[:], T.keepf[:], T.mk2[:], 0.0, A.mult, A.add)
-        for j in range(NS):
-            b = 16 - NS + j
-            op("S", ["ps1", "sl"], ["sg%d" % j], act, T.sgn[:, 256 * j:256 * j + 256], T.ps1[:, 0:256], AF.Sign, bias=T.sl[:, 16 * b + 15:16 * b + 16], scale=-1.0)
-            if j == 0:
-                op("S", ["zs", "oddl"], ["pp%d" % n], act, T["pp%d" % n][:], T.zs[:].indirect(c("oddl", 0, 8)), AF.Copy)
-                op("S", ["sl", "rep"], ["SBt"], act, T.SBt[:], T.sl[:].indirect(c("rep")), AF.Copy)
-        for j in range(NS):
-            b = 16 - NS + j
-            o, ck, ce = 1024 * (b // 4) + b % 4, "S%d" % (b // 4), 1024 * (b // 4) + 1024
-            op("S", ["sg%d" % j, "Ct"], [ck], act, T.Ct[:, o:o + 64 * b:4], T.sgn[:, 256 * j:256 * j + 16 * b], AF.Sign, bias=-0.5, scale=-1.0, acc=True)
-            if b < 15: op("S", ["sg%d" % j, "Ct"], [ck], act, T.Ct[:, o + 64 * b + 64:ce:4], T.sgn[:, 256 * j + 16 * b + 16:256 * j + 256], AF.Sign, bias=0.5, scale=-1.0, acc=True)
-        for b in range(16 - NS):
-            k = b // 4
-            o, s1 = 1024 * k + b % 4, T.sl[:, 16 * b + 15:16 * b + 16]
-            if b: op("V", ["ps0", "sl", "Ct"], ["C%d" % k], vts, T.Ct[:, o:o + 64 * b:4], T.ps0[:, 0:16 * b], s1, None, A.is_gt, acc=True)
-            op("V", ["ps0", "sl", "Ct"], ["C%d" % k], vts, T.Ct[:, o + 64 * b + 64:1024 * k + 1024:4], T.ps0[:, 16 * b + 16:256], s1, None, A.is_ge, acc=True)
-            if b == 1:
-                op("V", ["zq", "oddl"], ["pk%d" % n], vcp, T["pk%d" % n][:].bitcast(dt.uint32), T.zq[:].bitcast(dt.uint32).indirect(c("oddl", 0, 8)))
-            if b == 7: op("V", ["C0", "C1", "Ct"], ["cq0"], V.quantize_mx, T.cq[:, 0:512], T.cs[:, 0:512], T.Ct[:, 0:2048])
-        need("G", [last["pk%d" % n], last["pp%d" % n]])
-        g.remote_dma(T["lc%d" % n][:].bitcast(dt.uint8), T["pk%d" % n][:].bitcast(dt.uint8), T.sem["arr%d" % n], T.sem.snd, pid, rid, m4)
-        g.remote_dma(T["lp%d" % n][:], T["pp%d" % n][:], T.sem["arr%d" % n], T.sem.snd, pid, rid, m4)
-        op("V", ["ps0", "SBt"], ["dd"], vtt, T.dd[:], T.ps0[:, 0:256], T.SBt[:], A.subtract)
-        op("V", ["dd", "m0"], ["Dt"], vtt, T.Dt[:, 0::4], T.dd[:], T.m0[:], A.is_gt)
-        op("V", ["C2", "S2", "Ct"] if NS < 8 else ["S2", "Ct"], ["cq2"], V.quantize_mx, T.cq[:, 512:768], T.cs[:, 512:768], T.Ct[:, 2048:3072])
-        op("V", ["Dt"], ["dq"], V.quantize_mx, T.dq[:], T.dqs[:], T.Dt[:])
-        op("V", ["S3", "Ct"], ["cq3"], V.quantize_mx, T.cq[:, 768:1024], T.cs[:, 768:1024], T.Ct[:, 3072:4096])
+        op("V", ["mk2", "keepb"], ["sl"], vscan, T.sl[:], T.keepb[:], T.mk2[:], 0.0, A.mult, A.add)
 
-        def total(lq, ls, rq, rs, key, ra, start, stop):
-            op("T", [lq, ls, key], ["ps2"], PE.matmul_mx, T.ps2[:, 0:256], T[lq][:], T[ls][:], T[rq][:, ra:ra + 256], T[rs][:, ra:ra + 256], start, stop, acc=not start)
-        total("bc", "bs", "cq", "cs", "cq0", 0, True, False)
-        total("bc", "bs", "cq", "cs", "cq0", 256, False, False)
-        total("mc", "ms", "cq", "cs", "cq2", 512, False, False)
-        total("bc", "bs", "dq", "dqs", "dq", 0, False, False)
-        total("hc", "hs", "cq", "cs", "cq3", 768, False, True)
-        op("V", ["ps2", "crow"], ["stw"], vtt, T.stw[:], T.ps2[:, 0:256], T.crow[:], A.add)
-        op("V", ["stw", "cu", "mask"], ["mg"], vtt, T.mg[:], T.stw[:].indirect(c("cu")), T.mask[:], A.mult)
-        op("V", ["stw", "cu", "Ko"], ["Krow"], vtt, T.Krow[:], T.stw[:].indirect(c("cu")), T.Ko[:], A.add)
-        op("V", ["mg", "keepb"], ["mgo"], vscan, T.mgo[:], T.keepb[:], T.mg[:], 0.0, A.mult, A.add)
-        op("V", ["mgo", "lk"], ["Kl"], vtt, c("Kl"), T.mgo[:, 15::16], c("lk", 0, 16), A.add)
-        order_begin(n + 1)
+        def signs(k, lo, hi):
+            for t in range(4):
+                b = 4 * k + t
+                op("S", ["ps1", "sl"], ["sg%d" % k], act, T.sg[:, 1024 * k + 4 * lo + t:1024 * k + 4 * hi:4], T.ps1[:, lo:hi], AF.Sign,
+                   bias=T.sl[:, 16 * b + 15:16 * b + 16], scale=-1.0, acc=t > 0)
+
+        def direct(k, lo, hi, how):
+            for t in range(4):
+                b = 4 * k + t
+                op("V", ["ps0", "sl"], ["Cd%d" % k], vts, T.Ct[:, 1024 * k + 4 * lo + t:1024 * k + 4 * hi:4], T.ps0[:, lo:hi], T.sl[:, 16 * b + 15:16 * b + 16], None, how, acc=t > 0)
+
+        def middle(k):
+            a = 1280 * k
+            op("V", ["sg%d" % k, "mid"], ["Cm%d" % k], vtt, T.Ct[:, a:a + 256], T.sg[:, a:a + 256], T.mid[:], A.is_lt)
+
+        def side(q, k, right):
+            a, b = (1280 * k + 256, 1024 * k + 1024) if right else (1024 * k, 1280 * k)
+            key = "C%s%d" % ("lr"[right], k)
+            if q == "V": op("V", ["sg%d" % k], [key], vts, T.Ct[:, a:b], T.sg[:, a:b], 0.0, None, A.is_le if right else A.is_lt)
+            elif right: op("S", ["sg%d" % k], [key], act, T.Ct[:, a:b], T.sg[:, a:b], AF.Sign, bias=1.0, scale=-1.0)
+            else: op("S", ["sg%d" % k], [key], act, T.Ct[:, a:b], T.sg[:, a:b], AF.Relu, scale=-1.0)
+
+        def total(k, keys, start, stop):
+            op("V", keys, ["cq%d" % k], V.quantize_mx, T.cq[:, 256 * k:256 * k + 256], T.cs[:, 256 * k:256 * k + 256], T.Ct[:, 1024 * k:1024 * k + 1024])
+            mm("ps2", "bc", "bs", 0, "cq", "cs", 256 * k, 256, start, stop, "cq%d" % k)
+        signs(0, 0, 64)
+        signs(1, 0, 256)
+        signs(3, 192, 256)
+        signs(2, 0, 256)
+        side("S", 2, 0)
+        direct(0, 64, 256, A.is_ge)
+        middle(0)
+        total(0, ["Cd0", "Cm0"], True, False)
+        direct(3, 0, 192, A.is_gt)
+        side("V", 1, 0)
+        side("V", 1, 1)
+        middle(1)
+        total(1, ["Cl1", "Cr1", "Cm1"], False, False)
+        middle(3)
+        total(3, ["Cd3", "Cm3"], False, False)
+        middle(2)
+        side("V", 2, 1)
+        total(2, ["Cl2", "Cr2", "Cm2"], False, True)
+        op("V", ["ps2"], ["stw"], vts, T.stw[:], T.ps2[:, 0:256], 2.0, None, A.mult)
+        op("V", ["stw", "cu", "ks"], ["Krow"], vtt, T.Krow[:], T.stw[:].indirect(c("cu")), T.ks[:, 0:256], A.add)
+        ranks(n + 1)
         unpack_keep()
-        if n == R - 1: quant("vq", "vqs", "vin", 0, 128)
-        order_tables(n + 1)
-        op("V", ["lo"], ["lou"], vcp, c("lou"), c("lo"))
-        for t in range(4):
-            op("S", ["F%d" % t, "lou"], ["G%d" % t], act, T.G[:, 256 * t:256 * t + 256], T.F[:, 256 * t:256 * t + 256].indirect(c("lou")), AF.Copy)
+        if n == 0: op("S", ["junk"], ["tab2"], act, T.tab2[:, 2304:HW], T.junk[:, 0:HW - 2304], AF.Identity, scale=0.0, bias=1.0)
         need("T", [("arr%d" % n, 8, "R", {})])
         ends["arr%d" % n] = 8
         for t in range(4):
-            mm("ps%d" % (4 + t), "wq", "wp", 128 * t, "lc%d" % n, "lp%d" % n, 0, 128)
-            op("S", ["ps%d" % (4 + t)], ["H%d" % t], act, T.H[:, 128 * t:128 * t + 128], T["ps%d" % (4 + t)][:, 0:128], AF.Copy, scale=0.03125)
-        keep_keys()
-        if n == R - 1:
-            op("G", [], ["ior"], g.iota, T.ior[:], [[1, 256]], 0, 0, allow_small_or_imprecise_dtypes=True)
-            op("V", ["lk", "tt"], ["cf"], vtt, c("cf"), c("lk", 0, 16), c("tt", 0, 16), A.subtract)
-            op("V", ["cf"], ["colI"], vts, c("colI"), c("cf"), 256.0, None, A.mult)
-            op("V", ["colI"], ["c_lo"], vts, c("c_lo"), c("colI"), 15, None, A.bitwise_and)
-            op("V", ["colI"], ["c_hi"], vts, c("c_hi"), c("colI"), 4, None, A.arith_shift_right)
-            op("V", ["colI"], ["colU"], vcp, c("colU"), c("colI"))
-            op("V", ["c_lo"], ["cf"], vts, c("cf"), c("c_lo"), 16.0, None, A.mult)
-            op("V", ["cf", "c_hi"], ["cp"], vtt, c("cp"), c("cf"), c("c_hi"), A.add)
-            op("V", ["cp"], ["piU"], vcp, c("piU"), c("cp"))
-            op("V", ["piU", "ior"], ["inv"], vcp, T.inv[:].indirect(c("piU")), T.ior[:])
-            dma("div", [("Y", c("ivl"), T.inv[0::16, :], ["inv"], ["ivl"])])
-        order_places()
-        op("V", ["place"], ["sh4"], vts, c("sh4"), c("place", 0, 16), 4, None, A.arith_shift_right)
-        op("V", ["sh4"], ["hu"], vcp, c("hu"), c("sh4"))
+            mm("ps%d" % (4 + t), "wq", "wp", 128 * t, "lc%d" % n, "lp%d" % n, 0, 256)
+            op("S", ["ps%d" % (4 + t)], ["H%d" % t], act, T.H[:, 128 * t:128 * t + 128], T["ps%d" % (4 + t)][:, 1:256:2], AF.Copy, scale=0.03125)
+        tables(n + 1)
         if n < R - 1:
-            for t in range(4): deal(t, "X%d" % t, T.X[:, t:1024:4])
-            tail()
-            unpack_pairs()
+            slots("G", [T.G[:, 256 * t:256 * t + 256] for t in range(4)])
+            pairs(T.ks[:, 0:256], "ks")
+            if n == R - 2:
+                op("V", ["sdp"], ["cf"], vts, c("cf"), c("sdx", 1, 32, 2), -M, None, A.add)
+                op("V", ["A", "cf"], ["cg"], vtt, c("cg"), T.AB[:, 15:256:16], c("cf"), A.subtract)
+                op("V", ["cg"], ["colU"], vts, c("colU"), c("cg"), 256.0, None, A.mult)
+            places(n + 1, "gm")
+            op("V", ["plc"], ["hu"], vts, c("hu"), T.plc[:, 15::16], 0.0625, -0.46875, A.mult, A.add)
+            deal("G", XK, [T.X[:, t:1024:4] for t in range(4)])
+            unpack()
             cells(n + 1)
         else:
-            op("V", ["ivl"], ["iu"], vcp, c("iu"), c("ivl"))
+            pairs(T.Krow[:], "Krow")
+            op("V", ["colU", "kval"], ["ivr"], vcp, T.ivr[:].indirect(c("colU")), T.kval[:])
+            hold(T.ivs[:], "ivs", "c1", T.ivr[:], "ivr")
+            op("V", ["ivs", "pfix1"], ["iu"], vts, c("iu"), T.ivs[:, 15::16], pfix1, None, A.add)
+            op("S", ["Krow", "iu"], ["ptk"], act, T.ptk[:], T.Krow[:].indirect(c("iu")), AF.Identity, bias=-0.498)
+            op("V", ["ruS", "ruV"], ["rf"], vcp, c("rf"), c("ru"))
+            quant("vq", "vqs", "vin", 0, 128)
+            op("V", ["ptk"], ["ptf"], vts, T.ptf[:], T.ptk[:], M, -M, A.add, A.add)
+            dma("dpt", [("Y", T.pt[:], T.ptf[0::16, :], ["ptf"], [])])
+            places(n + 1, "gm0")
+            op("V", ["plc", "rf"], ["plf"], vtt, c("plf"), T.plc[:, 15::16], c("rf"), A.add)
+            op("V", ["plf"], ["hu"], vts, c("hu"), c("plf"), 0.0625, -0.46875, A.mult, A.add)
             for t in range(4):
-                deal(t, "XP%d" % t, T.XP[:, 256 * t:256 * t + 256])
+                op("V", ["H%d" % t, "hu", "F%d" % t], ["XP%d" % t], vtt, T.XP[:, 256 * t:256 * t + 256], T.H[:, 128 * t:128 * t + 128].indirect(c("hu")), T.F[:, 256 * t:256 * t + 256], A.add)
                 if t < 3: op("S", ["XP%d" % t, "iu"], ["Xf%d" % t], act, T.Xf[:, t:1024:4], T.XP[:, 256 * t:256 * t + 256].indirect(c("iu")), AF.Copy)
                 else: op("V", ["XP%d" % t, "iu"], ["Xf%d" % t], vcp, T.Xf[:, t:1024:4], T.XP[:, 256 * t:256 * t + 256].indirect(c("iu")))
 
-    op("V", ["Xf0", "Xf1", "Xf2", "Xf3"], ["fq", "fqs"], V.quantize_mx, T.fq[:], T.fqs[:], T.Xf[:])
+    quant("fq", "fqs", "Xf", 0, 256, ["Xf0", "Xf1", "Xf2", "Xf3"])
     mm("ps0", "vq", "vqs", 0, "fq", "fqs", 0, 256)
-    op("V", ["Ko", "colU"], ["prs"], vcp, T.prs[:].indirect(c("colU")), T.Ko[:])
-    dma("dend", [("Y", T.oc[:], T.fq[:].bitcast(dt.uint8), ["fq"], [])] + [("YS"[k % 2], T.osc[4 * k:4 * k + 4, :], T.fqs[32 * k:32 * k + 4, :], ["fqs"], []) for k in range(4)])
+    dma("dend", [("Y", T.oc[:], T.fq[:].bitcast(dt.uint8), ["fq"], [])] + [("Y", T.osc[4 * k:4 * k + 4, :], T.fqs[32 * k:32 * k + 4, :], ["fqs"], []) for k in range(4)])
     op("S", ["ps0"], ["yo"], act, T.yo[:], T.ps0[:, 0:256], AF.Copy)
-    op("V", ["prs"], ["pti"], vts, T.pti[:], T.prs[:], -0.498, None, A.add)
-    op("V", ["pti"], ["ptf"], vcp, T.ptf[:], T.pti[:])
-    dma("dend", [("S", T.y[:], T.yo[:], ["yo"], []), ("Y", T.pt[:], T.ptf[0::16, :], ["ptf"], [])])
+    dma("dend", [("S", T.y[:], T.yo[:], ["yo"], [])])
     for s, v in ends.items(): g.wait_ge(T.sem[s], v)
     g.wait_ge(T.sem.snd, 8 * R)

@@ -2,7 +2,8 @@ from concourse.mybir import dt, AluOpType as A, ActivationFunctionType as AF
 
 N, R, C = 8, 3, 256
 HW = 2832
-NV = 7
+NV = 6
+NA = 12
 ND = 2
 M = 12582912.0
 FAR = 4096.0
@@ -27,14 +28,14 @@ def _scratch():
             LISTS[n] = (buf, at, w)
             at += (w + 15) // 16 * 16
         sb(buf, at, d)
-    lists("lstf", "float32", "kl el Kl acc rl rf sd0 sdx of pm cf cg plf par", {"sd0": 32, "sdx": 64, "of": 32})
-    lists("lsti", "int32", "iB pl ip iq", {"ip": 2, "iq": 4})
+    lists("lstf", "float32", "kl el Kl acc rl rf rg sd0 sdx of pm cf cg plf par", {"sd0": 32, "sdx": 64, "of": 32})
+    lists("lsti", "int32", "iB pl ip iq", {"ip": 2, "iq": 8})
     lists("lstu", "uint16", "kapU ul ru ou lou pu hu cu ku colU iu L", {})
     sb("prow", 256, "int32")
-    sb("er Krow mk2 sl Ks kT los ivs ptk ptf yo", 256)
+    sb("er Krow mk2 sl Ks kT los ivs ptk ptf ptg yo", 256)
     sb("AB", 512)
     sb("ks", 264)
-    sb("mask iX c1 c2 keepb kval lor ivr stw gt gtT gm gm0 gk prw mid kuh", 256, "bfloat16")
+    sb("mask iX c1 c2 keepb kval lor ivr stw gt gtT gm gm1 rst prw mid0 mid1 mid kuh", 256, "bfloat16")
     sb("plc", 256, "float16")
     sb("junk", 256 * (16 - NV), "bfloat16")
     sb("cmp", 256 * NV, "bfloat16")
@@ -132,11 +133,11 @@ def rank_program(g, core, T, topo):
         op("T", [lq, ls] + ([key] if key else [rq, rs]), [bank], PE.matmul_mx, T[bank][:, 0:n], T[lq][:, la:la + 128], T[ls][:, la:la + 128],
            T[rq][:, ra:ra + n], T[rs][:, ra:ra + n], start, stop, acc=not start)
 
-    def hold(out, ok, cn, row, rk):
-        op("V", [cn, rk], [ok], vscan, out, T[cn][:], row, 0.0, A.add, A.min)
+    def hold(out, ok, cn, row, rk, w=256):
+        op("V", [cn, rk], [ok], vscan, out, T[cn][:, 0:w], row, 0.0, A.add, A.min)
 
-    dma("drow", [("YS"[x % 2], T.prow[x::16, :], T.p[:], [], ["prow"]) for x in range(16)])
     dma("dp", [("Y", c("pl"), T.p[:], [], ["pl"])])
+    dma("drow", [("SY"[x % 2], T.prow[x::16, :], T.p[:], [], ["prow"]) for x in range(16)])
     dma("dx", [("Y", T.xin[:], T.x[:], [], ["xin"])])
     dma("du", [("Y", T.uin[:], T.u[:], [], ["uin"])])
 
@@ -158,58 +159,44 @@ def rank_program(g, core, T, topo):
     iota("iX", [[0, 16], [1, 16]], small=True)
     zeros("h", 0, width(0) + 8)
     iota("prw", [[0, 8], [1, 2], [0, 16]], small=True)
-    iota("gk", [[32, 8], [0, 2], [1, 16]], small=True)
+    iota("rst", [[-16, 16], [-4096, 16]], 1024, small=True)
+    iota("mid0", [[1, 64], [-16, 4]], small=True)
+    zeros("Wp", 0, 2048)
     op("G", ["one"], ["Bt"], g.affine_select, T.Bt[:], T.one[:, 0:512], [[-16, 8], [0, 64]], A.is_ge, 0.0, 0, 1)
     op("G", ["Bt"], ["Bt"], g.affine_select, T.Bt[:], T.Bt[:], [[16, 8], [0, 64]], A.is_ge, 0.0, 15, -1)
-    iota("mid", [[1, 64], [-16, 4]], small=True)
+    for k, (sh, bits) in enumerate(((0, 15), (0, 7), (3, 1), (2, 1), (4, 1))):
+        op("V", ["ip"], ["iq%d" % k], vts, c("iq", k, k + 1), c("ip", 0, 1), sh, bits, A.arith_shift_right, A.bitwise_and)
+    op("V", ["iq%d" % k for k in range(5)], ["pa"], vcp, c("par", 0, 5), c("iq", 0, 5))
+    pa, pr, phi, pc, ph, pa16, pfix, pfix1, pown, ptab, px, pw, pp1, pp8, pp16, pmid = [c("par", k, k + 1) for k in range(16)]
     op("V", [], ["kse"], V.memset, T.ks[:, 256:264], HW - 1.0)
-    op("V", [], ["sc"], V.memset, T.sc[:, 0:128], 0.0)
-    op("V", [], ["sd0"], V.memset, c("sd0"), 0.0)
-    op("V", ["ip"], ["iq0"], vts, c("iq", 0, 1), c("ip", 0, 1), 15, None, A.bitwise_and)
-    op("V", ["ip"], ["iq1"], vts, c("iq", 1, 2), c("ip", 0, 1), 4, 6, A.arith_shift_right, A.bitwise_and)
-    op("V", ["ip"], ["iq2"], vts, c("iq", 2, 3), c("ip", 0, 1), 16, None, A.bitwise_and)
-    op("V", ["iq0", "iq1", "iq2"], ["pa"], vcp, c("par", 0, 3), c("iq", 0, 3))
-    pa, pq, ph, pa16, pfix, pfix1, pown, ptab, pk = [c("par", k, k + 1) for k in range(9)]
     op("V", ["iB", "pa"], ["el"], vts, c("el"), c("iB"), 16.0, pa, A.mult, A.add)
     op("V", ["pa"], ["pa16"], vts, pa16, pa, 16.0, None, A.mult)
-    op("V", ["pa"], ["pfix"], vts, pfix, pa, -FAR, 15 * FAR, A.mult, A.add)
-    op("V", ["pa"], ["pfix1"], vts, pfix1, pa, -FAR, 15 * FAR - 1, A.mult, A.add)
-    op("V", ["pa"], ["pown"], vtt, pown, pa, pq, A.subtract)
-    op("V", ["pa"], ["ptab"], vts, ptab, pa, 8.0, None, A.is_lt)
-    op("V", ["pa"], ["pk"], vts, pk, pa, 15.0, None, A.is_equal)
-    op("V", ["iB", "pa16"], ["kapU"], vts, c("kapU"), c("iB"), pa16, None, A.add)
-    op("V", ["iB"], ["ul"], vts, c("ul"), c("iB"), 16.0, None, A.mult)
+    op("V", ["pa"], ["px"], vts, px, pr, 2.0, phi, A.mult, A.add)
     op("V", ["el"], ["kl"], vts, c("kl"), c("el"), 1.0 / 256, None, A.mult)
-    op("V", ["el"], ["sdd"], vts, c("sdx", 0, 32, 2), c("el"), M + HW - 1.0, None, A.add)
-    op("S", ["kval"], ["er"], act, T.er[:], T.kval[:], AF.Identity, scale=1.0 / 256, bias=-1.0 / 256)
+    op("V", ["iB", "pa16"], ["kapU"], vts, c("kapU"), c("iB"), pa16, None, A.add)
+    op("V", ["px"], ["pw"], vts, pw, px, ph, -8.0, A.add, A.add)
+    op("V", [], ["sc"], V.memset, T.sc[:, 0:128], 0.0)
+    op("V", [], ["sd0"], V.memset, c("sd0"), 0.0)
     for t in range(4): quant("ec%d" % t, "es%d" % t, "EE", 4 - t, 128)
+    for o, key, scale, bias in ((pfix, "pfix", -FAR, 15 * FAR), (pfix1, "pfix1", -FAR, 15 * FAR - 1),
+                                (pp1, "pp1", 1.0, 1003.0), (pp8, "pp8", 0.125, 1003 / 8 - 0.4375), (pp16, "pp16", 0.0625, 1003 / 16 - 0.46875),
+                                (pmid, "pmid", -1.0, -0.5)):
+        op("S", ["pa"], [key], act, o, pa, AF.Identity, scale=scale, bias=bias)
+    op("S", ["el"], ["sdd"], act, c("sdx", 0, 32, 2), c("el"), AF.Identity, bias=M + HW - 1.0)
+    op("S", ["kval"], ["er"], act, T.er[:], T.kval[:], AF.Identity, scale=1.0 / 256, bias=-1.0 / 256)
     op("V", ["pl", "kl"], ["Kl"], vtt, c("Kl"), c("pl"), c("kl"), A.add)
+    op("V", ["pw"], ["pown"], vts, pown, pw, pc, 1.0, A.subtract, A.add)
+    op("V", ["pw"], ["ptab"], vts, ptab, pw, 0.0, None, A.not_equal)
+    op("V", ["iB"], ["ul"], vts, c("ul"), c("iB"), 16.0, None, A.mult)
     op("V", ["prow", "kapU", "er"], ["Krow"], vtt, T.Krow[:], T.prow[:].indirect(c("kapU")), T.er[:], A.add)
-
-    def consts1():
-        op("V", ["iX", "pa"], ["mask"], vts, T.mask[:], T.iX[:], pa, None, A.is_equal)
-
-    def consts2():
-        op("S", ["mask"], ["c2"], act, T.c2[:], T.mask[:], AF.Copy, scale=FAR)
-        op("S", ["junk"], ["tab2"], act, T.tab2[:, 0:2304], T.junk[:, 0:2304], AF.Identity, scale=0.0, bias=1.0)
-        op("S", ["mask"], ["c1"], act, T.c1[:], T.mask[:], AF.Identity, scale=18 * FAR, bias=-FAR)
-        op("S", ["iX"], ["keepb"], act, T.keepb[:], T.iX[:], AF.Sign)
-
-    def consts3():
-        op("V", ["prw", "pown", "ptab"], ["gm0"], vts, T.gm0[:], T.prw[:], pown, ptab, A.not_equal, A.mult)
-        op("V", ["gk", "pa", "pk"], ["gk"], vts, T.gk[:], T.gk[:], ph, pk, A.add, A.mult)
-        quant("uq", "us", "uin", 0, 128)
-        op("V", ["gm0", "gk"], ["gm"], vtt, T.gm[:], T.gm0[:], T.gk[:], A.add)
-        op("V", ["uq", "ul"], ["u2"], vcp, T.u2[:].bitcast(dt.uint32), T.uq[:].bitcast(dt.uint32).indirect(c("ul", 0, 8)))
-        op("V", ["mid", "pa"], ["mid"], vts, T.mid[:], T.mid[:], pa, 0.5, A.is_gt, A.subtract)
-        quant("bc", "bs", "Bt", 0, 128)
 
     def ranks(n):
         if n:
-            hold(T.Ks[:], "Ks", "c1", T.Krow[:], "Krow")
-            op("S", ["Ks", "pfix"], ["Kl"], act, c("Kl", NV, 16), T.Ks[:, 16 * NV + 15::16], AF.Identity, bias=pfix)
+            hold(T.Ks[:, 16 * NV:256], "KsS", "c1", T.Krow[:, 16 * NV:256], "Krow", 256 - 16 * NV)
+            hold(T.Ks[:, 0:16 * NV], "Ks", "c1", T.Krow[:, 0:16 * NV], "Krow", 16 * NV)
+            op("S", ["KsS", "pfix"], ["Kl"], act, c("Kl", NV, 16), T.Ks[:, 16 * NV + 15::16], AF.Identity, bias=pfix)
         for b in range(NV, 16):
-            op("S", ["Krow", "Kl"], ["junk", "acc"], act, T.junk[:, 256 * (b - NV):256 * (b - NV) + 256], T.Krow[:], AF.Sign, bias=c("Kl", b, b + 1), scale=-1.0,
+            op("S", ["Krow", "Kl"], ["junk", "acc%d" % (b >= NA)], act, T.junk[:, 256 * (b - NV):256 * (b - NV) + 256], T.Krow[:], AF.Sign, bias=c("Kl", b, b + 1), scale=-1.0,
                accum_out=c("acc", b, b + 1), acc=b > NV)
         for b in range(NV):
             o = T.cmp[:, 256 * b:256 * b + 256]
@@ -217,49 +204,72 @@ def rank_program(g, core, T, topo):
             else: op("V", ["Krow", "Kl"], ["cmp"], vts, o, T.Krow[:], c("Kl", b, b + 1), None, A.is_lt, acc=True)
         w = 128 * NV
         op("V", ["cmp"], ["sc"], vscan, T.sc[:, 128:128 + w], T.cmp[:, 0:2 * w:2], T.cmp[:, 1:2 * w:2], 0.0, A.add, A.add)
+        op("V", ["acc0"], ["ruS"], vts, c("ru", NV, NA), c("acc", NV, NA), 0.5, 127.5, A.mult, A.add)
         op("V", ["sc"], ["rl"], vtt, c("rl", 0, NV), T.sc[:, 255::128], T.sc[:, 127:127 + w:128], A.subtract)
+        if n == 0: op("V", ["iX", "pa"], ["mask"], vts, T.mask[:], T.iX[:], pa, None, A.is_equal)
         op("V", ["rl"], ["ruV"], vcp, c("ru", 0, NV), c("rl", 0, NV))
-        if n == 0: consts1()
-        op("V", ["acc"], ["ruS"], vts, c("ru", NV, 16), c("acc", NV, 16), 0.5, 127.5, A.mult, A.add)
+        op("V", ["ruS", "ruV", "Krow", "kse"], ["ks"], vcp, T.ks[:, 0:256].indirect(c("ru", 0, NA)), T.Krow[:, 0:16 * NA])
+        op("V", ["acc1"], ["ruT"], vts, c("ru", NA, 16), c("acc", NA, 16), 0.5, 127.5, A.mult, A.add)
+        op("V", ["ruT", "Krow"], ["ks"], vcp, T.ks[:, 0:256].indirect(c("ru", NA, 16)), T.Krow[:, 16 * NA:256], acc=True)
+
+    RU = ["ruS", "ruV", "ruT"]
 
     def tables(n):
         w = width(n)
-        op("V", ["ruS", "ruV", "Krow", "kse"], ["ks"], vcp, T.ks[:, 0:256].indirect(c("ru")), T.Krow[:])
         hold(T.AB[:, 0:256], "A", "c2", T.ks[:, 0:256], "ks")
         hold(T.AB[:, 256:512], "B", "c2", T.ks[:, 1:257], "ks")
         op("V", ["A", "B"], ["sdp"], vts, c("sdx", 1, 64, 2), T.AB[:, 15::16], -0.498, M, A.add, A.add)
         op("V", ["sdp"], ["sd0"], vtt, c("sd0", 1, 32, 2), c("sdx", 1, 32, 2), c("sdx", 33, 64, 2), A.is_equal)
+        if n == 0: columns(0)
         op("V", ["sd0", "sdp", "sdd"], ["of"], vscan, c("of"), c("sd0"), c("sdx", 0, 32), 0.0, A.mult, A.max)
+        if n == 0: columns(1)
         op("V", ["of"], ["ou"], vts, c("ou"), c("of", 1, 32, 2), 1.0 - M, None, A.add)
+        if n == 0: columns(2, "lou")
         op("V", ["ou", "kval"], ["h"], vcp, T.h[:].indirect(c("ou")), T.kval[:])
+        if n == 0: regather("X", XO, (0,))
         op("V", ["h"], ["tabs"], vscan, T.tabs[:, 0:w + 8], T.h[:, 0:w + 8], T.h[:, 0:w + 8], 0.0, A.max, A.max)
         items = []
-        for e in range(N):
-            hs = e + e % 2
-            if hs < N: items.append((T.tab2[16 * hs + e::16, 0:w], T.tabs[16 * e:16 * e + N - hs, 1:w + 1]))
-            if hs: items.append((T.tab2[e:16 * hs:16, 0:w], T.tabs[16 * e + 8:16 * e + 8 + hs, 0:w]))
+        for i in range(4):
+            rows = 15 - 4 * i
+            items.append((T.tab2[32 * i + 11 - i::8, 0:w], T.tabs[i:i + 8 * rows:8, 1:w + 1]))
+            items.append((T.tab2[4 + i:4 + i + 8 * rows:8, 0:w], T.tabs[32 * i + 12 + i::8, 0:w]))
         dma("dtab%d" % n, [("YS"[k % 2], o, i, ["tabs"], ["tab2"]) for k, (o, i) in enumerate(items)])
         if 0 < n < R: zeros("h", 0, width(n + 1) + 8)
 
-    def pairs(row, key):
-        op("V", [key], ["kT"], V.transpose, T.kT[:], row)
+    def columns(step, out="colU"):
+        if step == 0: op("V", ["sdp"], ["cf"], vts, c("cf"), c("sdx", 1, 32, 2), -M, None, A.add)
+        if step == 1: op("V", ["A", "cf"], ["cg"], vtt, c("cg"), T.AB[:, 15:256:16], c("cf"), A.subtract)
+        if step == 2: op("V", ["cg"], [out], vts, c(out), c("cg"), 256.0, None, A.mult)
+
+    def inverse(lst, keys, row, out):
+        op("V", keys + ["kval"], [row], vcp, T[row][:].indirect(c(lst)), T.kval[:])
+        hold(T.los[:], "los", "c1", T[row][:], row)
+        op("V", ["los", "pfix1"], [out], vts, c(out), T.los[:, 15::16], pfix1, None, A.add)
+
+    def pairs(src, key):
+        op("V", [key], ["kT"], V.transpose, T.kT[:], src)
         op("V", ["kT"], ["pm"], vts, c("pm"), T.kT[:, 0::16], -0.498, M, A.add, A.add)
+
+    def lookups():
         op("V", ["pm"], ["L"], vts, c("L"), c("pm"), -M, None, A.add)
 
-    def slots(key, outs):
-        op("V", ["ruS", "ruV", "kval"], ["lor"], vcp, T.lor[:].indirect(c("ru")), T.kval[:])
-        hold(T.los[:], "los", "c1", T.lor[:], "lor")
-        op("V", ["los", "pfix1"], ["lou"], vts, c("lou"), T.los[:, 15::16], pfix1, None, A.add)
-        for t in range(4):
-            op("S", ["F%d" % t, "lou"], ["%s%d" % (key, t)], act, outs[t], T.F[:, 256 * t:256 * t + 256].indirect(c("lou")), AF.Copy)
+    XO = [T.X[:, t:1024:4] for t in range(4)]
 
-    def places(n, gm):
-        op("V", ["tab2", "L", gm], ["gt"], vtt, T.gt[:], T.tab2[:, 0:width(n)].indirect(c("L")), T[gm][:], A.mult)
+    def regather(key, outs, which=range(4), q="S"):
+        for t in which:
+            src = T.F[:, 256 * t:256 * t + 256].indirect(c("lou"))
+            if q == "S": op("S", ["F%d" % t, "lou"], ["%s%d" % (key, t)], act, outs[t], src, AF.Copy)
+            else: op("V", ["F%d" % t, "lou"], ["%s%d" % (key, t)], vcp, outs[t], src)
+
+    def places(n):
+        op("V", ["tab2", "L", "gm"], ["gt"], vtt, T.gt[:], T.tab2[:, 0:width(n)].indirect(c("L")), T.gm[:], A.mult)
         op("V", ["gt"], ["gtT"], V.transpose, T.gtT[:], T.gt[:])
-        op("V", ["gtT", "keepb"], ["plc"], vscan, T.plc[:], T.keepb[:], T.gtT[:], 0.0, A.mult, A.add)
+        op("V", ["gtT", "rst"], ["plc"], vscan, T.plc[:], T.rst[:], T.gtT[:], -FAR, A.max, A.subtract)
+
+    def place_list():
+        op("V", ["plc", "pp1"], ["pu"], vts, c("pu"), T.plc[:, 15::16], -1.0, pp1, A.mult, A.add)
 
     def cells(n):
-        op("V", ["plc"], ["pu"], vcp, c("pu"), T.plc[:, 15::16])
         op("V", ["pu", "kval"], ["Wp"], vcp, T.Wp[:].indirect(c("pu")), T.kval[:])
         op("V", ["Wp"], ["Ws"], vscan, T.Ws[:], T.Wp[:, 0::2], T.Wp[:, 1::2], 1.0, A.max, A.max)
         hold(T.kuh[:], "kuh", "c2", T.Ws[:, 3::4], "Ws")
@@ -282,25 +292,33 @@ def rank_program(g, core, T, topo):
         for t in range(4):
             op("S", ["ps%d" % (4 + t)], ["F%d" % t], act, T.F[:, 256 * t:256 * t + 256], T["ps%d" % (4 + t)][:, 0:256], AF.Copy, scale=2.0)
 
-    def deal(src, keys, outs):
+    def deal():
         for t in range(4 - ND, 4):
             op("S", ["H%d" % t, "hu"], ["Hg%d" % t], act, T.Hg[:, 256 * t:256 * t + 256], T.H[:, 128 * t:128 * t + 128].indirect(c("hu")), AF.Copy)
         for t in range(4):
-            f = T[src][:, 256 * t:256 * t + 256]
-            if t < 4 - ND: op("V", ["H%d" % t, "hu", "%s%d" % (src, t)], [keys[t]], vtt, outs[t], T.H[:, 128 * t:128 * t + 128].indirect(c("hu")), f, A.add)
-            else: op("V", ["Hg%d" % t, "%s%d" % (src, t)], [keys[t]], vtt, outs[t], T.Hg[:, 256 * t:256 * t + 256], f, A.add)
+            o, f = T.X[:, t:1024:4], T.G[:, 256 * t:256 * t + 256]
+            if t < 4 - ND: op("V", ["H%d" % t, "hu", "G%d" % t], [XK[t]], vtt, o, T.H[:, 128 * t:128 * t + 128].indirect(c("hu")), f, A.add)
+            else: op("V", ["Hg%d" % t, "G%d" % t], [XK[t]], vtt, o, T.Hg[:, 256 * t:256 * t + 256], f, A.add)
 
     ranks(0)
-    consts2()
+    op("S", ["mask"], ["c2"], act, T.c2[:], T.mask[:], AF.Copy, scale=FAR)
     for t in range(4): op("S", ["xin"], ["F%d" % t], act, T.F[:, 256 * t:256 * t + 256], T.xin[:, t::4], AF.Copy)
+    op("S", ["junk"], ["tab2"], act, T.tab2[:, 0:2048], T.junk[:, 0:2048], AF.Identity, scale=0.0, bias=3.0)
     tables(0)
-    zeros("Wp", 0, 2048)
-    slots("X", [T.X[:, t:1024:4] for t in range(4)])
+    regather("X", XO, (1, 2))
+    regather("X", XO, (3,), "V")
     pairs(T.ks[:, 0:256], "ks")
-    consts3()
-    op("S", ["us", "ul"], ["u2s"], act, T.u2s[:], T.us[:].indirect(c("ul", 0, 8)), AF.Copy)
+    quant("uq", "us", "uin", 0, 128)
+    lookups()
+    op("V", ["prw", "pown", "ptab"], ["gm"], vts, T.gm[:], T.prw[:], pown, ptab, A.not_equal, A.mult)
+    op("V", ["uq", "ul"], ["u2"], vcp, T.u2[:].bitcast(dt.uint32), T.uq[:].bitcast(dt.uint32).indirect(c("ul", 0, 8)))
     unpack()
-    places(0, "gm")
+    places(0)
+    place_list()
+    op("S", ["us", "ul"], ["u2s"], act, T.u2s[:], T.us[:].indirect(c("ul", 0, 8)), AF.Copy)
+    op("S", ["mask"], ["c1"], act, T.c1[:], T.mask[:], AF.Identity, scale=18 * FAR, bias=-FAR)
+    op("S", ["mid0", "pmid"], ["mid1"], act, T.mid1[:], T.mid0[:], AF.Sign, bias=pmid)
+    op("S", ["mid1"], ["mid"], act, T.mid[:], T.mid1[:], AF.Copy, scale=0.5)
     cells(0)
     dma("dw", [("Y", T.wq[:].bitcast(dt.uint8), T.wc[:], ["gt"], ["wq"]), ("Y", T.wp[:], T.ws[:], [], ["wp"])])
     dma("dv", [("Y", T.vin[:], T.v[:], [], ["vin"])])
@@ -315,7 +333,6 @@ def rank_program(g, core, T, topo):
             op("V", ["P%d" % t, "ku"], ["Z%d" % t], vcp, T.Z[:, t:1024:4], T.P[:, 256 * t:256 * t + 256].indirect(c("ku")))
         for t in (2, 3):
             op("S", ["P%d" % t, "ku"], ["Z%d" % t], act, T.Z[:, t:1024:4], T.P[:, 256 * t:256 * t + 256].indirect(c("ku")), AF.Copy)
-        op("V", ["plc"], ["cu"], vts, c("cu"), T.plc[:, 15::16], 0.125, -0.4375, A.mult, A.add)
         quant(zq, zs, "Z", 0, 256, ["Z0", "Z1", "Z2", "Z3"])
         need("G", [last[zq]])
         g.remote_dma(T["lc%d" % n][:].bitcast(dt.uint8), T[zq][:].bitcast(dt.uint8), T.sem["arr%d" % n], T.sem.snd, pid, rid, m4)
@@ -324,19 +341,29 @@ def rank_program(g, core, T, topo):
         if n < R - 1: zeros("Wp", 0, 2048)
         mm("ps0", "u2", "u2s", 0, zq, zs, 0, 256)
         mm("ps1", "u2", "u2s", 0, zq, zs, 0, 256)
-        op("V", ["ps0", "mask"], ["mk2"], vtt, T.mk2[:], T.ps0[:, 0:256], T.mask[:], A.mult)
-        op("V", ["mk2", "keepb"], ["sl"], vscan, T.sl[:], T.keepb[:], T.mk2[:], 0.0, A.mult, A.add)
+        op("V", ["plc", "pp8"], ["cu"], vts, c("cu"), T.plc[:, 15::16], -0.125, pp8, A.mult, A.add)
+        if n == 0:
+            op("V", ["iX"], ["keepb"], vts, T.keepb[:], T.iX[:], 1.0, None, A.min)
+            quant("bc", "bs", "Bt", 0, 128)
+        if n == 1: quant("vq", "vqs", "vin", 0, 128)
+        if n == R - 1:
+            columns(0)
+            columns(1)
+        for k in (0, 1):
+            a, b = 128 * k, 128 * k + 128
+            op("V", ["ps0", "mask"], ["mk%d" % k], vtt, T.mk2[:, a:b], T.ps0[:, a:b], T.mask[:, a:b], A.mult)
+            op("V", ["mk%d" % k, "keepb"], ["sl%d" % k], vscan, T.sl[:, a:b], T.keepb[:, a:b], T.mk2[:, a:b], 0.0, A.mult, A.add)
 
         def signs(k, lo, hi):
             for t in range(4):
                 b = 4 * k + t
-                op("S", ["ps1", "sl"], ["sg%d" % k], act, T.sg[:, 1024 * k + 4 * lo + t:1024 * k + 4 * hi:4], T.ps1[:, lo:hi], AF.Sign,
+                op("S", ["ps1", "sl%d" % (k // 2)], ["sg%d" % k], act, T.sg[:, 1024 * k + 4 * lo + t:1024 * k + 4 * hi:4], T.ps1[:, lo:hi], AF.Sign,
                    bias=T.sl[:, 16 * b + 15:16 * b + 16], scale=-1.0, acc=t > 0)
 
         def direct(k, lo, hi, how):
             for t in range(4):
                 b = 4 * k + t
-                op("V", ["ps0", "sl"], ["Cd%d" % k], vts, T.Ct[:, 1024 * k + 4 * lo + t:1024 * k + 4 * hi:4], T.ps0[:, lo:hi], T.sl[:, 16 * b + 15:16 * b + 16], None, how, acc=t > 0)
+                op("V", ["ps0", "sl%d" % (k // 2)], ["Cd%d" % k], vts, T.Ct[:, 1024 * k + 4 * lo + t:1024 * k + 4 * hi:4], T.ps0[:, lo:hi], T.sl[:, 16 * b + 15:16 * b + 16], None, how, acc=t > 0)
 
         def middle(k):
             a = 1280 * k
@@ -349,32 +376,36 @@ def rank_program(g, core, T, topo):
             elif right: op("S", ["sg%d" % k], [key], act, T.Ct[:, a:b], T.sg[:, a:b], AF.Sign, bias=1.0, scale=-1.0)
             else: op("S", ["sg%d" % k], [key], act, T.Ct[:, a:b], T.sg[:, a:b], AF.Relu, scale=-1.0)
 
-        def total(k, keys, start, stop):
-            op("V", keys, ["cq%d" % k], V.quantize_mx, T.cq[:, 256 * k:256 * k + 256], T.cs[:, 256 * k:256 * k + 256], T.Ct[:, 1024 * k:1024 * k + 1024])
-            mm("ps2", "bc", "bs", 0, "cq", "cs", 256 * k, 256, start, stop, "cq%d" % k)
+        def total(k, keys, start, stop, halves=(0, 1)):
+            a, b, key = 256 * k + 128 * halves[0], 256 * k + 128 * halves[-1] + 128, "cq%d%d" % (k, halves[0])
+            op("V", keys, [key], V.quantize_mx, T.cq[:, a:b], T.cs[:, a:b], T.Ct[:, 4 * a:4 * b])
+            for j in halves: mm("ps%d" % (2 + j), "bc", "bs", 0, "cq", "cs", 256 * k + 128 * j, 128, start, stop, key)
         signs(0, 0, 64)
         signs(1, 0, 256)
         signs(3, 192, 256)
+        side("S", 1, 1)
+        side("S", 1, 0)
         signs(2, 0, 256)
         side("S", 2, 0)
         direct(0, 64, 256, A.is_ge)
         middle(0)
-        total(0, ["Cd0", "Cm0"], True, False)
         direct(3, 0, 192, A.is_gt)
-        side("V", 1, 0)
-        side("V", 1, 1)
-        middle(1)
-        total(1, ["Cl1", "Cr1", "Cm1"], False, False)
+        total(0, ["Cd0", "Cm0"], True, False)
         middle(3)
+        middle(1)
         total(3, ["Cd3", "Cm3"], False, False)
+        total(1, ["Cl1", "Cr1", "Cm1"], False, False)
         middle(2)
         side("V", 2, 1)
-        total(2, ["Cl2", "Cr2", "Cm2"], False, True)
-        op("V", ["ps2"], ["stw"], vts, T.stw[:], T.ps2[:, 0:256], 2.0, None, A.mult)
-        op("V", ["stw", "cu", "ks"], ["Krow"], vtt, T.Krow[:], T.stw[:].indirect(c("cu")), T.ks[:, 0:256], A.add)
+        total(2, ["Cr2", "Cm2"], False, True, (1,))
+        total(2, ["Cl2"], False, True, (0,))
+        if n == R - 1: columns(2)
+        op("S", ["ps3"], ["stw1"], act, T.stw[:, 128:256], T.ps3[:, 0:128], AF.Copy, scale=2.0)
+        op("V", ["ps2"], ["stw0"], vts, T.stw[:, 0:128], T.ps2[:, 0:128], 2.0, None, A.mult)
+        op("V", ["stw0", "stw1", "cu", "ks"], ["Krow"], vtt, T.Krow[:], T.stw[:].indirect(c("cu")), T.ks[:, 0:256], A.add)
         ranks(n + 1)
         unpack_keep()
-        if n == 0: op("S", ["junk"], ["tab2"], act, T.tab2[:, 2304:HW], T.junk[:, 0:HW - 2304], AF.Identity, scale=0.0, bias=1.0)
+        if n == 0: op("S", ["junk"], ["tab2"], act, T.tab2[:, 2048:HW], T.junk[:, 0:HW - 2048], AF.Identity, scale=0.0, bias=3.0)
         need("T", [("arr%d" % n, 8, "R", {})])
         ends["arr%d" % n] = 8
         for t in range(4):
@@ -382,39 +413,42 @@ def rank_program(g, core, T, topo):
             op("S", ["ps%d" % (4 + t)], ["H%d" % t], act, T.H[:, 128 * t:128 * t + 128], T["ps%d" % (4 + t)][:, 1:256:2], AF.Copy, scale=0.03125)
         tables(n + 1)
         if n < R - 1:
-            slots("G", [T.G[:, 256 * t:256 * t + 256] for t in range(4)])
+            inverse("ru", RU, "lor", "lou")
+            regather("G", [T.G[:, 256 * t:256 * t + 256] for t in range(4)])
             pairs(T.ks[:, 0:256], "ks")
-            if n == R - 2:
-                op("V", ["sdp"], ["cf"], vts, c("cf"), c("sdx", 1, 32, 2), -M, None, A.add)
-                op("V", ["A", "cf"], ["cg"], vtt, c("cg"), T.AB[:, 15:256:16], c("cf"), A.subtract)
-                op("V", ["cg"], ["colU"], vts, c("colU"), c("cg"), 256.0, None, A.mult)
-            places(n + 1, "gm")
-            op("V", ["plc"], ["hu"], vts, c("hu"), T.plc[:, 15::16], 0.0625, -0.46875, A.mult, A.add)
-            deal("G", XK, [T.X[:, t:1024:4] for t in range(4)])
+            lookups()
+            places(n + 1)
+            op("V", ["plc", "pp16"], ["hu"], vts, c("hu"), T.plc[:, 15::16], -0.0625, pp16, A.mult, A.add)
+            place_list()
+            deal()
             unpack()
             cells(n + 1)
-        else:
-            pairs(T.Krow[:], "Krow")
-            op("V", ["colU", "kval"], ["ivr"], vcp, T.ivr[:].indirect(c("colU")), T.kval[:])
-            hold(T.ivs[:], "ivs", "c1", T.ivr[:], "ivr")
-            op("V", ["ivs", "pfix1"], ["iu"], vts, c("iu"), T.ivs[:, 15::16], pfix1, None, A.add)
-            op("S", ["Krow", "iu"], ["ptk"], act, T.ptk[:], T.Krow[:].indirect(c("iu")), AF.Identity, bias=-0.498)
-            op("V", ["ruS", "ruV"], ["rf"], vcp, c("rf"), c("ru"))
-            quant("vq", "vqs", "vin", 0, 128)
-            op("V", ["ptk"], ["ptf"], vts, T.ptf[:], T.ptk[:], M, -M, A.add, A.add)
-            dma("dpt", [("Y", T.pt[:], T.ptf[0::16, :], ["ptf"], [])])
-            places(n + 1, "gm0")
-            op("V", ["plc", "rf"], ["plf"], vtt, c("plf"), T.plc[:, 15::16], c("rf"), A.add)
-            op("V", ["plf"], ["hu"], vts, c("hu"), c("plf"), 0.0625, -0.46875, A.mult, A.add)
-            for t in range(4):
-                op("V", ["H%d" % t, "hu", "F%d" % t], ["XP%d" % t], vtt, T.XP[:, 256 * t:256 * t + 256], T.H[:, 128 * t:128 * t + 128].indirect(c("hu")), T.F[:, 256 * t:256 * t + 256], A.add)
-                if t < 3: op("S", ["XP%d" % t, "iu"], ["Xf%d" % t], act, T.Xf[:, t:1024:4], T.XP[:, 256 * t:256 * t + 256].indirect(c("iu")), AF.Copy)
-                else: op("V", ["XP%d" % t, "iu"], ["Xf%d" % t], vcp, T.Xf[:, t:1024:4], T.XP[:, 256 * t:256 * t + 256].indirect(c("iu")))
+
+    inverse("colU", ["colU"], "ivr", "iu")
+    pairs(T.Krow[:], "Krow")
+    op("V", RU + ["pp1"], ["rg"], vts, c("rg"), c("ru"), pp1, None, A.add)
+    lookups()
+    op("V", ["rg", "el"], ["rf"], vtt, c("rf"), c("rg"), c("el"), A.subtract)
+    op("S", ["Krow", "iu"], ["ptk"], act, T.ptk[:], T.Krow[:].indirect(c("iu")), AF.Identity, bias=-0.498)
+    op("S", ["ptk"], ["ptf"], act, T.ptf[:], T.ptk[:], AF.Identity, bias=M)
+    op("S", ["ptf"], ["ptg"], act, T.ptg[:], T.ptf[:], AF.Identity, bias=-M)
+    dma("dpt", [("Y", T.pt[:], T.ptg[0::16, :], ["ptg"], [])])
+    places(R)
+    op("V", ["plc", "rf"], ["plf"], vtt, c("plf"), c("rf"), T.plc[:, 15::16], A.subtract)
+    op("V", ["plf"], ["hu"], vts, c("hu"), c("plf"), 0.0625, -0.46875, A.mult, A.add)
+    op("S", ["H3", "hu"], ["Hg3"], act, T.Hg[:, 768:1024], T.H[:, 384:512].indirect(c("hu")), AF.Copy)
+    for t in range(4):
+        h, hk = (T.H[:, 128 * t:128 * t + 128].indirect(c("hu")), "H%d" % t) if t < 3 else (T.Hg[:, 768:1024], "Hg3")
+        op("V", [hk, "hu", "F%d" % t], ["XP%d" % t], vtt, T.XP[:, 256 * t:256 * t + 256], h, T.F[:, 256 * t:256 * t + 256], A.add)
+        if t < 3: op("S", ["XP%d" % t, "iu"], ["Xf%d" % t], act, T.Xf[:, t:1024:4], T.XP[:, 256 * t:256 * t + 256].indirect(c("iu")), AF.Copy)
+        else: op("V", ["XP%d" % t, "iu"], ["Xf%d" % t], vcp, T.Xf[:, t:1024:4], T.XP[:, 256 * t:256 * t + 256].indirect(c("iu")))
 
     quant("fq", "fqs", "Xf", 0, 256, ["Xf0", "Xf1", "Xf2", "Xf3"])
-    mm("ps0", "vq", "vqs", 0, "fq", "fqs", 0, 256)
-    dma("dend", [("Y", T.oc[:], T.fq[:].bitcast(dt.uint8), ["fq"], [])] + [("Y", T.osc[4 * k:4 * k + 4, :], T.fqs[32 * k:32 * k + 4, :], ["fqs"], []) for k in range(4)])
-    op("S", ["ps0"], ["yo"], act, T.yo[:], T.ps0[:, 0:256], AF.Copy)
-    dma("dend", [("S", T.y[:], T.yo[:], ["yo"], [])])
+    for k in (0, 1): mm("ps%d" % k, "vq", "vqs", 0, "fq", "fqs", 128 * k, 128)
+    scales = [(T.osc[4 * j:4 * j + 4, :], T.fqs[32 * j:32 * j + 4, :], ["fqs"], []) for j in range(4)]
+    dma("dend", [("Y", T.oc[:], T.fq[:].bitcast(dt.uint8), ["fq"], []), ("S",) + scales[0]] + [("Y",) + x for x in scales[1:]])
+    op("S", ["ps0"], ["yo0"], act, T.yo[:, 0:128], T.ps0[:, 0:128], AF.Copy)
+    op("V", ["ps1"], ["yo1"], vcp, T.yo[:, 128:256], T.ps1[:, 0:128])
+    dma("dend", [("S", T.y[:], T.yo[:], ["yo0", "yo1"], [])])
     for s, v in ends.items(): g.wait_ge(T.sem[s], v)
     g.wait_ge(T.sem.snd, 8 * R)

@@ -3,8 +3,8 @@ from concourse.mybir import dt, AluOpType as A, ActivationFunctionType as AF
 N, R, C = 8, 3, 256
 HW = 2832
 NV = 6
-NA = 12
 ND = 2
+NA = 12
 M = 12582912.0
 FAR = 4096.0
 F8 = "float8_e4m3fn_x4"
@@ -28,29 +28,29 @@ def _scratch():
             LISTS[n] = (buf, at, w)
             at += (w + 15) // 16 * 16
         sb(buf, at, d)
-    lists("lstf", "float32", "kl el Kl acc rl rf rg sd0 sdx of pm cf cg plf par", {"sd0": 32, "sdx": 64, "of": 32})
-    lists("lsti", "int32", "iB pl ip iq", {"ip": 2, "iq": 8})
-    lists("lstu", "uint16", "kapU ul ru ou lou pu hu cu ku colU iu L", {})
+    lists("lstf", "float32", "kl el Kl K16 acc rl rf rg sd0 sdx of pm cf cg plf par", {"sd0": 32, "sdx": 64, "of": 32})
+    lists("lsti", "int32", "iB iU pl ip iq", {"ip": 2, "iq": 8})
+    lists("lstu", "uint16", "kapU ul ru0 ru1 ou pu hu cu ku colU L", {"ul": 24})
     sb("prow", 256, "int32")
-    sb("er Krow mk2 sl Ks kT los ivs ptk ptf ptg yo", 256)
+    sb("er Ksl Krow sl Ks kT ptf ptg yo", 256)
     sb("AB", 512)
     sb("ks", 264)
-    sb("mask iX c1 c2 keepb kval lor ivr stw gt gtT gm gm1 rst prw mid0 mid1 mid kuh", 256, "bfloat16")
+    sb("away iX c1 c2 kval stw gt gtT gm rst prw mid0 mid1 mid kuh", 256, "bfloat16")
     sb("plc", 256, "float16")
     sb("junk", 256 * (16 - NV), "bfloat16")
     sb("cmp", 256 * NV, "bfloat16")
-    sb("sc", 128 * NV + 128, "float16")
+    sb("sc", 128 * NV, "float16")
     sb("h", HW + 256, "bfloat16")
     sb("tabs tab2", HW, "bfloat16")
     sb("Wp", 2048, "bfloat16")
     sb("uin vin Bt H", 512, "bfloat16")
     sb("Ct sg", 4096, "bfloat16")
-    sb("Ws Z P F G Hg XP Xf xin", 1024, "bfloat16")
+    sb("Ws Z P F Fc G Hg Xf xin", 1024, "bfloat16")
     sb("X", 1032, "bfloat16")
     sb("EE one", 520, "bfloat16")
     for t in range(4): mx("ec%d" % t, "es%d" % t, 128)
     for n, m, w in (("bc", "bs", 128), ("xq", "xs", 256), ("xr", "xt", 256), ("cq", "cs", 1024),
-                    ("uq", "us", 128), ("u2", "u2s", 128), ("vq", "vqs", 128), ("wq", "wp", 512), ("fq", "fqs", 256)): mx(n, m, w)
+                    ("uq", "us", 128), ("u2", "u2s", 384), ("vq", "vqs", 128), ("wq", "wp", 512), ("fq", "fqs", 256)): mx(n, m, w)
     for k in range(R):
         mx("zq%d" % k, "zs%d" % k, 256)
         mx("lc%d" % k, "lp%d" % k, 256)
@@ -59,7 +59,8 @@ def _scratch():
 
 
 SCRATCH = _scratch()
-DSEM = ["dp", "drow", "dx", "du", "dw", "dv", "dend", "dpt"] + ["dtab%d" % k for k in range(R + 1)]
+DSEM = ["dp", "drow", "dx", "du", "dw", "dv", "dend", "dpt"] + ["dt%s%d" % (x, k) for x in "ab" for k in range(R + 1)]
+TAB2 = ["tab2", "tab3"]
 SEMAPHORES = ["qV", "qS", "qT", "qG", "snd"] + ["arr%d" % k for k in range(R)] + DSEM
 
 
@@ -160,14 +161,16 @@ def rank_program(g, core, T, topo):
     zeros("h", 0, width(0) + 8)
     iota("prw", [[0, 8], [1, 2], [0, 16]], small=True)
     iota("rst", [[-16, 16], [-4096, 16]], 1024, small=True)
-    iota("mid0", [[1, 64], [-16, 4]], small=True)
+    iota("iU", [[16, 2], [32, 4], [0, 2]])
     zeros("Wp", 0, 2048)
-    op("G", ["one"], ["Bt"], g.affine_select, T.Bt[:], T.one[:, 0:512], [[-16, 8], [0, 64]], A.is_ge, 0.0, 0, 1)
-    op("G", ["Bt"], ["Bt"], g.affine_select, T.Bt[:], T.Bt[:], [[16, 8], [0, 64]], A.is_ge, 0.0, 15, -1)
+    iota("mid0", [[1, 64], [-32, 2], [0, 2]], small=True)
+    zeros("Bt", 0, 512)
+    for j in range(N):
+        op("G", ["Bt"], ["Bt"], g.iota, T.Bt[j // 2 * 32:j // 2 * 32 + 32, 64 * j + j % 2:64 * j + 64:2], [[0, 32]], 1, 0, allow_small_or_imprecise_dtypes=True, acc=True)
     for k, (sh, bits) in enumerate(((0, 15), (0, 7), (3, 1), (2, 1), (4, 1))):
         op("V", ["ip"], ["iq%d" % k], vts, c("iq", k, k + 1), c("ip", 0, 1), sh, bits, A.arith_shift_right, A.bitwise_and)
     op("V", ["iq%d" % k for k in range(5)], ["pa"], vcp, c("par", 0, 5), c("iq", 0, 5))
-    pa, pr, phi, pc, ph, pa16, pfix, pfix1, pown, ptab, px, pw, pp1, pp8, pp16, pmid = [c("par", k, k + 1) for k in range(16)]
+    pa, pr, phi, pc, ph, pa16, pfix, p16, pown, ptab, px, pw, pp1, pp8, pp16, pmid = [c("par", k, k + 1) for k in range(16)]
     op("V", [], ["kse"], V.memset, T.ks[:, 256:264], HW - 1.0)
     op("V", ["iB", "pa"], ["el"], vts, c("el"), c("iB"), 16.0, pa, A.mult, A.add)
     op("V", ["pa"], ["pa16"], vts, pa16, pa, 16.0, None, A.mult)
@@ -175,44 +178,49 @@ def rank_program(g, core, T, topo):
     op("V", ["el"], ["kl"], vts, c("kl"), c("el"), 1.0 / 256, None, A.mult)
     op("V", ["iB", "pa16"], ["kapU"], vts, c("kapU"), c("iB"), pa16, None, A.add)
     op("V", ["px"], ["pw"], vts, pw, px, ph, -8.0, A.add, A.add)
-    op("V", [], ["sc"], V.memset, T.sc[:, 0:128], 0.0)
     op("V", [], ["sd0"], V.memset, c("sd0"), 0.0)
     for t in range(4): quant("ec%d" % t, "es%d" % t, "EE", 4 - t, 128)
-    for o, key, scale, bias in ((pfix, "pfix", -FAR, 15 * FAR), (pfix1, "pfix1", -FAR, 15 * FAR - 1),
-                                (pp1, "pp1", 1.0, 1003.0), (pp8, "pp8", 0.125, 1003 / 8 - 0.4375), (pp16, "pp16", 0.0625, 1003 / 16 - 0.46875),
-                                (pmid, "pmid", -1.0, -0.5)):
+    for o, key, scale, bias in ((pfix, "pfix", -FAR, 15 * FAR),
+                                (p16, "p16", -1.0, -0.5),
+                                (pp1, "pp1", 1.0, 1003.0), (pp8, "pp8", 0.125, 1003 / 8 - 0.4375), (pp16, "pp16", 0.0625, 1003 / 16 - 0.46875)):
         op("S", ["pa"], [key], act, o, pa, AF.Identity, scale=scale, bias=bias)
+    op("S", ["p16"], ["pmid"], act, pmid, ph, AF.Identity, scale=-16.0, bias=p16)
     op("S", ["el"], ["sdd"], act, c("sdx", 0, 32, 2), c("el"), AF.Identity, bias=M + HW - 1.0)
     op("S", ["kval"], ["er"], act, T.er[:], T.kval[:], AF.Identity, scale=1.0 / 256, bias=-1.0 / 256)
     op("V", ["pl", "kl"], ["Kl"], vtt, c("Kl"), c("pl"), c("kl"), A.add)
     op("V", ["pw"], ["pown"], vts, pown, pw, pc, 1.0, A.subtract, A.add)
     op("V", ["pw"], ["ptab"], vts, ptab, pw, 0.0, None, A.not_equal)
-    op("V", ["iB"], ["ul"], vts, c("ul"), c("iB"), 16.0, None, A.mult)
-    op("V", ["prow", "kapU", "er"], ["Krow"], vtt, T.Krow[:], T.prow[:].indirect(c("kapU")), T.er[:], A.add)
+    op("V", ["iB"], ["ul"], vts, c("ul", 0, 8), c("iB", 0, 8), 16.0, None, A.mult)
+    KR = ["Kr0", "Kr1"]
+    op("V", ["prow", "kapU", "er"], KR, vtt, T.Krow[:], T.prow[:].indirect(c("kapU")), T.er[:], A.add)
+
+    def count(b):
+        op("V", ["cmp%d" % b], ["sc%d" % b], vscan, T.sc[:, 128 * b:128 * b + 128], T.cmp[:, 256 * b:256 * b + 128], T.cmp[:, 256 * b + 128:256 * b + 256], 0.0, A.add, A.add)
 
     def ranks(n):
+        ru = "ru%d" % (n % 2)
         if n:
-            hold(T.Ks[:, 16 * NV:256], "KsS", "c1", T.Krow[:, 16 * NV:256], "Krow", 256 - 16 * NV)
-            hold(T.Ks[:, 0:16 * NV], "Ks", "c1", T.Krow[:, 0:16 * NV], "Krow", 16 * NV)
-            op("S", ["KsS", "pfix"], ["Kl"], act, c("Kl", NV, 16), T.Ks[:, 16 * NV + 15::16], AF.Identity, bias=pfix)
-        for b in range(NV, 16):
-            op("S", ["Krow", "Kl"], ["junk", "acc%d" % (b >= NA)], act, T.junk[:, 256 * (b - NV):256 * (b - NV) + 256], T.Krow[:], AF.Sign, bias=c("Kl", b, b + 1), scale=-1.0,
-               accum_out=c("acc", b, b + 1), acc=b > NV)
+            hold(T.Ks[:, 128:256], "Ks1", "c1", T.Krow[:, 128:256], "Kr1", 128)
+            hold(T.Ks[:, 0:128], "Ks0", "c1", T.Krow[:, 0:128], "Kr0", 128)
+            op("S", ["Ks1", "pfix"], ["Kl"], act, c("Kl", 8, 16), T.Ks[:, 143::16], AF.Identity, bias=pfix)
+        for j, b in enumerate(list(range(8, NA)) + list(range(NV, 8)) + list(range(NA, 16))):
+            if n and j == 1 and NV < 8: op("S", ["Ks0", "pfix"], ["Km"], act, c("Kl", NV, 8), T.Ks[:, 16 * NV + 15:128:16], AF.Identity, bias=pfix)
+            op("S", KR + ["Kl" if b >= 8 or n == 0 else "Km"], ["junk", "acc%d" % (b >= NA)], act, T.junk[:, 256 * j:256 * j + 256], T.Krow[:], AF.Sign, bias=c("Kl", b, b + 1),
+               scale=-1.0, accum_out=c("acc", b, b + 1), acc=j > 0)
         for b in range(NV):
             o = T.cmp[:, 256 * b:256 * b + 256]
-            if n: op("V", ["Krow", "Ks", "pfix"], ["cmp"], vts, o, T.Krow[:], pfix, T.Ks[:, 16 * b + 15:16 * b + 16], A.subtract, A.is_lt, acc=True)
-            else: op("V", ["Krow", "Kl"], ["cmp"], vts, o, T.Krow[:], c("Kl", b, b + 1), None, A.is_lt, acc=True)
-        w = 128 * NV
-        op("V", ["cmp"], ["sc"], vscan, T.sc[:, 128:128 + w], T.cmp[:, 0:2 * w:2], T.cmp[:, 1:2 * w:2], 0.0, A.add, A.add)
-        op("V", ["acc0"], ["ruS"], vts, c("ru", NV, NA), c("acc", NV, NA), 0.5, 127.5, A.mult, A.add)
-        op("V", ["sc"], ["rl"], vtt, c("rl", 0, NV), T.sc[:, 255::128], T.sc[:, 127:127 + w:128], A.subtract)
-        if n == 0: op("V", ["iX", "pa"], ["mask"], vts, T.mask[:], T.iX[:], pa, None, A.is_equal)
-        op("V", ["rl"], ["ruV"], vcp, c("ru", 0, NV), c("rl", 0, NV))
-        op("V", ["ruS", "ruV", "Krow", "kse"], ["ks"], vcp, T.ks[:, 0:256].indirect(c("ru", 0, NA)), T.Krow[:, 0:16 * NA])
-        op("V", ["acc1"], ["ruT"], vts, c("ru", NA, 16), c("acc", NA, 16), 0.5, 127.5, A.mult, A.add)
-        op("V", ["ruT", "Krow"], ["ks"], vcp, T.ks[:, 0:256].indirect(c("ru", NA, 16)), T.Krow[:, 16 * NA:256], acc=True)
+            if n: op("V", KR + ["Ks0", "pfix"], ["cmp%d" % b], vts, o, T.Krow[:], pfix, T.Ks[:, 16 * b + 15:16 * b + 16], A.subtract, A.is_lt)
+            else: op("V", KR + ["Kl"], ["cmp%d" % b], vts, o, T.Krow[:], c("Kl", b, b + 1), None, A.is_lt)
+            if b: count(b - 1)
+        op("V", ["acc0"], [ru + "S"], vts, c(ru, NV, NA), c("acc", NV, NA), 0.5, 127.5, A.mult, A.add)
+        count(NV - 1)
+        op("V", ["sc%d" % b for b in range(NV)], [ru + "V"], vcp, c(ru, 0, NV), T.sc[:, 127::128])
+        op("V", [ru + "S", ru + "V", "kse"] + KR, ["ks"], vcp, T.ks[:, 0:256].indirect(c(ru, 0, NA)), T.Krow[:, 0:16 * NA])
+        op("V", ["acc1"], [ru + "T"], vts, c(ru, NA, 16), c("acc", NA, 16), 0.5, 127.5, A.mult, A.add)
+        op("V", [ru + "T"] + KR, ["ks"], vcp, T.ks[:, 0:256].indirect(c(ru, NA, 16)), T.Krow[:, 16 * NA:256], acc=True)
 
-    RU = ["ruS", "ruV", "ruT"]
+    def rank_keys(n):
+        return ["ru%d%s" % (n % 2, x) for x in "SVT"]
 
     def tables(n):
         w = width(n)
@@ -224,45 +232,44 @@ def rank_program(g, core, T, topo):
         op("V", ["sd0", "sdp", "sdd"], ["of"], vscan, c("of"), c("sd0"), c("sdx", 0, 32), 0.0, A.mult, A.max)
         if n == 0: columns(1)
         op("V", ["of"], ["ou"], vts, c("ou"), c("of", 1, 32, 2), 1.0 - M, None, A.add)
-        if n == 0: columns(2, "lou")
+        if n == 0: columns(2)
         op("V", ["ou", "kval"], ["h"], vcp, T.h[:].indirect(c("ou")), T.kval[:])
-        if n == 0: regather("X", XO, (0,))
-        op("V", ["h"], ["tabs"], vscan, T.tabs[:, 0:w + 8], T.h[:, 0:w + 8], T.h[:, 0:w + 8], 0.0, A.max, A.max)
-        items = []
-        for i in range(4):
-            rows = 15 - 4 * i
-            items.append((T.tab2[32 * i + 11 - i::8, 0:w], T.tabs[i:i + 8 * rows:8, 1:w + 1]))
-            items.append((T.tab2[4 + i:4 + i + 8 * rows:8, 0:w], T.tabs[32 * i + 12 + i::8, 0:w]))
-        dma("dtab%d" % n, [("YS"[k % 2], o, i, ["tabs"], ["tab2"]) for k, (o, i) in enumerate(items)])
+
+        def copies(which, a, b):
+            items = []
+            for i in which:
+                rows = 15 - 4 * i
+                items.append((T.tab2[32 * i + 11 - i::8, a:b], T.tabs[i:i + 8 * rows:8, a + 1:b + 1]))
+                items.append((T.tab2[4 + i:4 + i + 8 * rows:8, a:b], T.tabs[32 * i + 12 + i::8, a:b]))
+            return items
+        m = w // 16 * 8
+        op("V", ["h"], ["tabs0"], vscan, T.tabs[:, 0:m + 8], T.h[:, 0:m + 8], T.h[:, 0:m + 8], 0.0, A.max, A.max)
+        dma("dta%d" % n, [("YS"[k % 2], o, i, ["tabs0"], TAB2[0:1]) for k, (o, i) in enumerate(copies((0, 1), 0, m))])
+        op("V", ["h", "tabs0"], ["tabs1"], vscan, T.tabs[:, m + 8:w + 8], T.h[:, m + 8:w + 8], T.h[:, m + 8:w + 8], T.tabs[:, m + 7:m + 8], A.max, A.max)
+        dma("dtb%d" % n, [("YS"[k % 2], o, i, ["tabs0", "tabs1"], TAB2[1:2]) for k, (o, i) in enumerate(copies((0, 1), m, w) + copies((2, 3), 0, w))])
         if 0 < n < R: zeros("h", 0, width(n + 1) + 8)
 
-    def columns(step, out="colU"):
+    def columns(step):
         if step == 0: op("V", ["sdp"], ["cf"], vts, c("cf"), c("sdx", 1, 32, 2), -M, None, A.add)
         if step == 1: op("V", ["A", "cf"], ["cg"], vtt, c("cg"), T.AB[:, 15:256:16], c("cf"), A.subtract)
-        if step == 2: op("V", ["cg"], [out], vts, c(out), c("cg"), 256.0, None, A.mult)
+        if step == 2: op("V", ["cg"], ["colU"], vts, c("colU"), c("cg"), 256.0, None, A.mult)
 
-    def inverse(lst, keys, row, out):
-        op("V", keys + ["kval"], [row], vcp, T[row][:].indirect(c(lst)), T.kval[:])
-        hold(T.los[:], "los", "c1", T[row][:], row)
-        op("V", ["los", "pfix1"], [out], vts, c(out), T.los[:, 15::16], pfix1, None, A.add)
-
-    def pairs(src, key):
-        op("V", [key], ["kT"], V.transpose, T.kT[:], src)
-        op("V", ["kT"], ["pm"], vts, c("pm"), T.kT[:, 0::16], -0.498, M, A.add, A.add)
-
-    def lookups():
-        op("V", ["pm"], ["L"], vts, c("L"), c("pm"), -M, None, A.add)
+    def pairs(step, src=None, key=None):
+        if step == 0: op("V", key, ["kT"], V.transpose, T.kT[:], src)
+        if step == 1: op("V", ["kT"], ["pm"], vts, c("pm"), T.kT[:, 0::16], -0.498, M, A.add, A.add)
+        if step == 2: op("V", ["pm"], ["L"], vts, c("L"), c("pm"), -M, None, A.add)
 
     XO = [T.X[:, t:1024:4] for t in range(4)]
+    GO = [T.G[:, 256 * t:256 * t + 256] for t in range(4)]
 
-    def regather(key, outs, which=range(4), q="S"):
+    def regather(key, outs, which, q="S"):
         for t in which:
-            src = T.F[:, 256 * t:256 * t + 256].indirect(c("lou"))
-            if q == "S": op("S", ["F%d" % t, "lou"], ["%s%d" % (key, t)], act, outs[t], src, AF.Copy)
-            else: op("V", ["F%d" % t, "lou"], ["%s%d" % (key, t)], vcp, outs[t], src)
+            src = T.Fc[:, 256 * t:256 * t + 256].indirect(c("colU"))
+            if q == "S": op("S", ["Fc%d" % t, "colU"], ["%s%d" % (key, t)], act, outs[t], src, AF.Copy)
+            else: op("V", ["Fc%d" % t, "colU"], ["%s%d" % (key, t)], vcp, outs[t], src)
 
     def places(n):
-        op("V", ["tab2", "L", "gm"], ["gt"], vtt, T.gt[:], T.tab2[:, 0:width(n)].indirect(c("L")), T.gm[:], A.mult)
+        op("V", TAB2 + ["L", "gm"], ["gt"], vtt, T.gt[:], T.tab2[:, 0:width(n)].indirect(c("L")), T.gm[:], A.mult)
         op("V", ["gt"], ["gtT"], V.transpose, T.gtT[:], T.gt[:])
         op("V", ["gtT", "rst"], ["plc"], vscan, T.plc[:], T.rst[:], T.gtT[:], -FAR, A.max, A.subtract)
 
@@ -277,48 +284,53 @@ def rank_program(g, core, T, topo):
 
     XK = ["X0", "X1", "X2", "X3"]
 
-    def unpack():
+    def tail():
         op("S", XK, ["Xu"], act, T.X[:, 1024:1028], T.X[:, 1020:1024], AF.Copy)
+
+    def unpack():
         quant("xq", "xs", "X", 0, 256, XK)
         quant("xr", "xt", "X", 4, 256, XK + ["Xu"])
         for t in range(4):
             mm("ps%d" % t, "ec%d" % t, "es%d" % t, 0, "xq", "xs", 0, 256, True, False)
             mm("ps%d" % t, "ec%d" % t, "es%d" % t, 0, "xr", "xt", 0, 256, False, True)
             op("S", ["ps%d" % t], ["P%d" % t], act, T.P[:, 256 * t:256 * t + 256], T["ps%d" % t][:, 0:256], AF.Copy)
-        for t in range(4):
-            mm("ps%d" % (4 + t), "ec%d" % t, "es%d" % t, 0, "xq", "xs", 0, 256)
 
-    def unpack_keep():
+    def unpack_keep(n):
         for t in range(4):
-            op("S", ["ps%d" % (4 + t)], ["F%d" % t], act, T.F[:, 256 * t:256 * t + 256], T["ps%d" % (4 + t)][:, 0:256], AF.Copy, scale=2.0)
+            mm("ps%d" % t, "ec%d" % t, "es%d" % t, 0, "xq", "xs", 0, 256)
+            op("S", ["ps%d" % t], ["F%d" % t], act, T.F[:, 256 * t:256 * t + 256], T["ps%d" % t][:, 0:256], AF.Copy, scale=2.0)
+        for t in range(4):
+            op("S", ["F%d" % t] + rank_keys(n), ["Fc%d" % t], act, T.Fc[:, 256 * t:256 * t + 256], T.F[:, 256 * t:256 * t + 256].indirect(c("ru%d" % (n % 2))), AF.Copy)
 
-    def deal():
+    def deal(src, out):
         for t in range(4 - ND, 4):
             op("S", ["H%d" % t, "hu"], ["Hg%d" % t], act, T.Hg[:, 256 * t:256 * t + 256], T.H[:, 128 * t:128 * t + 128].indirect(c("hu")), AF.Copy)
         for t in range(4):
-            o, f = T.X[:, t:1024:4], T.G[:, 256 * t:256 * t + 256]
-            if t < 4 - ND: op("V", ["H%d" % t, "hu", "G%d" % t], [XK[t]], vtt, o, T.H[:, 128 * t:128 * t + 128].indirect(c("hu")), f, A.add)
-            else: op("V", ["Hg%d" % t, "G%d" % t], [XK[t]], vtt, o, T.Hg[:, 256 * t:256 * t + 256], f, A.add)
+            h, hk = (T.H[:, 128 * t:128 * t + 128].indirect(c("hu")), "H%d" % t) if t < 4 - ND else (T.Hg[:, 256 * t:256 * t + 256], "Hg%d" % t)
+            op("V", [hk, "hu", "%s%d" % (src, t)], ["%s%d" % (out, t)], vtt, T[out][:, t:1024:4], h, T[src][:, 256 * t:256 * t + 256], A.add)
 
     ranks(0)
-    op("S", ["mask"], ["c2"], act, T.c2[:], T.mask[:], AF.Copy, scale=FAR)
-    for t in range(4): op("S", ["xin"], ["F%d" % t], act, T.F[:, 256 * t:256 * t + 256], T.xin[:, t::4], AF.Copy)
-    op("S", ["junk"], ["tab2"], act, T.tab2[:, 0:2048], T.junk[:, 0:2048], AF.Identity, scale=0.0, bias=3.0)
+    op("S", ["iX", "pa"], ["away"], act, T.away[:], T.iX[:], AF.Abs, scale=-1.0, bias=pa)
+    op("S", ["away"], ["c2"], act, T.c2[:], T.away[:], AF.Relu, scale=-FAR, bias=FAR)
+    for t in range(4): op("S", ["xin"], ["Fc%d" % t], act, T.Fc[:, 256 * t:256 * t + 256], T.xin[:, t::4], AF.Copy)
+    op("S", ["junk"], TAB2, act, T.tab2[:, 0:2048], T.junk[:, 0:2048], AF.Identity, scale=0.0, bias=3.0)
     tables(0)
-    regather("X", XO, (1, 2))
-    regather("X", XO, (3,), "V")
-    pairs(T.ks[:, 0:256], "ks")
+    regather("X", XO, range(4))
+    pairs(0, T.ks[:, 0:256], ["ks"])
+    op("V", ["iU"], ["ul2"], vcp, c("ul", 8, 24), c("iU"))
+    pairs(1)
     quant("uq", "us", "uin", 0, 128)
-    lookups()
+    pairs(2)
     op("V", ["prw", "pown", "ptab"], ["gm"], vts, T.gm[:], T.prw[:], pown, ptab, A.not_equal, A.mult)
-    op("V", ["uq", "ul"], ["u2"], vcp, T.u2[:].bitcast(dt.uint32), T.uq[:].bitcast(dt.uint32).indirect(c("ul", 0, 8)))
-    unpack()
+    op("V", ["uq", "ul", "ul2"], ["u2"], vcp, T.u2[:].bitcast(dt.uint32), T.uq[:].bitcast(dt.uint32).indirect(c("ul")))
     places(0)
     place_list()
-    op("S", ["us", "ul"], ["u2s"], act, T.u2s[:], T.us[:].indirect(c("ul", 0, 8)), AF.Copy)
-    op("S", ["mask"], ["c1"], act, T.c1[:], T.mask[:], AF.Identity, scale=18 * FAR, bias=-FAR)
+    tail()
+    op("S", ["us", "ul", "ul2"], ["u2s"], act, T.u2s[:], T.us[:].indirect(c("ul")), AF.Copy)
+    op("S", ["c2"], ["c1"], act, T.c1[:], T.c2[:], AF.Identity, scale=18.0, bias=-FAR)
     op("S", ["mid0", "pmid"], ["mid1"], act, T.mid1[:], T.mid0[:], AF.Sign, bias=pmid)
     op("S", ["mid1"], ["mid"], act, T.mid[:], T.mid1[:], AF.Copy, scale=0.5)
+    unpack()
     cells(0)
     dma("dw", [("Y", T.wq[:].bitcast(dt.uint8), T.wc[:], ["gt"], ["wq"]), ("Y", T.wp[:], T.ws[:], [], ["wp"])])
     dma("dv", [("Y", T.vin[:], T.v[:], [], ["vin"])])
@@ -328,120 +340,115 @@ def rank_program(g, core, T, topo):
     m4 = sum(1 << e for e in topo.engines(core, nxt)[0:4])
 
     for n in range(R):
-        zq, zs = "zq%d" % n, "zs%d" % n
+        zq, zs, ru = "zq%d" % n, "zs%d" % n, "ru%d" % (n % 2)
         for t in (0, 1):
             op("V", ["P%d" % t, "ku"], ["Z%d" % t], vcp, T.Z[:, t:1024:4], T.P[:, 256 * t:256 * t + 256].indirect(c("ku")))
         for t in (2, 3):
             op("S", ["P%d" % t, "ku"], ["Z%d" % t], act, T.Z[:, t:1024:4], T.P[:, 256 * t:256 * t + 256].indirect(c("ku")), AF.Copy)
-        quant(zq, zs, "Z", 0, 256, ["Z0", "Z1", "Z2", "Z3"])
+        op("V", ["plc", "pp8"], ["cu"], vts, c("cu"), T.plc[:, 15::16], -0.125, pp8, A.mult, A.add)
+        for k, bank in ((0, "ps0"), (1, "ps7")):
+            a, b = 128 * k, 128 * k + 128
+            op("V", ["Z0", "Z1", "Z2", "Z3"], [zq + str(k), zq], V.quantize_mx, T[zq][:, a:b], T[zs][:, a:b], T.Z[:, 4 * a:4 * b], acc=k > 0)
+            mm(bank, "u2", "u2s", 0, zq, zs, a, 128, key=zq + str(k))
         need("G", [last[zq]])
         g.remote_dma(T["lc%d" % n][:].bitcast(dt.uint8), T[zq][:].bitcast(dt.uint8), T.sem["arr%d" % n], T.sem.snd, pid, rid, m4)
         g.remote_dma(T["lp%d" % n][:], T[zs][:], T.sem["arr%d" % n], T.sem.snd, pid, rid, m4)
-        if n == 0: zeros("h", 0, width(1) + 8)
-        if n < R - 1: zeros("Wp", 0, 2048)
-        mm("ps0", "u2", "u2s", 0, zq, zs, 0, 256)
-        mm("ps1", "u2", "u2s", 0, zq, zs, 0, 256)
-        op("V", ["plc", "pp8"], ["cu"], vts, c("cu"), T.plc[:, 15::16], -0.125, pp8, A.mult, A.add)
         if n == 0:
-            op("V", ["iX"], ["keepb"], vts, T.keepb[:], T.iX[:], 1.0, None, A.min)
-            quant("bc", "bs", "Bt", 0, 128)
-        if n == 1: quant("vq", "vqs", "vin", 0, 128)
-        if n == R - 1:
-            columns(0)
-            columns(1)
-        for k in (0, 1):
-            a, b = 128 * k, 128 * k + 128
-            op("V", ["ps0", "mask"], ["mk%d" % k], vtt, T.mk2[:, a:b], T.ps0[:, a:b], T.mask[:, a:b], A.mult)
-            op("V", ["mk%d" % k, "keepb"], ["sl%d" % k], vscan, T.sl[:, a:b], T.keepb[:, a:b], T.mk2[:, a:b], 0.0, A.mult, A.add)
+            op("G", ["Bt"], TAB2, g.iota, T.tab2[:, 2048:HW], [[0, HW - 2048]], 3, 0, allow_small_or_imprecise_dtypes=True)
+            zeros("h", 0, width(1) + 8)
+        if n < R - 1: zeros("Wp", 0, 2048)
+        for bank, la in ((1, 128), (3, 128), (2, 256), (4, 256)): mm("ps%d" % bank, "u2", "u2s", la, zq, zs, 0, 256, key=zq)
+        for k, bank in ((0, "ps0"), (1, "ps7")): op("V", [bank], ["sl%d" % k], V.transpose, T.sl[:, 128 * k:128 * k + 128], T[bank][:, 0:128])
 
-        def signs(k, lo, hi):
-            for t in range(4):
-                b = 4 * k + t
-                op("S", ["ps1", "sl%d" % (k // 2)], ["sg%d" % k], act, T.sg[:, 1024 * k + 4 * lo + t:1024 * k + 4 * hi:4], T.ps1[:, lo:hi], AF.Sign,
-                   bias=T.sl[:, 16 * b + 15:16 * b + 16], scale=-1.0, acc=t > 0)
+        def signs(k, lo, hi, ts=(0, 2, 1, 3)):
+            for t in ts:
+                b, bank = 64 * k + 16 * t, "ps%d" % (3 + t % 2)
+                op("S", [bank, "sl%d" % (k // 2)], ["sg%d" % k], act, T.sg[:, 1024 * k + 4 * lo + t:1024 * k + 4 * hi:4], T[bank][:, lo:hi], AF.Sign,
+                   bias=T.sl[:, b:b + 1], scale=-1.0, acc=True)
 
         def direct(k, lo, hi, how):
-            for t in range(4):
-                b = 4 * k + t
-                op("V", ["ps0", "sl%d" % (k // 2)], ["Cd%d" % k], vts, T.Ct[:, 1024 * k + 4 * lo + t:1024 * k + 4 * hi:4], T.ps0[:, lo:hi], T.sl[:, 16 * b + 15:16 * b + 16], None, how, acc=t > 0)
+            for t in (0, 2, 1, 3):
+                b, bank = 64 * k + 16 * t, "ps%d" % (1 + t % 2)
+                op("V", [bank, "sl%d" % (k // 2)], ["Cd%d" % k], vts, T.Ct[:, 1024 * k + 4 * lo + t:1024 * k + 4 * hi:4], T[bank][:, lo:hi], T.sl[:, b:b + 1], None, how, acc=True)
 
         def middle(k):
             a = 1280 * k
             op("V", ["sg%d" % k, "mid"], ["Cm%d" % k], vtt, T.Ct[:, a:a + 256], T.sg[:, a:a + 256], T.mid[:], A.is_lt)
 
-        def side(q, k, right):
+        def side(k, right, first=0, step=1):
             a, b = (1280 * k + 256, 1024 * k + 1024) if right else (1024 * k, 1280 * k)
-            key = "C%s%d" % ("lr"[right], k)
-            if q == "V": op("V", ["sg%d" % k], [key], vts, T.Ct[:, a:b], T.sg[:, a:b], 0.0, None, A.is_le if right else A.is_lt)
-            elif right: op("S", ["sg%d" % k], [key], act, T.Ct[:, a:b], T.sg[:, a:b], AF.Sign, bias=1.0, scale=-1.0)
-            else: op("S", ["sg%d" % k], [key], act, T.Ct[:, a:b], T.sg[:, a:b], AF.Relu, scale=-1.0)
+            o, i, key = T.Ct[:, a + first:b:step], T.sg[:, a + first:b:step], "C%s%d" % ("lr"[right], k)
+            if right: op("S", ["sg%d" % k], [key], act, o, i, AF.Sign, bias=1.0, scale=-1.0)
+            else: op("S", ["sg%d" % k], [key], act, o, i, AF.Relu, scale=-1.0)
 
         def total(k, keys, start, stop, halves=(0, 1)):
             a, b, key = 256 * k + 128 * halves[0], 256 * k + 128 * halves[-1] + 128, "cq%d%d" % (k, halves[0])
             op("V", keys, [key], V.quantize_mx, T.cq[:, a:b], T.cs[:, a:b], T.Ct[:, 4 * a:4 * b])
-            for j in halves: mm("ps%d" % (2 + j), "bc", "bs", 0, "cq", "cs", 256 * k + 128 * j, 128, start, stop, key)
-        signs(0, 0, 64)
-        signs(1, 0, 256)
+            for j in halves: mm("ps%d" % (5 + j), "bc", "bs", 0, "cq", "cs", 256 * k + 128 * j, 128, start, stop, key)
+        signs(0, 0, 64, (0, 2))
+        signs(1, 0, 256, (0,))
+        signs(0, 0, 64, (1, 3))
+        signs(1, 0, 256, (2, 1, 3))
         signs(3, 192, 256)
-        side("S", 1, 1)
-        side("S", 1, 0)
         signs(2, 0, 256)
-        side("S", 2, 0)
+        side(1, 1)
+        side(2, 0)
         direct(0, 64, 256, A.is_ge)
         middle(0)
         direct(3, 0, 192, A.is_gt)
+        if n == 0: quant("bc", "bs", "Bt", 0, 128)
         total(0, ["Cd0", "Cm0"], True, False)
         middle(3)
+        op("V", ["sg1"], ["Cl1"], vts, T.Ct[:, 1024:1280], T.sg[:, 1024:1280], 0.0, None, A.is_lt)
         middle(1)
         total(3, ["Cd3", "Cm3"], False, False)
-        total(1, ["Cl1", "Cr1", "Cm1"], False, False)
         middle(2)
-        side("V", 2, 1)
+        op("V", ["sg2"], ["Cr2"], vts, T.Ct[:, 2816:3072], T.sg[:, 2816:3072], 0.0, None, A.is_le)
+        total(1, ["Cl1", "Cr1", "Cm1"], False, False)
         total(2, ["Cr2", "Cm2"], False, True, (1,))
         total(2, ["Cl2"], False, True, (0,))
-        if n == R - 1: columns(2)
-        op("S", ["ps3"], ["stw1"], act, T.stw[:, 128:256], T.ps3[:, 0:128], AF.Copy, scale=2.0)
-        op("V", ["ps2"], ["stw0"], vts, T.stw[:, 0:128], T.ps2[:, 0:128], 2.0, None, A.mult)
-        op("V", ["stw0", "stw1", "cu", "ks"], ["Krow"], vtt, T.Krow[:], T.stw[:].indirect(c("cu")), T.ks[:, 0:256], A.add)
+        op("S", ["ps6"], ["stw1"], act, T.stw[:, 128:256], T.ps6[:, 0:128], AF.Copy)
+        op("V", ["ps5"], ["stw0"], vcp, T.stw[:, 0:128], T.ps5[:, 0:128])
+        op("V", ["stw0", "stw1", "cu", "ks"], ["Ksl"], vtt, T.Ksl[:], T.stw[:].indirect(c("cu")), T.ks[:, 0:256], A.add)
+        op("S", ["Ksl"] + rank_keys(n), ["Kr0"], act, T.Krow[:, 0:128], T.Ksl[:].indirect(c(ru, 0, 8)), AF.Copy)
+        op("V", ["Ksl"] + rank_keys(n), ["Kr1"], vcp, T.Krow[:, 128:256], T.Ksl[:].indirect(c(ru, 8, 16)))
         ranks(n + 1)
-        unpack_keep()
-        if n == 0: op("S", ["junk"], ["tab2"], act, T.tab2[:, 2048:HW], T.junk[:, 0:HW - 2048], AF.Identity, scale=0.0, bias=3.0)
+        unpack_keep(n)
         need("T", [("arr%d" % n, 8, "R", {})])
         ends["arr%d" % n] = 8
-        for t in range(4):
-            mm("ps%d" % (4 + t), "wq", "wp", 128 * t, "lc%d" % n, "lp%d" % n, 0, 256)
-            op("S", ["ps%d" % (4 + t)], ["H%d" % t], act, T.H[:, 128 * t:128 * t + 128], T["ps%d" % (4 + t)][:, 1:256:2], AF.Copy, scale=0.03125)
+        for t in range(4): mm("ps%d" % (4 + t), "wq", "wp", 128 * t, "lc%d" % n, "lp%d" % n, 0, 256)
+        for t in range(4): op("S", ["ps%d" % (4 + t)], ["H%d" % t], act, T.H[:, 128 * t:128 * t + 128], T["ps%d" % (4 + t)][:, 1:256:2], AF.Copy, scale=0.03125)
         tables(n + 1)
         if n < R - 1:
-            inverse("ru", RU, "lor", "lou")
-            regather("G", [T.G[:, 256 * t:256 * t + 256] for t in range(4)])
-            pairs(T.ks[:, 0:256], "ks")
-            lookups()
+            columns(0)
+            pairs(0, T.ks[:, 0:256], ["ks"])
+            columns(1)
+            pairs(1)
+            columns(2)
+            pairs(2)
+            regather("G", GO, (1, 2, 3))
+            regather("G", GO, (0,), "V")
             places(n + 1)
             op("V", ["plc", "pp16"], ["hu"], vts, c("hu"), T.plc[:, 15::16], -0.0625, pp16, A.mult, A.add)
             place_list()
-            deal()
+            deal("G", "X")
+            tail()
             unpack()
             cells(n + 1)
 
-    inverse("colU", ["colU"], "ivr", "iu")
-    pairs(T.Krow[:], "Krow")
-    op("V", RU + ["pp1"], ["rg"], vts, c("rg"), c("ru"), pp1, None, A.add)
-    lookups()
+    pairs(0, T.Krow[:], KR)
+    op("V", rank_keys(R) + ["pp1"], ["rg"], vts, c("rg"), c("ru%d" % (R % 2)), pp1, None, A.add)
+    pairs(1)
     op("V", ["rg", "el"], ["rf"], vtt, c("rf"), c("rg"), c("el"), A.subtract)
-    op("S", ["Krow", "iu"], ["ptk"], act, T.ptk[:], T.Krow[:].indirect(c("iu")), AF.Identity, bias=-0.498)
-    op("S", ["ptk"], ["ptf"], act, T.ptf[:], T.ptk[:], AF.Identity, bias=M)
-    op("S", ["ptf"], ["ptg"], act, T.ptg[:], T.ptf[:], AF.Identity, bias=-M)
+    pairs(2)
+    quant("vq", "vqs", "vin", 0, 128)
+    op("V", KR, ["ptf"], vts, T.ptf[:], T.Krow[:], -0.498, M, A.add, A.add)
+    op("V", ["ptf"], ["ptg"], vts, T.ptg[:], T.ptf[:], -M, None, A.add)
     dma("dpt", [("Y", T.pt[:], T.ptg[0::16, :], ["ptg"], [])])
     places(R)
     op("V", ["plc", "rf"], ["plf"], vtt, c("plf"), c("rf"), T.plc[:, 15::16], A.subtract)
     op("V", ["plf"], ["hu"], vts, c("hu"), c("plf"), 0.0625, -0.46875, A.mult, A.add)
-    op("S", ["H3", "hu"], ["Hg3"], act, T.Hg[:, 768:1024], T.H[:, 384:512].indirect(c("hu")), AF.Copy)
-    for t in range(4):
-        h, hk = (T.H[:, 128 * t:128 * t + 128].indirect(c("hu")), "H%d" % t) if t < 3 else (T.Hg[:, 768:1024], "Hg3")
-        op("V", [hk, "hu", "F%d" % t], ["XP%d" % t], vtt, T.XP[:, 256 * t:256 * t + 256], h, T.F[:, 256 * t:256 * t + 256], A.add)
-        if t < 3: op("S", ["XP%d" % t, "iu"], ["Xf%d" % t], act, T.Xf[:, t:1024:4], T.XP[:, 256 * t:256 * t + 256].indirect(c("iu")), AF.Copy)
-        else: op("V", ["XP%d" % t, "iu"], ["Xf%d" % t], vcp, T.Xf[:, t:1024:4], T.XP[:, 256 * t:256 * t + 256].indirect(c("iu")))
+    deal("Fc", "Xf")
 
     quant("fq", "fqs", "Xf", 0, 256, ["Xf0", "Xf1", "Xf2", "Xf3"])
     for k in (0, 1): mm("ps%d" % k, "vq", "vqs", 0, "fq", "fqs", 128 * k, 128)

@@ -2,10 +2,11 @@ from concourse.mybir import dt, AluOpType as A, ActivationFunctionType as AF
 
 N, R, C = 8, 3, 256
 HW = 2832
-NV = 6
+NV = 5
 ND = 2
 NA = 12
-M = 12582912.0
+NE = 8
+M = 8388608.0
 FAR = 4096.0
 F8 = "float8_e4m3fn_x4"
 LISTS = {}
@@ -28,29 +29,30 @@ def _scratch():
             LISTS[n] = (buf, at, w)
             at += (w + 15) // 16 * 16
         sb(buf, at, d)
-    lists("lstf", "float32", "kl el Kl K16 acc rl rf rg sd0 sdx of pm cf cg plf par", {"sd0": 32, "sdx": 64, "of": 32})
+    lists("lstf", "float32", "kl el Kl acc rf rg sd0 sdx of cg plf par pas", {"sd0": 32, "sdx": 32, "of": 32})
     lists("lsti", "int32", "iB iU pl ip iq", {"ip": 2, "iq": 8})
-    lists("lstu", "uint16", "kapU ul ru0 ru1 ou pu hu cu ku colU L", {"ul": 24})
-    sb("prow", 256, "int32")
-    sb("er Ksl Krow sl Ks kT ptf ptg yo", 256)
+    lists("lstu", "uint16", "pU ul ru rk0 rk1 ou pu hu cu ku colU L", {})
+    sb("num", 2048)
+    sb("er Ksl Krow sl Ks kT ptf yo away near", 256)
     sb("AB", 512)
     sb("ks", 264)
-    sb("away iX c1 c2 kval stw gt gtT gm rst prw mid0 mid1 mid kuh", 256, "bfloat16")
+    sb("iX cs c2 kval stw gt gtT gm0 gm rst prw kuh rs rc rh", 256, "bfloat16")
+    sb("mid0 mid1 mid", 256, "bfloat16")
     sb("plc", 256, "float16")
     sb("junk", 256 * (16 - NV), "bfloat16")
     sb("cmp", 256 * NV, "bfloat16")
     sb("sc", 128 * NV, "float16")
-    sb("h", HW + 256, "bfloat16")
-    sb("tabs tab2", HW, "bfloat16")
+    sb("h", HW + 2048, "bfloat16")
+    sb("tabs", HW, "bfloat16")
     sb("Wp", 2048, "bfloat16")
     sb("uin vin Bt H", 512, "bfloat16")
     sb("Ct sg", 4096, "bfloat16")
     sb("Ws Z P F Fc G Hg Xf xin", 1024, "bfloat16")
     sb("X", 1032, "bfloat16")
-    sb("EE one", 520, "bfloat16")
+    sb("EE", 520, "bfloat16")
     for t in range(4): mx("ec%d" % t, "es%d" % t, 128)
-    for n, m, w in (("bc", "bs", 128), ("xq", "xs", 256), ("xr", "xt", 256), ("cq", "cs", 1024),
-                    ("uq", "us", 128), ("u2", "u2s", 384), ("vq", "vqs", 128), ("wq", "wp", 512), ("fq", "fqs", 256)): mx(n, m, w)
+    for n, m, w in (("bc", "bs", 128), ("xq", "xs", 256), ("xr", "xt", 256), ("cq", "cs_", 1024),
+                    ("uq", "us", 128), ("u2", "u2s", 256), ("vq", "vqs", 128), ("wq", "wp", 512), ("fq", "fqs", 256)): mx(n, m, w)
     for k in range(R):
         mx("zq%d" % k, "zs%d" % k, 256)
         mx("lc%d" % k, "lp%d" % k, 256)
@@ -59,7 +61,7 @@ def _scratch():
 
 
 SCRATCH = _scratch()
-DSEM = ["dp", "drow", "dx", "du", "dw", "dv", "dend", "dpt"] + ["dt%s%d" % (x, k) for x in "ab" for k in range(R + 1)]
+DSEM = ["df", "dh", "dp", "dx", "du", "dw", "dv", "dend", "dpt"] + ["dt%s%d" % (x, k) for x in "ab" for k in range(R + 1)]
 TAB2 = ["tab2", "tab3"]
 SEMAPHORES = ["qV", "qS", "qT", "qG", "snd"] + ["arr%d" % k for k in range(R)] + DSEM
 
@@ -134,11 +136,16 @@ def rank_program(g, core, T, topo):
         op("T", [lq, ls] + ([key] if key else [rq, rs]), [bank], PE.matmul_mx, T[bank][:, 0:n], T[lq][:, la:la + 128], T[ls][:, la:la + 128],
            T[rq][:, ra:ra + n], T[rs][:, ra:ra + n], start, stop, acc=not start)
 
-    def hold(out, ok, cn, row, rk, w=256):
-        op("V", [cn, rk], [ok], vscan, out, T[cn][:, 0:w], row, 0.0, A.add, A.min)
+    def hold(out, ok, row, rk):
+        op("V", ["c2", rk], [ok], vscan, out, T.c2[:], row, 0.0, A.add, A.min)
+
+    def turn(out, ok, row, rk, w=256):
+        op("V", ["cs", "sig", rk], [ok], vscan, out, T.cs[:, 0:w], row, psig, A.mult, A.min)
+
+    def gather(out, ok, win, wk, lst, lk):
+        op("S", wk + lk, [ok], act, out, win.indirect(lst), AF.Copy)
 
     dma("dp", [("Y", c("pl"), T.p[:], [], ["pl"])])
-    dma("drow", [("SY"[x % 2], T.prow[x::16, :], T.p[:], [], ["prow"]) for x in range(16)])
     dma("dx", [("Y", T.xin[:], T.x[:], [], ["xin"])])
     dma("du", [("Y", T.uin[:], T.u[:], [], ["uin"])])
 
@@ -151,113 +158,120 @@ def rank_program(g, core, T, topo):
         op("G", [], [n], g.iota, T[n][:, a:b], [[0, b - a]], 0, 0, allow_small_or_imprecise_dtypes=True)
 
     def width(n):
-        return (2048 + 255 * n + 7) // 8 * 8
+        return (2049 + 255 * n + 7) // 8 * 8
+    NUM = ["num%d" % j for j in range(8)]
+    op("V", [], ["halves"], V.memset, T.gt[:], 0.5)
+    op("V", ["halves"], NUM[0:1], vscan, T.num[:, 0:256], T.gt[:], T.gt[:], -1.0, A.add, A.add)
     iota("ip", [[0, 2]], 0, 1)
     iota("iB", [[1, 16]])
-    op("V", [], ["one"], V.memset, T.one[:], 0.5)
-    op("G", ["one"], ["EE"], g.affine_select, T.EE[:], T.one[:], [[-1, 520]], A.is_equal, 0.0, 4, 4)
-    iota("kval", [[1, 256]], 1, small=True)
-    iota("iX", [[0, 16], [1, 16]], small=True)
-    zeros("h", 0, width(0) + 8)
-    iota("prw", [[0, 8], [1, 2], [0, 16]], small=True)
-    iota("rst", [[-16, 16], [-4096, 16]], 1024, small=True)
     iota("iU", [[16, 2], [32, 4], [0, 2]])
-    zeros("Wp", 0, 2048)
-    iota("mid0", [[1, 64], [-32, 2], [0, 2]], small=True)
+    iota("iX", [[0, 16], [1, 16]], small=True)
+    HALF = (width(0) + 8) // 2
+    zeros("Wp", 0, HALF)
+    dma("dh", [("Y", T.h[:, a:a + HALF], T.Wp[:, 0:HALF], ["Wp"], ["h"]) for a in (0, HALF)])
+    dma("df", [("Y", T.Wp[:, HALF:2048], T.Wp[:, 0:2048 - HALF], ["Wp"], ["Wq"])])
+    op("G", [], ["kse"], g.iota, T.ks[:, 256:264], [[0, 8]], HW - 1, 0, allow_small_or_imprecise_dtypes=True)
+    op("G", [], ["sd0"], g.iota, c("sd0"), [[0, 32]], 0, 0, allow_small_or_imprecise_dtypes=True)
+    op("G", [], ["sdd"], g.iota, c("sdx", 0, 32, 2), [[128, 16]], HW, 1, allow_small_or_imprecise_dtypes=True)
+    op("G", ["Wp"], ["EE"], g.affine_select, T.EE[:], T.Wp[:, 0:520], [[-1, 520]], A.not_equal, 0.5, 4, 4)
+    for k, (sh, bits) in enumerate(((0, 15), (0, 7), (3, 15), (3, 3), (0, 31))):
+        op("V", ["ip"], ["iq%d" % k], vts, c("iq", k, k + 1), c("ip", 0, 1), sh, bits, A.arith_shift_right, A.bitwise_and)
+    op("V", NUM[0:1], [NUM[7]], vts, T.num[:, 1792:2048], T.num[:, 0:256], 1792.0, None, A.add)
+    op("V", ["iq%d" % k for k in range(5)], ["pa", "pr"], vcp, c("par", 0, 5), c("iq", 0, 5))
+    op("V", NUM[0:1], [NUM[5]], vts, T.num[:, 1280:1536], T.num[:, 0:256], 1280.0, None, A.add)
+    pa, pr, pm, pm4, pq, pb, pp1, pp16 = [c("par", k, k + 1) for k in range(8)]
+    psig, pneg, phalf, pfar, pw, pv, pside, pdist, pth, pno, pnil, pcut, pout = [c("pas", k, k + 1) for k in range(13)]
+    for j in range(1, 5): op("S", NUM[0:1], [NUM[j]], act, T.num[:, 256 * j:256 * j + 256], T.num[:, 0:256], AF.Identity, bias=256.0 * j)
+    op("S", NUM[0:1], ["er"], act, T.er[:], T.num[:, 0:256], AF.Identity, scale=1.0 / 256, bias=1.0 + 1.0 / 512)
+    op("V", ["iB", "pa"], ["el"], vts, c("el"), c("iB"), 16.0, pa, A.mult, A.add)
+    op("V", NUM[0:1], [NUM[6]], vts, T.num[:, 1536:1792], T.num[:, 0:256], 1536.0, None, A.add)
+    op("V", ["el"], ["kl"], vts, c("kl"), c("el"), 1.0 / 256, 1.0 + 1.0 / 512, A.mult, A.add)
+    op("V", ["pl"], ["pU"], vcp, c("pU"), c("pl"))
+    op("V", ["pl", "kl"], ["Kl"], vtt, c("Kl"), c("pl"), c("kl"), A.add)
+    op("V", NUM + ["pU", "er"], ["Krow"], vtt, T.Krow[:], T.num[:].indirect(c("pU")), T.er[:], A.add)
+    op("V", ["iX", "pa"], ["c2"], vts, T.c2[:], T.iX[:], pa, FAR, A.is_equal, A.mult)
+    iota("prw", [[0, 8], [2, 2], [0, 16]], small=True)
+    iota("rst", [[-16, 16], [-8192, 16]], 1024 + 9 * 256, small=True)
+    iota("mid0", [[2, 64], [0, 2], [-64, 2]], -1, small=True)
     zeros("Bt", 0, 512)
     for j in range(N):
-        op("G", ["Bt"], ["Bt"], g.iota, T.Bt[j // 2 * 32:j // 2 * 32 + 32, 64 * j + j % 2:64 * j + 64:2], [[0, 32]], 1, 0, allow_small_or_imprecise_dtypes=True, acc=True)
-    for k, (sh, bits) in enumerate(((0, 15), (0, 7), (3, 1), (2, 1), (4, 1))):
-        op("V", ["ip"], ["iq%d" % k], vts, c("iq", k, k + 1), c("ip", 0, 1), sh, bits, A.arith_shift_right, A.bitwise_and)
-    op("V", ["iq%d" % k for k in range(5)], ["pa"], vcp, c("par", 0, 5), c("iq", 0, 5))
-    pa, pr, phi, pc, ph, pa16, pfix, p16, pown, ptab, px, pw, pp1, pp8, pp16, pmid = [c("par", k, k + 1) for k in range(16)]
-    op("V", [], ["kse"], V.memset, T.ks[:, 256:264], HW - 1.0)
-    op("V", ["iB", "pa"], ["el"], vts, c("el"), c("iB"), 16.0, pa, A.mult, A.add)
-    op("V", ["pa"], ["pa16"], vts, pa16, pa, 16.0, None, A.mult)
-    op("V", ["pa"], ["px"], vts, px, pr, 2.0, phi, A.mult, A.add)
-    op("V", ["el"], ["kl"], vts, c("kl"), c("el"), 1.0 / 256, None, A.mult)
-    op("V", ["iB", "pa16"], ["kapU"], vts, c("kapU"), c("iB"), pa16, None, A.add)
-    op("V", ["px"], ["pw"], vts, pw, px, ph, -8.0, A.add, A.add)
-    op("V", [], ["sd0"], V.memset, c("sd0"), 0.0)
-    for t in range(4): quant("ec%d" % t, "es%d" % t, "EE", 4 - t, 128)
-    for o, key, scale, bias in ((pfix, "pfix", -FAR, 15 * FAR),
-                                (p16, "p16", -1.0, -0.5),
-                                (pp1, "pp1", 1.0, 1003.0), (pp8, "pp8", 0.125, 1003 / 8 - 0.4375), (pp16, "pp16", 0.0625, 1003 / 16 - 0.46875)):
-        op("S", ["pa"], [key], act, o, pa, AF.Identity, scale=scale, bias=bias)
-    op("S", ["p16"], ["pmid"], act, pmid, ph, AF.Identity, scale=-16.0, bias=p16)
-    op("S", ["el"], ["sdd"], act, c("sdx", 0, 32, 2), c("el"), AF.Identity, bias=M + HW - 1.0)
-    op("S", ["kval"], ["er"], act, T.er[:], T.kval[:], AF.Identity, scale=1.0 / 256, bias=-1.0 / 256)
-    op("V", ["pl", "kl"], ["Kl"], vtt, c("Kl"), c("pl"), c("kl"), A.add)
-    op("V", ["pw"], ["pown"], vts, pown, pw, pc, 1.0, A.subtract, A.add)
-    op("V", ["pw"], ["ptab"], vts, ptab, pw, 0.0, None, A.not_equal)
-    op("V", ["iB"], ["ul"], vts, c("ul", 0, 8), c("iB", 0, 8), 16.0, None, A.mult)
-    KR = ["Kr0", "Kr1"]
-    op("V", ["prow", "kapU", "er"], KR, vtt, T.Krow[:], T.prow[:].indirect(c("kapU")), T.er[:], A.add)
+        op("G", ["Bt"], ["Bt"], g.iota, T.Bt[j // 2 * 32:j // 2 * 32 + 32, 64 * j:64 * j + 64], [[0, 16], [2 * (j % 2) - 1, 2], [0, 2]], 1 - j % 2, 0, allow_small_or_imprecise_dtypes=True, acc=True)
 
     def count(b):
-        op("V", ["cmp%d" % b], ["sc%d" % b], vscan, T.sc[:, 128 * b:128 * b + 128], T.cmp[:, 256 * b:256 * b + 128], T.cmp[:, 256 * b + 128:256 * b + 256], 0.0, A.add, A.add)
+        op("V", ["cmp%d" % b], ["sc%d" % b], vscan, T.sc[:, 128 * b:128 * b + 128], T.cmp[:, 256 * b:256 * b + 128], T.cmp[:, 256 * b + 128:256 * b + 256], -127.5, A.add, A.add)
 
     def ranks(n):
-        ru = "ru%d" % (n % 2)
+        ru, row, rk = ("ru", T.Ksl, "Ksl") if n else ("rk0", T.Krow, "Krow")
         if n:
-            hold(T.Ks[:, 128:256], "Ks1", "c1", T.Krow[:, 128:256], "Kr1", 128)
-            hold(T.Ks[:, 0:128], "Ks0", "c1", T.Krow[:, 0:128], "Kr0", 128)
-            op("S", ["Ks1", "pfix"], ["Kl"], act, c("Kl", 8, 16), T.Ks[:, 143::16], AF.Identity, bias=pfix)
-        for j, b in enumerate(list(range(8, NA)) + list(range(NV, 8)) + list(range(NA, 16))):
-            if n and j == 1 and NV < 8: op("S", ["Ks0", "pfix"], ["Km"], act, c("Kl", NV, 8), T.Ks[:, 16 * NV + 15:128:16], AF.Identity, bias=pfix)
-            op("S", KR + ["Kl" if b >= 8 or n == 0 else "Km"], ["junk", "acc%d" % (b >= NA)], act, T.junk[:, 256 * j:256 * j + 256], T.Krow[:], AF.Sign, bias=c("Kl", b, b + 1),
-               scale=-1.0, accum_out=c("acc", b, b + 1), acc=j > 0)
+            for k in (0, 1): turn(T.Ks[:, 128 * k:128 * k + 128], "Ks%d" % k, row[:, 128 * k:128 * k + 128], rk, 128)
+
+        def key(b): return (T.Ks[:, 16 * b + 15:16 * b + 16], ["Ks%d" % (b // 8), "sig"]) if n else (c("Kl", b, b + 1), ["Kl"])
+        for j, b in enumerate(range(NV, 16)):
+            op("S", [rk] + key(b)[1], ["junk", "acc%d" % (b >= NA)], act, T.junk[:, 256 * j:256 * j + 256], row[:, 0:256], AF.Sign, bias=key(b)[0],
+               scale=pneg if n else -1.0, accum_out=c("acc", b, b + 1), acc=j > 0)
         for b in range(NV):
             o = T.cmp[:, 256 * b:256 * b + 256]
-            if n: op("V", KR + ["Ks0", "pfix"], ["cmp%d" % b], vts, o, T.Krow[:], pfix, T.Ks[:, 16 * b + 15:16 * b + 16], A.subtract, A.is_lt)
-            else: op("V", KR + ["Kl"], ["cmp%d" % b], vts, o, T.Krow[:], c("Kl", b, b + 1), None, A.is_lt)
+            if n: op("V", [rk] + key(b)[1], ["cmp%d" % b], vts, o, row[:, 0:256], psig, key(b)[0], A.mult, A.is_lt)
+            else: op("V", [rk] + key(b)[1], ["cmp%d" % b], vts, o, row[:, 0:256], key(b)[0], None, A.is_lt)
             if b: count(b - 1)
-        op("V", ["acc0"], [ru + "S"], vts, c(ru, NV, NA), c("acc", NV, NA), 0.5, 127.5, A.mult, A.add)
+        half = phalf if n else 0.5
+        if n == 0:
+            quant("uq", "us", "uin", 0, 128)
+            op("V", ["iU"], ["ul"], vcp, c("ul"), c("iU"))
+        op("V", ["acc0"], [ru + "S"], vts, c(ru, NV, NA), c("acc", NV, NA), half, 127.5, A.mult, A.add)
         count(NV - 1)
-        op("V", ["sc%d" % b for b in range(NV)], [ru + "V"], vcp, c(ru, 0, NV), T.sc[:, 127::128])
-        op("V", [ru + "S", ru + "V", "kse"] + KR, ["ks"], vcp, T.ks[:, 0:256].indirect(c(ru, 0, NA)), T.Krow[:, 0:16 * NA])
-        op("V", ["acc1"], [ru + "T"], vts, c(ru, NA, 16), c("acc", NA, 16), 0.5, 127.5, A.mult, A.add)
-        op("V", [ru + "T"] + KR, ["ks"], vcp, T.ks[:, 0:256].indirect(c(ru, NA, 16)), T.Krow[:, 16 * NA:256], acc=True)
+        op("V", ["sc%d" % b for b in range(NV)], [ru + "V"], vts, c(ru, 0, NV), T.sc[:, 127::128], psig if n else 1.0, 127.5, A.mult, A.add)
+        op("V", [ru + "S", ru + "V", "kse", rk], ["ks"], vcp, T.ks[:, 0:256].indirect(c(ru, 0, NA)), row[:, 0:16 * NA])
+        op("V", ["acc1"], [ru + "T"], vts, c(ru, NA, 16), c("acc", NA, 16), half, 127.5, A.mult, A.add)
+        op("V", [ru + "T", rk], ["ks"], vcp, T.ks[:, 0:256].indirect(c(ru, NA, 16)), row[:, 16 * NA:256], acc=True)
 
-    def rank_keys(n):
-        return ["ru%d%s" % (n % 2, x) for x in "SVT"]
+    def slots(n):
+        k = "rk%d" % (n % 2)
+        return c(k), [k + x for x in "SVT"]
 
     def tables(n):
         w = width(n)
-        hold(T.AB[:, 0:256], "A", "c2", T.ks[:, 0:256], "ks")
-        hold(T.AB[:, 256:512], "B", "c2", T.ks[:, 1:257], "ks")
-        op("V", ["A", "B"], ["sdp"], vts, c("sdx", 1, 64, 2), T.AB[:, 15::16], -0.498, M, A.add, A.add)
-        op("V", ["sdp"], ["sd0"], vtt, c("sd0", 1, 32, 2), c("sdx", 1, 32, 2), c("sdx", 33, 64, 2), A.is_equal)
+        hold(T.AB[:, 0:256], "A", T.ks[:, 0:256], "ks")
+        hold(T.AB[:, 256:512], "B", T.ks[:, 1:257], "ks")
+        op("V", ["A"], ["sdp"], vts, c("sdx", 1, 32, 2), T.AB[:, 15:256:16], M - 0.5, 1.0 - M, A.add, A.add)
+        op("V", ["sdp", "B"], ["sd0"], vtt, c("sd0", 1, 32, 2), T.AB[:, 271::16], c("sdx", 1, 32, 2), A.is_lt)
         if n == 0: columns(0)
-        op("V", ["sd0", "sdp", "sdd"], ["of"], vscan, c("of"), c("sd0"), c("sdx", 0, 32), 0.0, A.mult, A.max)
+        op("V", ["sd0", "sdp", "sdd"], ["of"], vscan, c("of"), c("sd0"), c("sdx"), 0.0, A.mult, A.max)
         if n == 0: columns(1)
-        op("V", ["of"], ["ou"], vts, c("ou"), c("of", 1, 32, 2), 1.0 - M, None, A.add)
-        if n == 0: columns(2)
+        op("V", ["of"], ["ou"], vcp, c("ou"), c("of", 1, 32, 2))
         op("V", ["ou", "kval"], ["h"], vcp, T.h[:].indirect(c("ou")), T.kval[:])
+        if n == 0:
+            regather("X", XO, range(4))
+            tail()
+            op("S", ["prw", "pside", "pout"], ["gm0"], act, T.gm0[:], T.prw[:], AF.Sign, scale=pside, bias=pout)
 
         def copies(which, a, b):
             items = []
             for i in which:
                 rows = 15 - 4 * i
-                items.append((T.tab2[32 * i + 11 - i::8, a:b], T.tabs[i:i + 8 * rows:8, a + 1:b + 1]))
-                items.append((T.tab2[4 + i:4 + i + 8 * rows:8, a:b], T.tabs[32 * i + 12 + i::8, a:b]))
+                items.append((T.tabs[32 * i + 9 + i::8, a:b], T.tabs[0:8 * rows:8, a + 1:b + 1]))
+                items.append((T.tabs[7 - i:8 * rows:8, a:b], T.tabs[32 * i + 8::8, a:b]))
             return items
         m = w // 16 * 8
         op("V", ["h"], ["tabs0"], vscan, T.tabs[:, 0:m + 8], T.h[:, 0:m + 8], T.h[:, 0:m + 8], 0.0, A.max, A.max)
-        dma("dta%d" % n, [("YS"[k % 2], o, i, ["tabs0"], TAB2[0:1]) for k, (o, i) in enumerate(copies((0, 1), 0, m))])
+        dma("dta%d" % n, [("Y", o, i, ["tabs0"], TAB2[0:1]) for o, i in copies((0, 1), 0, m)])
         op("V", ["h", "tabs0"], ["tabs1"], vscan, T.tabs[:, m + 8:w + 8], T.h[:, m + 8:w + 8], T.h[:, m + 8:w + 8], T.tabs[:, m + 7:m + 8], A.max, A.max)
         dma("dtb%d" % n, [("YS"[k % 2], o, i, ["tabs0", "tabs1"], TAB2[1:2]) for k, (o, i) in enumerate(copies((0, 1), m, w) + copies((2, 3), 0, w))])
         if 0 < n < R: zeros("h", 0, width(n + 1) + 8)
 
     def columns(step):
-        if step == 0: op("V", ["sdp"], ["cf"], vts, c("cf"), c("sdx", 1, 32, 2), -M, None, A.add)
-        if step == 1: op("V", ["A", "cf"], ["cg"], vtt, c("cg"), T.AB[:, 15:256:16], c("cf"), A.subtract)
-        if step == 2: op("V", ["cg"], ["colU"], vts, c("colU"), c("cg"), 256.0, None, A.mult)
+        if step == 0: op("V", ["A", "sdp"], ["cg"], vtt, c("cg"), T.AB[:, 15:256:16], c("sdx", 1, 32, 2), A.subtract)
+        if step == 1: op("V", ["cg"], ["colU"], vts, c("colU"), c("cg"), 256.0, 255.5, A.mult, A.add)
 
     def pairs(step, src=None, key=None):
         if step == 0: op("V", key, ["kT"], V.transpose, T.kT[:], src)
-        if step == 1: op("V", ["kT"], ["pm"], vts, c("pm"), T.kT[:, 0::16], -0.498, M, A.add, A.add)
-        if step == 2: op("V", ["pm"], ["L"], vts, c("L"), c("pm"), -M, None, A.add)
+        if step == 1: op("V", ["kT"], ["L"], vts, c("L"), T.kT[:, 0::16], -0.5, None, A.add)
+
+    def follow(step, n):
+        if step == 0: gather(T.rs[:], "rs", T.kval[:], ["kval"], c("ru"), ["ruS", "ruV", "ruT"])
+        if step == 1: gather(T.rc[:], "rc", T.rs[:], ["rs"], *slots(n))
+        if step == 2: turn(T.rh[:], "rh", T.rc[:], "rc")
+        if step == 3: op("V", ["rh", "sig"], slots(n + 1)[1], vts, slots(n + 1)[0], T.rh[:, 15::16], psig, -1.0, A.mult, A.add)
 
     XO = [T.X[:, t:1024:4] for t in range(4)]
     GO = [T.G[:, 256 * t:256 * t + 256] for t in range(4)]
@@ -269,7 +283,7 @@ def rank_program(g, core, T, topo):
             else: op("V", ["Fc%d" % t, "colU"], ["%s%d" % (key, t)], vcp, outs[t], src)
 
     def places(n):
-        op("V", TAB2 + ["L", "gm"], ["gt"], vtt, T.gt[:], T.tab2[:, 0:width(n)].indirect(c("L")), T.gm[:], A.mult)
+        op("V", TAB2 + ["tabs0", "tabs1", "L", "gm"], ["gt", "halves"], vtt, T.gt[:], T.tabs[:, 0:width(n)].indirect(c("L")), T.gm[:], A.max)
         op("V", ["gt"], ["gtT"], V.transpose, T.gtT[:], T.gt[:])
         op("V", ["gtT", "rst"], ["plc"], vscan, T.plc[:], T.rst[:], T.gtT[:], -FAR, A.max, A.subtract)
 
@@ -277,9 +291,9 @@ def rank_program(g, core, T, topo):
         op("V", ["plc", "pp1"], ["pu"], vts, c("pu"), T.plc[:, 15::16], -1.0, pp1, A.mult, A.add)
 
     def cells(n):
-        op("V", ["pu", "kval"], ["Wp"], vcp, T.Wp[:].indirect(c("pu")), T.kval[:])
+        op("V", ["pu", "kval", "Wq"], ["Wp"], vcp, T.Wp[:].indirect(c("pu")), T.kval[:])
         op("V", ["Wp"], ["Ws"], vscan, T.Ws[:], T.Wp[:, 0::2], T.Wp[:, 1::2], 1.0, A.max, A.max)
-        hold(T.kuh[:], "kuh", "c2", T.Ws[:, 3::4], "Ws")
+        hold(T.kuh[:], "kuh", T.Ws[:, 3::4], "Ws")
         op("V", ["kuh"], ["ku"], vts, c("ku"), T.kuh[:, 15::16], -1.0, None, A.add)
 
     XK = ["X0", "X1", "X2", "X3"]
@@ -295,12 +309,13 @@ def rank_program(g, core, T, topo):
             mm("ps%d" % t, "ec%d" % t, "es%d" % t, 0, "xr", "xt", 0, 256, False, True)
             op("S", ["ps%d" % t], ["P%d" % t], act, T.P[:, 256 * t:256 * t + 256], T["ps%d" % t][:, 0:256], AF.Copy)
 
-    def unpack_keep(n):
-        for t in range(4):
-            mm("ps%d" % t, "ec%d" % t, "es%d" % t, 0, "xq", "xs", 0, 256)
-            op("S", ["ps%d" % t], ["F%d" % t], act, T.F[:, 256 * t:256 * t + 256], T["ps%d" % t][:, 0:256], AF.Copy, scale=2.0)
-        for t in range(4):
-            op("S", ["F%d" % t] + rank_keys(n), ["Fc%d" % t], act, T.Fc[:, 256 * t:256 * t + 256], T.F[:, 256 * t:256 * t + 256].indirect(c("ru%d" % (n % 2))), AF.Copy)
+    def keep(step, ts, banks):
+        for t, bank in zip(ts, banks):
+            if step == 0: mm(bank, "ec%d" % t, "es%d" % t, 0, "xq", "xs", 0, 256)
+            else: op("S", [bank], ["F%d" % t], act, T.F[:, 256 * t:256 * t + 256], T[bank][:, 0:256], AF.Copy, scale=2.0)
+
+    def unsort(n, ts):
+        for t in ts: gather(T.Fc[:, 256 * t:256 * t + 256], "Fc%d" % t, T.F[:, 256 * t:256 * t + 256], ["F%d" % t], *slots(n))
 
     def deal(src, out):
         for t in range(4 - ND, 4):
@@ -309,153 +324,176 @@ def rank_program(g, core, T, topo):
             h, hk = (T.H[:, 128 * t:128 * t + 128].indirect(c("hu")), "H%d" % t) if t < 4 - ND else (T.Hg[:, 256 * t:256 * t + 256], "Hg%d" % t)
             op("V", [hk, "hu", "%s%d" % (src, t)], ["%s%d" % (out, t)], vtt, T[out][:, t:1024:4], h, T[src][:, 256 * t:256 * t + 256], A.add)
 
+    def counted():
+        for o, key, rd, i, fn, scale, bias in ((pw, "pw", "pr", pr, AF.Identity, -4.0, pm), (pv, "pv", "pr", pr, AF.Identity, -4.0, pm4),
+                                               (pnil, "pnil", "pr", pr, AF.Relu, -FAR, FAR), (pside, "pside", "pw", pw, AF.Sign, -1.0, -8.5),
+                                               (pdist, "pdist", "pw", pw, AF.Abs, 1.0, 8.5), (pth, "pth", "pv", pv, AF.Identity, -1.0, -15.5),
+                                               (pnil, "pnil", "pnil", pnil, AF.Identity, 1.0, -12.0), (pno, "pno", "pdist", pdist, AF.Relu, -FAR, 5 * FAR)):
+            op("S", [rd], [key], act, o, i, fn, scale=scale, bias=bias)
+        op("S", ["pth", "pside", "pnil"], ["pcut"], act, pcut, pth, AF.Identity, scale=pside, bias=pnil)
+
+    counted()
     ranks(0)
-    op("S", ["iX", "pa"], ["away"], act, T.away[:], T.iX[:], AF.Abs, scale=-1.0, bias=pa)
-    op("S", ["away"], ["c2"], act, T.c2[:], T.away[:], AF.Relu, scale=-FAR, bias=FAR)
+    op("S", NUM[0:1], ["kval"], act, T.kval[:], T.num[:, 0:256], AF.Identity, bias=1.0)
+    op("S", ["pcut", "pno"], ["pout"], act, pout, pcut, AF.Identity, bias=pno)
     for t in range(4): op("S", ["xin"], ["Fc%d" % t], act, T.Fc[:, 256 * t:256 * t + 256], T.xin[:, t::4], AF.Copy)
-    op("S", ["junk"], TAB2, act, T.tab2[:, 0:2048], T.junk[:, 0:2048], AF.Identity, scale=0.0, bias=3.0)
+    op("S", ["us", "ul"], ["u2s"], act, T.u2s[:], T.us[:].indirect(c("ul")), AF.Copy)
     tables(0)
-    regather("X", XO, range(4))
+    op("S", ["gm0"], ["gm"], act, T.gm[:], T.gm0[:], AF.Relu, scale=256.0)
+    op("S", ["pa"], ["sgn"], act, psig, pa, AF.Sign, bias=-14.5)
+    for o, key, scale, bias in ((pp1, "pp1", 1.0, 1024.0), (pb, "pb", 1.0, 2.0 / FAR), (pp16, "pp16", 0.0625, 64 - 0.46875)):
+        op("S", ["pa"], [key], act, o, pa, AF.Identity, scale=scale, bias=bias)
+    for o, scale in ((pneg, -1.0), (phalf, 0.5), (pfar, FAR)): op("S", ["sgn"], ["sig"], act, o, psig, AF.Copy, scale=scale, acc=True)
     pairs(0, T.ks[:, 0:256], ["ks"])
-    op("V", ["iU"], ["ul2"], vcp, c("ul", 8, 24), c("iU"))
+    quant("ec0", "es0", "EE", 4, 128)
     pairs(1)
-    quant("uq", "us", "uin", 0, 128)
-    pairs(2)
-    op("V", ["prw", "pown", "ptab"], ["gm"], vts, T.gm[:], T.prw[:], pown, ptab, A.not_equal, A.mult)
-    op("V", ["uq", "ul", "ul2"], ["u2"], vcp, T.u2[:].bitcast(dt.uint32), T.uq[:].bitcast(dt.uint32).indirect(c("ul")))
+    for t in range(1, 4): quant("ec%d" % t, "es%d" % t, "EE", 4 - t, 128)
+    unpack()
+    op("V", ["uq", "ul"], ["u2"], vcp, T.u2[:].bitcast(dt.uint32), T.uq[:].bitcast(dt.uint32).indirect(c("ul")))
     places(0)
     place_list()
-    tail()
-    op("S", ["us", "ul", "ul2"], ["u2s"], act, T.u2s[:], T.us[:].indirect(c("ul")), AF.Copy)
-    op("S", ["c2"], ["c1"], act, T.c1[:], T.c2[:], AF.Identity, scale=18.0, bias=-FAR)
-    op("S", ["mid0", "pmid"], ["mid1"], act, T.mid1[:], T.mid0[:], AF.Sign, bias=pmid)
-    op("S", ["mid1"], ["mid"], act, T.mid[:], T.mid1[:], AF.Copy, scale=0.5)
-    unpack()
+    op("S", ["mid0", "pr"], ["mid1"], act, T.mid1[:], T.mid0[:], AF.Sign, scale=-0.5, bias=pq)
+    op("S", ["iX", "pb"], ["away"], act, T.away[:], T.iX[:], AF.Abs, scale=-1.0, bias=pb)
+    op("S", ["mid1"], ["mid"], act, T.mid[:], T.mid1[:], AF.Copy, scale=-0.5)
+    keep(0, (0,), ("ps5",))
     cells(0)
     dma("dw", [("Y", T.wq[:].bitcast(dt.uint8), T.wc[:], ["gt"], ["wq"]), ("Y", T.wp[:], T.ws[:], [], ["wp"])])
     dma("dv", [("Y", T.vin[:], T.v[:], [], ["vin"])])
 
     nxt = T.cores[(rank + 1) % len(T.cores)]
     rid, pid, sen = topo.addr(nxt)
-    m4 = sum(1 << e for e in topo.engines(core, nxt)[0:4])
+    mask = sum(1 << e for e in topo.engines(core, nxt)[0:NE])
+
+    def layer(n):
+        need("T", [("arr%d" % n, 2 * NE, "R", {})])
+        ends["arr%d" % n] = 2 * NE
+        for t in range(4):
+            mm("ps%d" % (4 + t), "wq", "wp", 128 * t, "lc%d" % n, "lp%d" % n, 0, 256)
+            op("S", ["ps%d" % (4 + t)], ["H%d" % t], act, T.H[:, 128 * t:128 * t + 128], T["ps%d" % (4 + t)][:, 1:256:2], AF.Copy, scale=0.03125)
 
     for n in range(R):
-        zq, zs, ru = "zq%d" % n, "zs%d" % n, "ru%d" % (n % 2)
+        zq, zs = "zq%d" % n, "zs%d" % n
         for t in (0, 1):
             op("V", ["P%d" % t, "ku"], ["Z%d" % t], vcp, T.Z[:, t:1024:4], T.P[:, 256 * t:256 * t + 256].indirect(c("ku")))
         for t in (2, 3):
             op("S", ["P%d" % t, "ku"], ["Z%d" % t], act, T.Z[:, t:1024:4], T.P[:, 256 * t:256 * t + 256].indirect(c("ku")), AF.Copy)
-        op("V", ["plc", "pp8"], ["cu"], vts, c("cu"), T.plc[:, 15::16], -0.125, pp8, A.mult, A.add)
-        for k, bank in ((0, "ps0"), (1, "ps7")):
+        if n == 0:
+            op("S", ["away"], ["near"], act, T.near[:], T.away[:], AF.Relu, scale=-1.0, bias=1.0)
+            op("S", ["near", "sig"], ["cs"], act, T.cs[:], T.near[:], AF.Identity, scale=pfar, bias=1.0)
+        keep(1, (0,), ("ps5",))
+        op("V", ["pu"], ["cu"], vts, c("cu"), c("pu"), 0.125, -0.4375, A.mult, A.add)
+        for k in (0, 1):
             a, b = 128 * k, 128 * k + 128
             op("V", ["Z0", "Z1", "Z2", "Z3"], [zq + str(k), zq], V.quantize_mx, T[zq][:, a:b], T[zs][:, a:b], T.Z[:, 4 * a:4 * b], acc=k > 0)
-            mm(bank, "u2", "u2s", 0, zq, zs, a, 128, key=zq + str(k))
-        need("G", [last[zq]])
-        g.remote_dma(T["lc%d" % n][:].bitcast(dt.uint8), T[zq][:].bitcast(dt.uint8), T.sem["arr%d" % n], T.sem.snd, pid, rid, m4)
-        g.remote_dma(T["lp%d" % n][:], T[zs][:], T.sem["arr%d" % n], T.sem.snd, pid, rid, m4)
-        if n == 0:
-            op("G", ["Bt"], TAB2, g.iota, T.tab2[:, 2048:HW], [[0, HW - 2048]], 3, 0, allow_small_or_imprecise_dtypes=True)
-            zeros("h", 0, width(1) + 8)
+            if k == 0: mm("ps0", "uq", "us", 0, zq, zs, 0, 128, key=zq + "0")
+        need("G", [last[zq], last["Bt"]])
+        g.remote_dma(T["lc%d" % n][:].bitcast(dt.uint8), T[zq][:].bitcast(dt.uint8), T.sem["arr%d" % n], T.sem.snd, pid, rid, mask)
+        g.remote_dma(T["lp%d" % n][:], T[zs][:], T.sem["arr%d" % n], T.sem.snd, pid, rid, mask)
+        if n == 0: zeros("h", 0, width(1) + 8)
         if n < R - 1: zeros("Wp", 0, 2048)
-        for bank, la in ((1, 128), (3, 128), (2, 256), (4, 256)): mm("ps%d" % bank, "u2", "u2s", la, zq, zs, 0, 256, key=zq)
-        for k, bank in ((0, "ps0"), (1, "ps7")): op("V", [bank], ["sl%d" % k], V.transpose, T.sl[:, 128 * k:128 * k + 128], T[bank][:, 0:128])
+        for bank, la in ((1, 0), (3, 0), (2, 128), (4, 128)): mm("ps%d" % bank, "u2", "u2s", la, zq, zs, 0, 256, key=zq)
+        mm("ps7", "uq", "us", 0, zq, zs, 128, 128, key=zq)
 
-        def signs(k, lo, hi, ts=(0, 2, 1, 3)):
+        def turned(k): op("V", ["ps%d" % (7 * k)], ["sl%d" % k], V.transpose, T.sl[:, 128 * k:128 * k + 128], T["ps%d" % (7 * k)][:, 0:128])
+        turned(0)
+
+        def signs(k, lo, hi, ts=range(4)):
             for t in ts:
-                b, bank = 64 * k + 16 * t, "ps%d" % (3 + t % 2)
+                b, bank = 64 * k + 32 * (t % 2) + 16 * (t // 2), "ps%d" % (3 + t // 2)
                 op("S", [bank, "sl%d" % (k // 2)], ["sg%d" % k], act, T.sg[:, 1024 * k + 4 * lo + t:1024 * k + 4 * hi:4], T[bank][:, lo:hi], AF.Sign,
                    bias=T.sl[:, b:b + 1], scale=-1.0, acc=True)
 
         def direct(k, lo, hi, how):
-            for t in (0, 2, 1, 3):
-                b, bank = 64 * k + 16 * t, "ps%d" % (1 + t % 2)
+            for t in range(4):
+                b, bank = 64 * k + 32 * (t % 2) + 16 * (t // 2), "ps%d" % (1 + t // 2)
                 op("V", [bank, "sl%d" % (k // 2)], ["Cd%d" % k], vts, T.Ct[:, 1024 * k + 4 * lo + t:1024 * k + 4 * hi:4], T[bank][:, lo:hi], T.sl[:, b:b + 1], None, how, acc=True)
 
         def middle(k):
             a = 1280 * k
             op("V", ["sg%d" % k, "mid"], ["Cm%d" % k], vtt, T.Ct[:, a:a + 256], T.sg[:, a:a + 256], T.mid[:], A.is_lt)
 
-        def side(k, right, first=0, step=1):
-            a, b = (1280 * k + 256, 1024 * k + 1024) if right else (1024 * k, 1280 * k)
-            o, i, key = T.Ct[:, a + first:b:step], T.sg[:, a + first:b:step], "C%s%d" % ("lr"[right], k)
-            if right: op("S", ["sg%d" % k], [key], act, o, i, AF.Sign, bias=1.0, scale=-1.0)
-            else: op("S", ["sg%d" % k], [key], act, o, i, AF.Relu, scale=-1.0)
+        def side(k, right, a, b):
+            op("V", ["sg%d" % k], ["C%s%d" % ("lr"[right], k)], vts, T.Ct[:, a:b], T.sg[:, a:b], 0.0, None, A.is_le if right else A.is_lt)
 
         def total(k, keys, start, stop, halves=(0, 1)):
             a, b, key = 256 * k + 128 * halves[0], 256 * k + 128 * halves[-1] + 128, "cq%d%d" % (k, halves[0])
-            op("V", keys, [key], V.quantize_mx, T.cq[:, a:b], T.cs[:, a:b], T.Ct[:, 4 * a:4 * b])
-            for j in halves: mm("ps%d" % (5 + j), "bc", "bs", 0, "cq", "cs", 256 * k + 128 * j, 128, start, stop, key)
-        signs(0, 0, 64, (0, 2))
-        signs(1, 0, 256, (0,))
-        signs(0, 0, 64, (1, 3))
-        signs(1, 0, 256, (2, 1, 3))
+            op("V", keys, [key], V.quantize_mx, T.cq[:, a:b], T.cs_[:, a:b], T.Ct[:, 4 * a:4 * b])
+            for j in halves: mm("ps%d" % (5 + j), "bc", "bs", 0, "cq", "cs_", 256 * k + 128 * j, 128, start, stop, key)
+        signs(1, 0, 256, (0, 1))
+        signs(0, 0, 64)
+        signs(1, 0, 256, (2, 3))
+        direct(0, 64, 256, A.is_ge)
+        turned(1)
         signs(3, 192, 256)
         signs(2, 0, 256)
-        side(1, 1)
-        side(2, 0)
-        direct(0, 64, 256, A.is_ge)
-        middle(0)
+        op("S", ["sg1"], ["Cr1"], act, T.Ct[:, 1536:2048], T.sg[:, 1536:2048], AF.Sign, bias=1.0, scale=-1.0)
+        op("S", ["sg2"], ["Cl2"], act, T.Ct[:, 2048:2560], T.sg[:, 2048:2560], AF.Relu, scale=-1.0)
         direct(3, 0, 192, A.is_gt)
+        middle(0)
         if n == 0: quant("bc", "bs", "Bt", 0, 128)
+        side(1, 0, 1024, 1280)
         total(0, ["Cd0", "Cm0"], True, False)
         middle(3)
-        op("V", ["sg1"], ["Cl1"], vts, T.Ct[:, 1024:1280], T.sg[:, 1024:1280], 0.0, None, A.is_lt)
         middle(1)
         total(3, ["Cd3", "Cm3"], False, False)
         middle(2)
-        op("V", ["sg2"], ["Cr2"], vts, T.Ct[:, 2816:3072], T.sg[:, 2816:3072], 0.0, None, A.is_le)
+        side(2, 1, 2816, 3072)
         total(1, ["Cl1", "Cr1", "Cm1"], False, False)
         total(2, ["Cr2", "Cm2"], False, True, (1,))
         total(2, ["Cl2"], False, True, (0,))
         op("S", ["ps6"], ["stw1"], act, T.stw[:, 128:256], T.ps6[:, 0:128], AF.Copy)
         op("V", ["ps5"], ["stw0"], vcp, T.stw[:, 0:128], T.ps5[:, 0:128])
         op("V", ["stw0", "stw1", "cu", "ks"], ["Ksl"], vtt, T.Ksl[:], T.stw[:].indirect(c("cu")), T.ks[:, 0:256], A.add)
-        op("S", ["Ksl"] + rank_keys(n), ["Kr0"], act, T.Krow[:, 0:128], T.Ksl[:].indirect(c(ru, 0, 8)), AF.Copy)
-        op("V", ["Ksl"] + rank_keys(n), ["Kr1"], vcp, T.Krow[:, 128:256], T.Ksl[:].indirect(c(ru, 8, 16)))
         ranks(n + 1)
-        unpack_keep(n)
-        need("T", [("arr%d" % n, 8, "R", {})])
-        ends["arr%d" % n] = 8
-        for t in range(4): mm("ps%d" % (4 + t), "wq", "wp", 128 * t, "lc%d" % n, "lp%d" % n, 0, 256)
-        for t in range(4): op("S", ["ps%d" % (4 + t)], ["H%d" % t], act, T.H[:, 128 * t:128 * t + 128], T["ps%d" % (4 + t)][:, 1:256:2], AF.Copy, scale=0.03125)
+        keep(0, (1, 2, 3), ("ps0", "ps1", "ps2"))
+        if n == R - 1: gather(T.Krow[:], "Krow", T.Ksl[:], ["Ksl"], *slots(n))
+        follow(0, n)
+        keep(1, (1, 2, 3), ("ps0", "ps1", "ps2"))
+        follow(1, n)
+        unsort(n, range(4))
         tables(n + 1)
         if n < R - 1:
             columns(0)
             pairs(0, T.ks[:, 0:256], ["ks"])
             columns(1)
+            follow(2, n)
             pairs(1)
-            columns(2)
-            pairs(2)
-            regather("G", GO, (1, 2, 3))
-            regather("G", GO, (0,), "V")
+            follow(3, n)
+            regather("G", GO, (0, 1))
+            layer(n)
+            regather("G", GO, (2, 3))
             places(n + 1)
             op("V", ["plc", "pp16"], ["hu"], vts, c("hu"), T.plc[:, 15::16], -0.0625, pp16, A.mult, A.add)
             place_list()
             deal("G", "X")
             tail()
             unpack()
+            keep(0, (0,), ("ps5",))
             cells(n + 1)
 
-    pairs(0, T.Krow[:], KR)
-    op("V", rank_keys(R) + ["pp1"], ["rg"], vts, c("rg"), c("ru%d" % (R % 2)), pp1, None, A.add)
+    layer(R - 1)
+    pairs(0, T.Krow[:], ["Krow"])
     pairs(1)
-    op("V", ["rg", "el"], ["rf"], vtt, c("rf"), c("rg"), c("el"), A.subtract)
-    pairs(2)
+    follow(2, R - 1)
+    op("V", ["rh", "sig", "pp1"], ["rg"], vts, c("rg"), T.rh[:, 15::16], psig, pp1, A.mult, A.add)
     quant("vq", "vqs", "vin", 0, 128)
-    op("V", KR, ["ptf"], vts, T.ptf[:], T.Krow[:], -0.498, M, A.add, A.add)
-    op("V", ["ptf"], ["ptg"], vts, T.ptg[:], T.ptf[:], -M, None, A.add)
-    dma("dpt", [("Y", T.pt[:], T.ptg[0::16, :], ["ptg"], [])])
+    op("V", ["rg", "el"], ["rf"], vtt, c("rf"), c("rg"), c("el"), A.subtract)
+    op("S", ["Krow"], ["near"], act, T.near[:], T.Krow[:], AF.Identity, bias=M - 0.5)
+    op("S", ["near"], ["ptf"], act, T.ptf[:], T.near[:], AF.Identity, bias=-1.0 - M)
+    dma("dpt", [("Y", T.pt[:], T.ptf[0::16, :], ["ptf"], [])])
     places(R)
     op("V", ["plc", "rf"], ["plf"], vtt, c("plf"), c("rf"), T.plc[:, 15::16], A.subtract)
-    op("V", ["plf"], ["hu"], vts, c("hu"), c("plf"), 0.0625, -0.46875, A.mult, A.add)
+    op("V", ["plf"], ["hu"], vts, c("hu"), c("plf"), 0.0625, -0.53125, A.mult, A.add)
     deal("Fc", "Xf")
 
-    quant("fq", "fqs", "Xf", 0, 256, ["Xf0", "Xf1", "Xf2", "Xf3"])
-    for k in (0, 1): mm("ps%d" % k, "vq", "vqs", 0, "fq", "fqs", 128 * k, 128)
+    for k in (0, 1):
+        a, b = 128 * k, 128 * k + 128
+        op("V", ["Xf0", "Xf1", "Xf2", "Xf3"], ["fq%d" % k, "fq", "fqs"], V.quantize_mx, T.fq[:, a:b], T.fqs[:, a:b], T.Xf[:, 4 * a:4 * b], acc=k > 0)
+        mm("ps%d" % k, "vq", "vqs", 0, "fq", "fqs", a, 128, key="fq%d" % k)
     scales = [(T.osc[4 * j:4 * j + 4, :], T.fqs[32 * j:32 * j + 4, :], ["fqs"], []) for j in range(4)]
     dma("dend", [("Y", T.oc[:], T.fq[:].bitcast(dt.uint8), ["fq"], []), ("S",) + scales[0]] + [("Y",) + x for x in scales[1:]])
     op("S", ["ps0"], ["yo0"], act, T.yo[:, 0:128], T.ps0[:, 0:128], AF.Copy)
     op("V", ["ps1"], ["yo1"], vcp, T.yo[:, 128:256], T.ps1[:, 0:128])
     dma("dend", [("S", T.y[:], T.yo[:], ["yo0", "yo1"], [])])
     for s, v in ends.items(): g.wait_ge(T.sem[s], v)
-    g.wait_ge(T.sem.snd, 8 * R)
+    g.wait_ge(T.sem.snd, 2 * NE * R)

from concourse.mybir import dt, AluOpType as A, ActivationFunctionType as AF

N, R, C = 8, 3, 256
HW = 2832
NV = 5
ND = 2
NA = 12
NE = 8
M = 8388608.0
FAR = 4096.0
F8 = "float8_e4m3fn_x4"
LISTS = {}


def _scratch():
    s = {}

    def sb(names, w, d="float32"):
        for n in names.split(): s[n] = ("sbuf", [128, w], d)

    def mx(n, m, w):
        sb(n, w, F8)
        sb(m, w, "uint8")

    def lists(buf, d, names, wide):
        at = 0
        for n in names.split():
            w = wide.get(n, 16)
            LISTS[n] = (buf, at, w)
            at += (w + 15) // 16 * 16
        sb(buf, at, d)
    lists("lstf", "float32", "kl el Kl acc rf rg sd0 sdx of cg plf par pas", {"sd0": 32, "sdx": 32, "of": 32})
    lists("lsti", "int32", "iB iU pl ip iq", {"ip": 2, "iq": 8})
    lists("lstu", "uint16", "pU ul ru rk0 rk1 ou pu hu cu ku colU L", {})
    sb("num", 2048)
    sb("er Ksl Krow sl Ks kT ptf yo away near", 256)
    sb("AB", 512)
    sb("ks", 264)
    sb("iX cs c2 kval stw gt gtT gm0 gm rst prw kuh rs rc rh", 256, "bfloat16")
    sb("mid0 mid1 mid", 256, "bfloat16")
    sb("plc", 256, "float16")
    sb("junk", 256 * (16 - NV), "bfloat16")
    sb("cmp", 256 * NV, "bfloat16")
    sb("sc", 128 * NV, "float16")
    sb("h", HW + 2048, "bfloat16")
    sb("tabs", HW, "bfloat16")
    sb("Wp", 2048, "bfloat16")
    sb("uin vin Bt H", 512, "bfloat16")
    sb("Ct sg", 4096, "bfloat16")
    sb("Ws Z P F Fc G Hg Xf xin", 1024, "bfloat16")
    sb("X", 1032, "bfloat16")
    sb("EE", 520, "bfloat16")
    for t in range(4): mx("ec%d" % t, "es%d" % t, 128)
    for n, m, w in (("bc", "bs", 128), ("xq", "xs", 256), ("xr", "xt", 256), ("cq", "cs_", 1024),
                    ("uq", "us", 128), ("u2", "u2s", 256), ("vq", "vqs", 128), ("wq", "wp", 512), ("fq", "fqs", 256)): mx(n, m, w)
    for k in range(R):
        mx("zq%d" % k, "zs%d" % k, 256)
        mx("lc%d" % k, "lp%d" % k, 256)
    for k in range(8): s["ps%d" % k] = ("psum", [128, 512], "float32")
    return s


SCRATCH = _scratch()
DSEM = ["df", "dh", "dp", "dx", "du", "dw", "dv", "dend", "dpt"] + ["dt%s%d" % (x, k) for x in "ab" for k in range(R + 1)]
TAB2 = ["tab2", "tab3"]
SEMAPHORES = ["qV", "qS", "qT", "qG", "snd"] + ["arr%d" % k for k in range(R)] + DSEM


def rank_program(g, core, T, topo):
    rank = T.rank_of(core)
    if rank is None:
        return
    eng = {"V": g.vector, "S": g.scalar, "T": g.tensor, "G": g, "Y": g.sync}
    know = {q: {} for q in eng}
    cnt, last, readers, ends = {}, {}, {}, {}

    def c(name, a=0, b=None, step=1):
        buf, at, w = LISTS[name]
        return T[buf][:, at + a:at + (w if b is None else b):step]

    def need(q, toks):
        best = {}
        for t in toks:
            if t[1] > best.get(t[0], (0, 0))[1]: best[t[0]] = t
        for t in sorted(best.values(), key=lambda t: -len(t[3])):
            if know[q].get(t[0], 0) >= t[1]: continue
            eng[q].wait_ge(T.sem[t[0]], t[1])
            for s, v in t[3].items():
                if v > know[q].get(s, 0): know[q][s] = v
            know[q][t[0]] = t[1]

    def deps(q, rd, wr, acc=False, copies=False):
        d = []
        for k in rd:
            if k in last: d.append(last[k])
            if k[:2] == "ps": d += [t for t in readers.get(k, []) if t[2] != q]
        for k in wr:
            if k in last and not (acc and last[k][2] == q): d.append(last[k])
            d += [t for t in readers.get(k, []) if copies or t[2] != q]
        return d

    def note(tok, rd, wr):
        for k in rd: readers.setdefault(k, []).append(tok)
        for k in wr:
            last[k] = tok
            readers[k] = []

    def op(q, rd, wr, fn, *a, acc=False, **kw):
        need(q, deps(q, rd, wr, acc))
        s = "q" + q
        cnt[s] = cnt.get(s, 0) + 1
        fn(*a, **kw).then_inc(T.sem[s], 1)
        note((s, cnt[s], q, {**know[q], s: cnt[s]}), rd, wr)
        ends[s] = cnt[s]

    def dma(sem, items):
        seen, rds, wrs = {}, [], []
        for q, o, i, rd, wr in items: need(q, deps(q, rd, wr, copies=True))
        for q, o, i, rd, wr in items:
            cnt[sem] = cnt.get(sem, 0) + 16
            eng[q].dma_start(o, i).then_inc(T.sem[sem], 16)
            for s, v in know[q].items(): seen[s] = max(v, seen.get(s, 0))
            rds += rd
            wrs += wr
        seen[sem] = cnt[sem]
        note((sem, cnt[sem], "dma", seen), rds, wrs)
        ends[sem] = cnt[sem]

    V, S, PE = g.vector, g.scalar, g.tensor
    vts, vtt, vcp, vscan, act = V.tensor_scalar, V.tensor_tensor, V.tensor_copy, V.tensor_tensor_scan, S.activation

    def quant(qn, sn, tn, a, n, rd=None):
        op("V", rd or [tn], [qn, sn], V.quantize_mx, T[qn][:, 0:n], T[sn][:, 0:n], T[tn][:, a:a + 4 * n])

    def mm(bank, lq, ls, la, rq, rs, ra, n, start=True, stop=True, key=None):
        op("T", [lq, ls] + ([key] if key else [rq, rs]), [bank], PE.matmul_mx, T[bank][:, 0:n], T[lq][:, la:la + 128], T[ls][:, la:la + 128],
           T[rq][:, ra:ra + n], T[rs][:, ra:ra + n], start, stop, acc=not start)

    def hold(out, ok, row, rk):
        op("V", ["c2", rk], [ok], vscan, out, T.c2[:], row, 0.0, A.add, A.min)

    def turn(out, ok, row, rk, w=256):
        op("V", ["cs", "sig", rk], [ok], vscan, out, T.cs[:, 0:w], row, psig, A.mult, A.min)

    def gather(out, ok, win, wk, lst, lk):
        op("S", wk + lk, [ok], act, out, win.indirect(lst), AF.Copy)

    dma("dp", [("Y", c("pl"), T.p[:], [], ["pl"])])
    dma("dx", [("Y", T.xin[:], T.x[:], [], ["xin"])])
    dma("du", [("Y", T.uin[:], T.u[:], [], ["uin"])])

    def iota(n, pat, base=0, cm=0, small=False):
        out = c(n) if n in LISTS else T[n][:]
        if small: op("G", [], [n], g.iota, out, pat, base, cm, allow_small_or_imprecise_dtypes=True)
        else: op("G", [], [n], g.iota, out, pat, base, cm)

    def zeros(n, a, b):
        op("G", [], [n], g.iota, T[n][:, a:b], [[0, b - a]], 0, 0, allow_small_or_imprecise_dtypes=True)

    def width(n):
        return (2049 + 255 * n + 7) // 8 * 8
    NUM = ["num%d" % j for j in range(8)]
    op("V", [], ["halves"], V.memset, T.gt[:], 0.5)
    op("V", ["halves"], NUM[0:1], vscan, T.num[:, 0:256], T.gt[:], T.gt[:], -1.0, A.add, A.add)
    iota("ip", [[0, 2]], 0, 1)
    iota("iB", [[1, 16]])
    iota("iU", [[16, 2], [32, 4], [0, 2]])
    iota("iX", [[0, 16], [1, 16]], small=True)
    HALF = (width(0) + 8) // 2
    zeros("Wp", 0, HALF)
    dma("dh", [("Y", T.h[:, a:a + HALF], T.Wp[:, 0:HALF], ["Wp"], ["h"]) for a in (0, HALF)])
    dma("df", [("Y", T.Wp[:, HALF:2048], T.Wp[:, 0:2048 - HALF], ["Wp"], ["Wq"])])
    op("G", [], ["kse"], g.iota, T.ks[:, 256:264], [[0, 8]], HW - 1, 0, allow_small_or_imprecise_dtypes=True)
    op("G", [], ["sd0"], g.iota, c("sd0"), [[0, 32]], 0, 0, allow_small_or_imprecise_dtypes=True)
    op("G", [], ["sdd"], g.iota, c("sdx", 0, 32, 2), [[128, 16]], HW, 1, allow_small_or_imprecise_dtypes=True)
    op("G", ["Wp"], ["EE"], g.affine_select, T.EE[:], T.Wp[:, 0:520], [[-1, 520]], A.not_equal, 0.5, 4, 4)
    for k, (sh, bits) in enumerate(((0, 15), (0, 7), (3, 15), (3, 3), (0, 31))):
        op("V", ["ip"], ["iq%d" % k], vts, c("iq", k, k + 1), c("ip", 0, 1), sh, bits, A.arith_shift_right, A.bitwise_and)
    op("V", NUM[0:1], [NUM[7]], vts, T.num[:, 1792:2048], T.num[:, 0:256], 1792.0, None, A.add)
    op("V", ["iq%d" % k for k in range(5)], ["pa", "pr"], vcp, c("par", 0, 5), c("iq", 0, 5))
    op("V", NUM[0:1], [NUM[5]], vts, T.num[:, 1280:1536], T.num[:, 0:256], 1280.0, None, A.add)
    pa, pr, pm, pm4, pq, pb, pp1, pp16 = [c("par", k, k + 1) for k in range(8)]
    psig, pneg, phalf, pfar, pw, pv, pside, pdist, pth, pno, pnil, pcut, pout = [c("pas", k, k + 1) for k in range(13)]
    for j in range(1, 5): op("S", NUM[0:1], [NUM[j]], act, T.num[:, 256 * j:256 * j + 256], T.num[:, 0:256], AF.Identity, bias=256.0 * j)
    op("S", NUM[0:1], ["er"], act, T.er[:], T.num[:, 0:256], AF.Identity, scale=1.0 / 256, bias=1.0 + 1.0 / 512)
    op("V", ["iB", "pa"], ["el"], vts, c("el"), c("iB"), 16.0, pa, A.mult, A.add)
    op("V", NUM[0:1], [NUM[6]], vts, T.num[:, 1536:1792], T.num[:, 0:256], 1536.0, None, A.add)
    op("V", ["el"], ["kl"], vts, c("kl"), c("el"), 1.0 / 256, 1.0 + 1.0 / 512, A.mult, A.add)
    op("V", ["pl"], ["pU"], vcp, c("pU"), c("pl"))
    op("V", ["pl", "kl"], ["Kl"], vtt, c("Kl"), c("pl"), c("kl"), A.add)
    op("V", NUM + ["pU", "er"], ["Krow"], vtt, T.Krow[:], T.num[:].indirect(c("pU")), T.er[:], A.add)
    op("V", ["iX", "pa"], ["c2"], vts, T.c2[:], T.iX[:], pa, FAR, A.is_equal, A.mult)
    iota("prw", [[0, 8], [2, 2], [0, 16]], small=True)
    iota("rst", [[-16, 16], [-8192, 16]], 1024 + 9 * 256, small=True)
    iota("mid0", [[2, 64], [0, 2], [-64, 2]], -1, small=True)
    zeros("Bt", 0, 512)
    for j in range(N):
        op("G", ["Bt"], ["Bt"], g.iota, T.Bt[j // 2 * 32:j // 2 * 32 + 32, 64 * j:64 * j + 64], [[0, 16], [2 * (j % 2) - 1, 2], [0, 2]], 1 - j % 2, 0, allow_small_or_imprecise_dtypes=True, acc=True)

    def count(b):
        op("V", ["cmp%d" % b], ["sc%d" % b], vscan, T.sc[:, 128 * b:128 * b + 128], T.cmp[:, 256 * b:256 * b + 128], T.cmp[:, 256 * b + 128:256 * b + 256], -127.5, A.add, A.add)

    def ranks(n):
        ru, row, rk = ("ru", T.Ksl, "Ksl") if n else ("rk0", T.Krow, "Krow")
        if n:
            for k in (0, 1): turn(T.Ks[:, 128 * k:128 * k + 128], "Ks%d" % k, row[:, 128 * k:128 * k + 128], rk, 128)

        def key(b): return (T.Ks[:, 16 * b + 15:16 * b + 16], ["Ks%d" % (b // 8), "sig"]) if n else (c("Kl", b, b + 1), ["Kl"])
        for j, b in enumerate(range(NV, 16)):
            op("S", [rk] + key(b)[1], ["junk", "acc%d" % (b >= NA)], act, T.junk[:, 256 * j:256 * j + 256], row[:, 0:256], AF.Sign, bias=key(b)[0],
               scale=pneg if n else -1.0, accum_out=c("acc", b, b + 1), acc=j > 0)
        for b in range(NV):
            o = T.cmp[:, 256 * b:256 * b + 256]
            if n: op("V", [rk] + key(b)[1], ["cmp%d" % b], vts, o, row[:, 0:256], psig, key(b)[0], A.mult, A.is_lt)
            else: op("V", [rk] + key(b)[1], ["cmp%d" % b], vts, o, row[:, 0:256], key(b)[0], None, A.is_lt)
            if b: count(b - 1)
        half = phalf if n else 0.5
        if n == 0:
            quant("uq", "us", "uin", 0, 128)
            op("V", ["iU"], ["ul"], vcp, c("ul"), c("iU"))
        op("V", ["acc0"], [ru + "S"], vts, c(ru, NV, NA), c("acc", NV, NA), half, 127.5, A.mult, A.add)
        count(NV - 1)
        op("V", ["sc%d" % b for b in range(NV)], [ru + "V"], vts, c(ru, 0, NV), T.sc[:, 127::128], psig if n else 1.0, 127.5, A.mult, A.add)
        op("V", [ru + "S", ru + "V", "kse", rk], ["ks"], vcp, T.ks[:, 0:256].indirect(c(ru, 0, NA)), row[:, 0:16 * NA])
        op("V", ["acc1"], [ru + "T"], vts, c(ru, NA, 16), c("acc", NA, 16), half, 127.5, A.mult, A.add)
        op("V", [ru + "T", rk], ["ks"], vcp, T.ks[:, 0:256].indirect(c(ru, NA, 16)), row[:, 16 * NA:256], acc=True)

    def slots(n):
        k = "rk%d" % (n % 2)
        return c(k), [k + x for x in "SVT"]

    def tables(n):
        w = width(n)
        hold(T.AB[:, 0:256], "A", T.ks[:, 0:256], "ks")
        hold(T.AB[:, 256:512], "B", T.ks[:, 1:257], "ks")
        op("V", ["A"], ["sdp"], vts, c("sdx", 1, 32, 2), T.AB[:, 15:256:16], M - 0.5, 1.0 - M, A.add, A.add)
        op("V", ["sdp", "B"], ["sd0"], vtt, c("sd0", 1, 32, 2), T.AB[:, 271::16], c("sdx", 1, 32, 2), A.is_lt)
        if n == 0: columns(0)
        op("V", ["sd0", "sdp", "sdd"], ["of"], vscan, c("of"), c("sd0"), c("sdx"), 0.0, A.mult, A.max)
        if n == 0: columns(1)
        op("V", ["of"], ["ou"], vcp, c("ou"), c("of", 1, 32, 2))
        op("V", ["ou", "kval"], ["h"], vcp, T.h[:].indirect(c("ou")), T.kval[:])
        if n == 0:
            regather("X", XO, range(4))
            tail()
            op("S", ["prw", "pside", "pout"], ["gm0"], act, T.gm0[:], T.prw[:], AF.Sign, scale=pside, bias=pout)

        def copies(which, a, b):
            items = []
            for i in which:
                rows = 15 - 4 * i
                items.append((T.tabs[32 * i + 9 + i::8, a:b], T.tabs[0:8 * rows:8, a + 1:b + 1]))
                items.append((T.tabs[7 - i:8 * rows:8, a:b], T.tabs[32 * i + 8::8, a:b]))
            return items
        m = w // 16 * 8
        op("V", ["h"], ["tabs0"], vscan, T.tabs[:, 0:m + 8], T.h[:, 0:m + 8], T.h[:, 0:m + 8], 0.0, A.max, A.max)
        dma("dta%d" % n, [("Y", o, i, ["tabs0"], TAB2[0:1]) for o, i in copies((0, 1), 0, m)])
        op("V", ["h", "tabs0"], ["tabs1"], vscan, T.tabs[:, m + 8:w + 8], T.h[:, m + 8:w + 8], T.h[:, m + 8:w + 8], T.tabs[:, m + 7:m + 8], A.max, A.max)
        dma("dtb%d" % n, [("YS"[k % 2], o, i, ["tabs0", "tabs1"], TAB2[1:2]) for k, (o, i) in enumerate(copies((0, 1), m, w) + copies((2, 3), 0, w))])
        if 0 < n < R: zeros("h", 0, width(n + 1) + 8)

    def columns(step):
        if step == 0: op("V", ["A", "sdp"], ["cg"], vtt, c("cg"), T.AB[:, 15:256:16], c("sdx", 1, 32, 2), A.subtract)
        if step == 1: op("V", ["cg"], ["colU"], vts, c("colU"), c("cg"), 256.0, 255.5, A.mult, A.add)

    def pairs(step, src=None, key=None):
        if step == 0: op("V", key, ["kT"], V.transpose, T.kT[:], src)
        if step == 1: op("V", ["kT"], ["L"], vts, c("L"), T.kT[:, 0::16], -0.5, None, A.add)

    def follow(step, n):
        if step == 0: gather(T.rs[:], "rs", T.kval[:], ["kval"], c("ru"), ["ruS", "ruV", "ruT"])
        if step == 1: gather(T.rc[:], "rc", T.rs[:], ["rs"], *slots(n))
        if step == 2: turn(T.rh[:], "rh", T.rc[:], "rc")
        if step == 3: op("V", ["rh", "sig"], slots(n + 1)[1], vts, slots(n + 1)[0], T.rh[:, 15::16], psig, -1.0, A.mult, A.add)

    XO = [T.X[:, t:1024:4] for t in range(4)]
    GO = [T.G[:, 256 * t:256 * t + 256] for t in range(4)]

    def regather(key, outs, which, q="S"):
        for t in which:
            src = T.Fc[:, 256 * t:256 * t + 256].indirect(c("colU"))
            if q == "S": op("S", ["Fc%d" % t, "colU"], ["%s%d" % (key, t)], act, outs[t], src, AF.Copy)
            else: op("V", ["Fc%d" % t, "colU"], ["%s%d" % (key, t)], vcp, outs[t], src)

    def places(n):
        op("V", TAB2 + ["tabs0", "tabs1", "L", "gm"], ["gt", "halves"], vtt, T.gt[:], T.tabs[:, 0:width(n)].indirect(c("L")), T.gm[:], A.max)
        op("V", ["gt"], ["gtT"], V.transpose, T.gtT[:], T.gt[:])
        op("V", ["gtT", "rst"], ["plc"], vscan, T.plc[:], T.rst[:], T.gtT[:], -FAR, A.max, A.subtract)

    def place_list():
        op("V", ["plc", "pp1"], ["pu"], vts, c("pu"), T.plc[:, 15::16], -1.0, pp1, A.mult, A.add)

    def cells(n):
        op("V", ["pu", "kval", "Wq"], ["Wp"], vcp, T.Wp[:].indirect(c("pu")), T.kval[:])
        op("V", ["Wp"], ["Ws"], vscan, T.Ws[:], T.Wp[:, 0::2], T.Wp[:, 1::2], 1.0, A.max, A.max)
        hold(T.kuh[:], "kuh", T.Ws[:, 3::4], "Ws")
        op("V", ["kuh"], ["ku"], vts, c("ku"), T.kuh[:, 15::16], -1.0, None, A.add)

    XK = ["X0", "X1", "X2", "X3"]

    def tail():
        op("S", XK, ["Xu"], act, T.X[:, 1024:1028], T.X[:, 1020:1024], AF.Copy)

    def unpack():
        quant("xq", "xs", "X", 0, 256, XK)
        quant("xr", "xt", "X", 4, 256, XK + ["Xu"])
        for t in range(4):
            mm("ps%d" % t, "ec%d" % t, "es%d" % t, 0, "xq", "xs", 0, 256, True, False)
            mm("ps%d" % t, "ec%d" % t, "es%d" % t, 0, "xr", "xt", 0, 256, False, True)
            op("S", ["ps%d" % t], ["P%d" % t], act, T.P[:, 256 * t:256 * t + 256], T["ps%d" % t][:, 0:256], AF.Copy)

    def keep(step, ts, banks):
        for t, bank in zip(ts, banks):
            if step == 0: mm(bank, "ec%d" % t, "es%d" % t, 0, "xq", "xs", 0, 256)
            else: op("S", [bank], ["F%d" % t], act, T.F[:, 256 * t:256 * t + 256], T[bank][:, 0:256], AF.Copy, scale=2.0)

    def unsort(n, ts):
        for t in ts: gather(T.Fc[:, 256 * t:256 * t + 256], "Fc%d" % t, T.F[:, 256 * t:256 * t + 256], ["F%d" % t], *slots(n))

    def deal(src, out):
        for t in range(4 - ND, 4):
            op("S", ["H%d" % t, "hu"], ["Hg%d" % t], act, T.Hg[:, 256 * t:256 * t + 256], T.H[:, 128 * t:128 * t + 128].indirect(c("hu")), AF.Copy)
        for t in range(4):
            h, hk = (T.H[:, 128 * t:128 * t + 128].indirect(c("hu")), "H%d" % t) if t < 4 - ND else (T.Hg[:, 256 * t:256 * t + 256], "Hg%d" % t)
            op("V", [hk, "hu", "%s%d" % (src, t)], ["%s%d" % (out, t)], vtt, T[out][:, t:1024:4], h, T[src][:, 256 * t:256 * t + 256], A.add)

    def counted():
        for o, key, rd, i, fn, scale, bias in ((pw, "pw", "pr", pr, AF.Identity, -4.0, pm), (pv, "pv", "pr", pr, AF.Identity, -4.0, pm4),
                                               (pnil, "pnil", "pr", pr, AF.Relu, -FAR, FAR), (pside, "pside", "pw", pw, AF.Sign, -1.0, -8.5),
                                               (pdist, "pdist", "pw", pw, AF.Abs, 1.0, 8.5), (pth, "pth", "pv", pv, AF.Identity, -1.0, -15.5),
                                               (pnil, "pnil", "pnil", pnil, AF.Identity, 1.0, -12.0), (pno, "pno", "pdist", pdist, AF.Relu, -FAR, 5 * FAR)):
            op("S", [rd], [key], act, o, i, fn, scale=scale, bias=bias)
        op("S", ["pth", "pside", "pnil"], ["pcut"], act, pcut, pth, AF.Identity, scale=pside, bias=pnil)

    counted()
    ranks(0)
    op("S", NUM[0:1], ["kval"], act, T.kval[:], T.num[:, 0:256], AF.Identity, bias=1.0)
    op("S", ["pcut", "pno"], ["pout"], act, pout, pcut, AF.Identity, bias=pno)
    for t in range(4): op("S", ["xin"], ["Fc%d" % t], act, T.Fc[:, 256 * t:256 * t + 256], T.xin[:, t::4], AF.Copy)
    op("S", ["us", "ul"], ["u2s"], act, T.u2s[:], T.us[:].indirect(c("ul")), AF.Copy)
    tables(0)
    op("S", ["gm0"], ["gm"], act, T.gm[:], T.gm0[:], AF.Relu, scale=256.0)
    op("S", ["pa"], ["sgn"], act, psig, pa, AF.Sign, bias=-14.5)
    for o, key, scale, bias in ((pp1, "pp1", 1.0, 1024.0), (pb, "pb", 1.0, 2.0 / FAR), (pp16, "pp16", 0.0625, 64 - 0.46875)):
        op("S", ["pa"], [key], act, o, pa, AF.Identity, scale=scale, bias=bias)
    for o, scale in ((pneg, -1.0), (phalf, 0.5), (pfar, FAR)): op("S", ["sgn"], ["sig"], act, o, psig, AF.Copy, scale=scale, acc=True)
    pairs(0, T.ks[:, 0:256], ["ks"])
    quant("ec0", "es0", "EE", 4, 128)
    pairs(1)
    for t in range(1, 4): quant("ec%d" % t, "es%d" % t, "EE", 4 - t, 128)
    unpack()
    op("V", ["uq", "ul"], ["u2"], vcp, T.u2[:].bitcast(dt.uint32), T.uq[:].bitcast(dt.uint32).indirect(c("ul")))
    places(0)
    place_list()
    op("S", ["mid0", "pr"], ["mid1"], act, T.mid1[:], T.mid0[:], AF.Sign, scale=-0.5, bias=pq)
    op("S", ["iX", "pb"], ["away"], act, T.away[:], T.iX[:], AF.Abs, scale=-1.0, bias=pb)
    op("S", ["mid1"], ["mid"], act, T.mid[:], T.mid1[:], AF.Copy, scale=-0.5)
    keep(0, (0,), ("ps5",))
    cells(0)
    dma("dw", [("Y", T.wq[:].bitcast(dt.uint8), T.wc[:], ["gt"], ["wq"]), ("Y", T.wp[:], T.ws[:], [], ["wp"])])
    dma("dv", [("Y", T.vin[:], T.v[:], [], ["vin"])])

    nxt = T.cores[(rank + 1) % len(T.cores)]
    rid, pid, sen = topo.addr(nxt)
    mask = sum(1 << e for e in topo.engines(core, nxt)[0:NE])

    def layer(n):
        need("T", [("arr%d" % n, 2 * NE, "R", {})])
        ends["arr%d" % n] = 2 * NE
        for t in range(4):
            mm("ps%d" % (4 + t), "wq", "wp", 128 * t, "lc%d" % n, "lp%d" % n, 0, 256)
            op("S", ["ps%d" % (4 + t)], ["H%d" % t], act, T.H[:, 128 * t:128 * t + 128], T["ps%d" % (4 + t)][:, 1:256:2], AF.Copy, scale=0.03125)

    for n in range(R):
        zq, zs = "zq%d" % n, "zs%d" % n
        for t in (0, 1):
            op("V", ["P%d" % t, "ku"], ["Z%d" % t], vcp, T.Z[:, t:1024:4], T.P[:, 256 * t:256 * t + 256].indirect(c("ku")))
        for t in (2, 3):
            op("S", ["P%d" % t, "ku"], ["Z%d" % t], act, T.Z[:, t:1024:4], T.P[:, 256 * t:256 * t + 256].indirect(c("ku")), AF.Copy)
        if n == 0:
            op("S", ["away"], ["near"], act, T.near[:], T.away[:], AF.Relu, scale=-1.0, bias=1.0)
            op("S", ["near", "sig"], ["cs"], act, T.cs[:], T.near[:], AF.Identity, scale=pfar, bias=1.0)
        keep(1, (0,), ("ps5",))
        op("V", ["pu"], ["cu"], vts, c("cu"), c("pu"), 0.125, -0.4375, A.mult, A.add)
        for k in (0, 1):
            a, b = 128 * k, 128 * k + 128
            op("V", ["Z0", "Z1", "Z2", "Z3"], [zq + str(k), zq], V.quantize_mx, T[zq][:, a:b], T[zs][:, a:b], T.Z[:, 4 * a:4 * b], acc=k > 0)
            if k == 0: mm("ps0", "uq", "us", 0, zq, zs, 0, 128, key=zq + "0")
        need("G", [last[zq], last["Bt"]])
        g.remote_dma(T["lc%d" % n][:].bitcast(dt.uint8), T[zq][:].bitcast(dt.uint8), T.sem["arr%d" % n], T.sem.snd, pid, rid, mask)
        g.remote_dma(T["lp%d" % n][:], T[zs][:], T.sem["arr%d" % n], T.sem.snd, pid, rid, mask)
        if n == 0: zeros("h", 0, width(1) + 8)
        if n < R - 1: zeros("Wp", 0, 2048)
        for bank, la in ((1, 0), (3, 0), (2, 128), (4, 128)): mm("ps%d" % bank, "u2", "u2s", la, zq, zs, 0, 256, key=zq)
        mm("ps7", "uq", "us", 0, zq, zs, 128, 128, key=zq)

        def turned(k): op("V", ["ps%d" % (7 * k)], ["sl%d" % k], V.transpose, T.sl[:, 128 * k:128 * k + 128], T["ps%d" % (7 * k)][:, 0:128])
        turned(0)

        def signs(k, lo, hi, ts=range(4)):
            for t in ts:
                b, bank = 64 * k + 32 * (t % 2) + 16 * (t // 2), "ps%d" % (3 + t // 2)
                op("S", [bank, "sl%d" % (k // 2)], ["sg%d" % k], act, T.sg[:, 1024 * k + 4 * lo + t:1024 * k + 4 * hi:4], T[bank][:, lo:hi], AF.Sign,
                   bias=T.sl[:, b:b + 1], scale=-1.0, acc=True)

        def direct(k, lo, hi, how):
            for t in range(4):
                b, bank = 64 * k + 32 * (t % 2) + 16 * (t // 2), "ps%d" % (1 + t // 2)
                op("V", [bank, "sl%d" % (k // 2)], ["Cd%d" % k], vts, T.Ct[:, 1024 * k + 4 * lo + t:1024 * k + 4 * hi:4], T[bank][:, lo:hi], T.sl[:, b:b + 1], None, how, acc=True)

        def middle(k):
            a = 1280 * k
            op("V", ["sg%d" % k, "mid"], ["Cm%d" % k], vtt, T.Ct[:, a:a + 256], T.sg[:, a:a + 256], T.mid[:], A.is_lt)

        def side(k, right, a, b):
            op("V", ["sg%d" % k], ["C%s%d" % ("lr"[right], k)], vts, T.Ct[:, a:b], T.sg[:, a:b], 0.0, None, A.is_le if right else A.is_lt)

        def total(k, keys, start, stop, halves=(0, 1)):
            a, b, key = 256 * k + 128 * halves[0], 256 * k + 128 * halves[-1] + 128, "cq%d%d" % (k, halves[0])
            op("V", keys, [key], V.quantize_mx, T.cq[:, a:b], T.cs_[:, a:b], T.Ct[:, 4 * a:4 * b])
            for j in halves: mm("ps%d" % (5 + j), "bc", "bs", 0, "cq", "cs_", 256 * k + 128 * j, 128, start, stop, key)
        signs(1, 0, 256, (0, 1))
        signs(0, 0, 64)
        signs(1, 0, 256, (2, 3))
        direct(0, 64, 256, A.is_ge)
        turned(1)
        signs(3, 192, 256)
        signs(2, 0, 256)
        op("S", ["sg1"], ["Cr1"], act, T.Ct[:, 1536:2048], T.sg[:, 1536:2048], AF.Sign, bias=1.0, scale=-1.0)
        op("S", ["sg2"], ["Cl2"], act, T.Ct[:, 2048:2560], T.sg[:, 2048:2560], AF.Relu, scale=-1.0)
        direct(3, 0, 192, A.is_gt)
        middle(0)
        if n == 0: quant("bc", "bs", "Bt", 0, 128)
        side(1, 0, 1024, 1280)
        total(0, ["Cd0", "Cm0"], True, False)
        middle(3)
        middle(1)
        total(3, ["Cd3", "Cm3"], False, False)
        middle(2)
        side(2, 1, 2816, 3072)
        total(1, ["Cl1", "Cr1", "Cm1"], False, False)
        total(2, ["Cr2", "Cm2"], False, True, (1,))
        total(2, ["Cl2"], False, True, (0,))
        op("S", ["ps6"], ["stw1"], act, T.stw[:, 128:256], T.ps6[:, 0:128], AF.Copy)
        op("V", ["ps5"], ["stw0"], vcp, T.stw[:, 0:128], T.ps5[:, 0:128])
        op("V", ["stw0", "stw1", "cu", "ks"], ["Ksl"], vtt, T.Ksl[:], T.stw[:].indirect(c("cu")), T.ks[:, 0:256], A.add)
        ranks(n + 1)
        keep(0, (1, 2, 3), ("ps0", "ps1", "ps2"))
        if n == R - 1: gather(T.Krow[:], "Krow", T.Ksl[:], ["Ksl"], *slots(n))
        follow(0, n)
        keep(1, (1, 2, 3), ("ps0", "ps1", "ps2"))
        follow(1, n)
        unsort(n, range(4))
        tables(n + 1)
        if n < R - 1:
            columns(0)
            pairs(0, T.ks[:, 0:256], ["ks"])
            columns(1)
            follow(2, n)
            pairs(1)
            follow(3, n)
            regather("G", GO, (0, 1))
            layer(n)
            regather("G", GO, (2, 3))
            places(n + 1)
            op("V", ["plc", "pp16"], ["hu"], vts, c("hu"), T.plc[:, 15::16], -0.0625, pp16, A.mult, A.add)
            place_list()
            deal("G", "X")
            tail()
            unpack()
            keep(0, (0,), ("ps5",))
            cells(n + 1)

    layer(R - 1)
    pairs(0, T.Krow[:], ["Krow"])
    pairs(1)
    follow(2, R - 1)
    op("V", ["rh", "sig", "pp1"], ["rg"], vts, c("rg"), T.rh[:, 15::16], psig, pp1, A.mult, A.add)
    quant("vq", "vqs", "vin", 0, 128)
    op("V", ["rg", "el"], ["rf"], vtt, c("rf"), c("rg"), c("el"), A.subtract)
    op("S", ["Krow"], ["near"], act, T.near[:], T.Krow[:], AF.Identity, bias=M - 0.5)
    op("S", ["near"], ["ptf"], act, T.ptf[:], T.near[:], AF.Identity, bias=-1.0 - M)
    dma("dpt", [("Y", T.pt[:], T.ptf[0::16, :], ["ptf"], [])])
    places(R)
    op("V", ["plc", "rf"], ["plf"], vtt, c("plf"), c("rf"), T.plc[:, 15::16], A.subtract)
    op("V", ["plf"], ["hu"], vts, c("hu"), c("plf"), 0.0625, -0.53125, A.mult, A.add)
    deal("Fc", "Xf")

    for k in (0, 1):
        a, b = 128 * k, 128 * k + 128
        op("V", ["Xf0", "Xf1", "Xf2", "Xf3"], ["fq%d" % k, "fq", "fqs"], V.quantize_mx, T.fq[:, a:b], T.fqs[:, a:b], T.Xf[:, 4 * a:4 * b], acc=k > 0)
        mm("ps%d" % k, "vq", "vqs", 0, "fq", "fqs", a, 128, key="fq%d" % k)
    scales = [(T.osc[4 * j:4 * j + 4, :], T.fqs[32 * j:32 * j + 4, :], ["fqs"], []) for j in range(4)]
    dma("dend", [("Y", T.oc[:], T.fq[:].bitcast(dt.uint8), ["fq"], []), ("S",) + scales[0]] + [("Y",) + x for x in scales[1:]])
    op("S", ["ps0"], ["yo0"], act, T.yo[:, 0:128], T.ps0[:, 0:128], AF.Copy)
    op("V", ["ps1"], ["yo1"], vcp, T.yo[:, 128:256], T.ps1[:, 0:128])
    dma("dend", [("S", T.y[:], T.yo[:], ["yo0", "yo1"], [])])
    for s, v in ends.items(): g.wait_ge(T.sem[s], v)
    g.wait_ge(T.sem.snd, 2 * NE * R)
